import numpy as np, ml_dtypes
CORES = [9,25,41,57]
N = 4
import mx_ref
BF = ml_dtypes.bfloat16
def gcols(t, e):
    v = np.concatenate([t.reshape(8, 16, -1, 4), np.zeros((8, 16, 1, 4), BF)], axis=2)
    return np.ascontiguousarray(np.stack([v[g][:, e[g]] for g in range(8)])).reshape(128, -1)
def tile(rs):
    return np.stack(rs, axis=2).reshape(128, -1).astype(BF)
def pick(q, e):
    c = np.concatenate([q[0].reshape(128, -1, 4), np.zeros((128, 1, 4), np.uint8)], axis=1); s = np.concatenate([q[1], np.ones((16, 1), np.uint8)], axis=1)
    return (np.ascontiguousarray(c[:, e].reshape(128, -1)), np.ascontiguousarray(s[:, e]))
def join(*qs):
    return (np.concatenate([q[0] for q in qs], axis=1), np.concatenate([q[1] for q in qs], axis=1))
def put(q, e, v):
    c, s = q[0].reshape(128, -1, 4).copy(), q[1].copy(); c[:, e] = v[0].reshape(128, -1, 4); s[:, e] = v[1]
    return (c.reshape(128, -1), s)
def pk(c, s):
    return (np.ascontiguousarray(c), mx_ref.live(s))
def emit(q):
    return q[0], q[1]
def packed(v, rng):
    q = [mx_ref.quantize(np.ascontiguousarray(v[r])) for r in range(N)]
    return np.stack([a for a, b in q]), np.stack([mx_ref.plane(b, rng) for a, b in q])
def values_of_codes():
    e, c = np.zeros((128, 128, 4), np.float32), np.zeros((128, 2, 4), np.uint8)
    e[np.arange(128), np.arange(128), 0] = 1
    c[:127, :, 0] = np.arange(256).reshape(2, 128).T[:127]
    return mx_ref.matmul(mx_ref.quantize(e.reshape(128, 512).astype(BF)), (c.reshape(128, 8), np.full((16, 2), 127, np.uint8))).T.reshape(-1).astype(np.float64)
CODE_VALUE, SCALE_VALUE = values_of_codes(), 2.0 ** (np.arange(256) - 127.0)
def decode(q):
    return (CODE_VALUE[q[0]].reshape(16, 8, -1, 4) * SCALE_VALUE[q[1]][:, None, :, None] + 0.0).reshape(128, -1).astype(np.float32)
def f(rng, *shape):
    return mx_ref.flush((rng.standard_normal(shape, dtype=np.float32) * np.exp2(rng.integers(-2, 3, shape[:-1] + (1,)))).astype(BF))
def wide(rng, *shape, cols=0):
    v = rng.standard_normal(shape, dtype=np.float32) * np.exp2(rng.integers(-12, 13, shape)).astype(np.float32)
    if cols: v *= np.repeat(np.exp2(rng.integers(-cols, cols + 1, shape[:-2] + (1, shape[-1] // 4))) * (rng.random(shape[:-2] + (1, shape[-1] // 4)) > 0.0625), 4, axis=-1).astype(np.float32)
    return mx_ref.flush(v.astype(BF))
C, A, R = 192, 48, 3
HOP = [1, 2, 3]
def lengths(p):
    z = p + np.float32(0.0)
    return 1 + (z[::16] > 0) + 2 * (z[1::16] > 0)
def walk(n):
    m, k, now = np.zeros((8, N * C + 4), bool), np.zeros((8, N * C), np.int64), np.full(8, -1)
    m[:, 0] = True
    for p in range(N * C):
        if p % C == 0: now = np.full(8, -1)
        now = now + m[:, p]
        k[:, p] = now
        m[np.arange(8), p + n[:, p]] |= m[:, p]
    return m[:, :N * C], k
def big(v):
    v = v.astype(np.float32)
    v[np.abs(v) < np.float32(2.0 ** -16)] = 0
    return v.astype(BF)
def numbers_of(rng):
    return {"x": big(f(rng, N, 128, 4 * C)), "u": np.array(f(rng, N, 128, 512)), "v": np.array(f(rng, N, 128, 512))}
def layers(rng):
    return big(f(rng, N, 128, 2048)).reshape(N, 8, 16, 4, 8, 16, 4)
def weights(rng, w):
    c, p = packed(w.reshape(N, 128, 2048), rng)
    return {"wc": c, "ws": p}
def setup_inputs(rng):
    return {**numbers_of(rng), **weights(rng, layers(rng))}
def setup_inputs_chains(rng):
    d = numbers_of(rng)
    k = rng.permutation(N) % 4
    unit = np.exp2(np.array([-28.0, -10.0, 0.0, 26.0])[k]).astype(np.float32)[:, None, None]
    by = np.exp2(np.array([-30.0, 0.0, 0.0, 30.0])[k]).astype(np.float32).astype(BF)
    o = rng.permutation(8)
    n = np.array([4, 4, 4, 3, 3, 2, 2, 1])[o]
    e = np.zeros((2, N, 8, C), np.float32)
    e[0] = np.where(n % 2 == 0, 8, -8)[None, :, None]
    e[1] = np.where(n > 2, 8, -8)[None, :, None]
    e[0, 0, :, 0] = np.where(o % 2 == 1, -1.0, -0.5)
    e[1, 0, :, 0] = np.where(o == 2, 1.0, 1.5)
    e[1, 1, o == 1, 3] = -8
    e[1, 2, o == 1, 1] = -8
    x = d["x"].reshape(N, 8, 16, C, 4)
    x[:, :, :8] = 0
    x[:, :, 0, :, 0] = (e[0] * unit).astype(BF)
    x[:, :, 1, :, 0] = (e[1] * unit).astype(BF)
    x[:, :, 2, :, 0] = unit.astype(BF)
    u = d["u"].reshape(N, 128, 128, 4)
    u[:, :, ::16] = 0
    u[:, :, 1::16] = 0
    w = layers(rng)
    w[:, :, :8] = 0
    w[:, :, :, :, :, :8] = 0
    for g in range(8):
        u[:, 16 * g, 16 * g, 0] = by
        u[:, 16 * g + 1, 16 * g + 1, 0] = by
        w[:, g, 2, 0, g, 0, 0] = 32
        w[:, g, 2, 0, g, 1, 0] = -32
    return {"x": x.reshape(N, 128, 4 * C), "u": u.reshape(N, 128, 512), "v": d["v"], **weights(rng, w)}
def setup_inputs_copies(rng):
    d = numbers_of(rng)
    o = rng.permutation(N)
    x = d["x"].reshape(N, 8, 16, C, 4)
    for r in range(N):
        k = rng.permutation(C) % 2 if r == o[1] else np.zeros(C, int)
        a = x[r][:, :8, :2].copy()
        x[r][:, :8] = a[:, :, k]
    x[o[0], :, :8] = 0
    u = d["u"].reshape(N, 8, 16, 128, 4)
    u[:, :, 8:, ::16] = 0
    u[:, :, 8:, 1::16] = 0
    w = layers(rng)
    w[:, :, 8:, :, :, :8] = 0
    return {"x": x.reshape(N, 128, 4 * C), "u": u.reshape(N, 128, 512), "v": d["v"], **weights(rng, w)}
def setup_inputs_spread(rng):
    d = setup_inputs(rng)
    d["x"] = big(wide(rng, N, 128, 4 * C, cols=6))
    return d
def check_inputs(d):
    b = []
    for k in ("x", "u", "v"):
        a = np.abs(d[k].astype(np.float32))
        if not (np.isfinite(a).all() and ((a == 0) | (a >= 2.0 ** -30) & (a <= 2.0 ** 30)).all()): b.append("a value of " + k)
    if ((d["wc"] & 127) == 127).any(): b.append("a code of wc is no number")
    for r in range(N):
        a = np.max(np.abs(CODE_VALUE[d["wc"][r]]).reshape(16, 8, 512, 4), axis=(1, 3)) * SCALE_VALUE[mx_ref.live(d["ws"][r])]
        if not ((a == 0) | (a >= 0.875 * 2.0 ** -30) & (a <= 1.125 * 2.0 ** 30)).all(): b.append("the largest size of a block of W")
    return b
def reference(x, u, v, wc, ws):
    qu = [mx_ref.quantize(u[r]) for r in range(N)]
    lay = [pk(wc[r], ws[r]) for r in range(N)]
    now = [x[r] for r in range(N)]
    first = [None] * N
    for t in range(R):
        q = [mx_ref.quantize(now[r]) for r in range(N)]
        n = np.concatenate([lengths(mx_ref.matmul(qu[r], q[r])) for r in range(N)], axis=1)
        mark, body = walk(n)
        for r in range(N):
            own = slice(C * r, C * r + C)
            s = np.argsort(~mark[:, own], axis=1, kind="stable")[:, :A]
            last = np.minimum(s + np.take_along_axis(n[:, own], s, axis=1) - 1, C - 1)
            val = decode(q[r]).astype(BF)
            pack = ((gcols(val, s).astype(np.float32) + gcols(val, last).astype(np.float32)) * np.float32(0.5)).astype(BF)
            sent = mx_ref.quantize(pack)
            w = lay[(r + HOP[t]) % N]
            h = tile([mx_ref.matmul(pick(w, np.arange(128 * b, 128 * b + 128)), sent) * np.float32(0.03125) for b in range(4)])
            came = decode(mx_ref.quantize(h)).astype(BF)
            k = body[:, own]
            now[r] = (now[r].astype(np.float32) + gcols(came, np.where(k < 0, -1, k % A)).astype(np.float32)).astype(BF)
            first[r] = s
    y, ol = np.zeros((N, 128, C), np.float32), np.zeros((N, 8, A), np.float32)
    oc, osc = np.zeros((N, 128, 4 * C), np.uint8), np.zeros((N, 16, C), np.uint8)
    for r in range(N):
        q = mx_ref.quantize(now[r])
        y[r] = mx_ref.matmul(mx_ref.quantize(v[r]), q)
        ol[r] = first[r]
        oc[r], osc[r] = emit(q)
    return {"y": y, "ol": ol, "oc": oc, "osc": osc}

@@ -1,0 +1,396 @@
+from concourse.bass import DstId, RemoteDMATransfer
+from concourse.mybir import dt, AluOpType, ActivationFunctionType
+
+ALU = AluOpType
+ACT = ActivationFunctionType
+N, C, A, R = 4, 192, 48, 3
+HOP = [1, 2, 3]
+RG = 208
+X4, U8 = "float8_e4m3fn_x4", "uint8"
+BF, F32, U16 = "bfloat16", "float32", "uint16"
+
+SCRATCH = {"ps": ("psum", [128, 4096], F32)}
+for _n, _w, _d in [
+        ("ut", 512, BF), ("vt", 512, BF), ("uq", 128, X4), ("us", 128, U8), ("upq", 256, X4), ("ups", 256, U8),
+        ("vq", 128, X4), ("vs", 128, U8), ("wq", 512, X4), ("wsc", 512, U8), ("fq", 128, X4), ("fs", 128, U8),
+        ("eall", 516, BF), ("eq", 512, X4), ("es", 512, U8), ("zt", 512, BF), ("ft", 512, BF), ("ht", 512, BF),
+        ("jm", 256, BF), ("pi", 8, "int32"), ("pf", 8, F32), ("dm", 256, BF), ("rp", 256, BF),
+        ("d3", 576, BF), ("z3", 576, BF), ("n1", 592, BF), ("nw", 7 * RG, BF), ("gm", 256, BF), ("sc", 256, BF),
+        ("uoff", 16, U16), ("x0", 16, U16), ("x1", 66, U16), ("msg", 64, BF),
+        ("ch1", 16, U16), ("ch2", 16, U16), ("osel", 16, U16), ("gsel", 16, U16), ("soff", 16, U16), ("goff", 16, U16),
+        ("k2", 4, U16), ("koff", 12, U16),
+        ("sb", 192, F32), ("junk", 1024, BF), ("jb", 12, F32), ("cb", 12, F32), ("acc", 12, F32), ("kk", 12, F32),
+        ("kq", 12, "int32"), ("kr", 12, F32), ("ks", 12, F32), ("vh", 768, BF), ("vh2", 768, BF), ("fa", 768, BF),
+        ("hw", 256, BF), ("yt", 192, F32)]:
+    SCRATCH[_n] = ("sbuf", [128, _w], _d)
+for _l in range(6):
+    SCRATCH["off%d" % _l] = ("sbuf", [128, 20], U16)
+for _t in range(R + 1):
+    for _n, _w, _d in [("t", 768, BF), ("tq", C, X4), ("ts", C, U8)]:
+        SCRATCH["%s%d" % (_n, _t)] = ("sbuf", [128, _w], _d)
+for _t in range(R):
+    for _n, _w, _d in [("hq", 128, X4), ("hs", 128, U8), ("lq", 176, X4), ("ls", 176, U8), ("gq", C, X4), ("gs", C, U8),
+                       ("ex", 16, BF), ("loff", 12, U16), ("ll", 12, U16), ("cand", 16, BF), ("lc", 16, BF),
+                       ("lm0_", 4, BF), ("lm1_", 4, BF), ("lm2_", 4, BF)]:
+        SCRATCH["%s%d" % (_n, _t)] = ("sbuf", [128, _w], _d)
+
+POOL = {"v": ["v%d" % i for i in range(56)], "s": ["s%d" % i for i in range(30)],
+        "t": ["t%d" % i for i in range(18)], "g": ["g%d" % i for i in range(5)],
+        "d": ["d%d" % i for i in range(14)]}
+SEMAPHORES = ([n for k in "vstgd" for n in POOL[k]] + ["sent"]
+              + ["%s%d" % (n, t) for t in range(R) for n in ("aq", "al", "ac", "ah", "am0_", "am1_", "am2_")])
+
+
+def clash(a, b):
+    return a[0] == b[0] and (a[1] is None or b[1] is None or a[1] == b[1])
+
+
+def keys(xs):
+    return [x if isinstance(x, tuple) else (x, None) for x in xs]
+
+
+def emit(g, T, ops, sent):
+    queues = {"v": g.vector, "s": g.scalar, "t": g.tensor, "g": g, "y": g.sync}
+    known = {q: set() for q in queues}
+    for n, o in enumerate(ops):
+        if o["q"] is None:
+            o["known"] = set()
+            continue
+        deps = set()
+        for m in range(n):
+            p = ops[m]
+            if p["kind"] == "remote" or m in known[o["q"]]:
+                continue
+            if (any(clash(a, b) for a in o["r"] + o["w"] for b in p["w"])
+                    or any(clash(a, b) for a in o["w"] for b in p["r"])):
+                deps.add(m)
+        deps = {m for m in deps if not any(m in ops[k]["known"] for k in deps)}
+        o["waits"] = sorted(deps)
+        for m in deps:
+            ops[m]["need"] = True
+            known[o["q"]] |= {m} | ops[m]["known"]
+        o["known"] = set(known[o["q"]])
+    last = {}
+    tail = []
+    for n, o in enumerate(ops):
+        if o["q"] is None:
+            if not o.get("need"):
+                tail.append(o["sig"])
+            continue
+        q = queues[o["q"]]
+        for m in o["waits"]:
+            q.wait_ge(T.sem[ops[m]["sig"][0]], ops[m]["sig"][1])
+        ins = o["fn"]()
+        if o["kind"] == "remote":
+            continue
+        if o["kind"] == "dma":
+            name = [s for s in POOL["d"] if s not in last][0]
+            last[name] = n
+            o["sig"] = (name, 16)
+            ins.then_inc(T.sem[name], 16)
+            if not o.get("need"):
+                tail.append(o["sig"])
+        elif o.get("need"):
+            name = [s for s in POOL[o["q"]] if s not in last or last[s] in o["known"]][0]
+            o["sig"] = (name, ops[last[name]]["sig"][1] + 1 if name in last else 1)
+            last[name] = n
+            ins.then_inc(T.sem[name], 1)
+    tail.insert(0, ("sent", sent[0]))
+    for name, val in tail:
+        g.wait_ge(T.sem[name], val)
+
+
+def rank_program(g, core, T, topo):
+    rank = T.rank_of(core)
+    if rank is None:
+        return
+    ops = []
+    sent = [0]
+    V, S, PE = g.vector, g.scalar, g.tensor
+    sem = T.sem
+
+    def op(q, fn, r=(), w=(), kind="compute"):
+        ops.append({"q": q, "fn": fn, "r": keys(r), "w": keys(w), "kind": kind})
+
+    def arrive(name, val, w):
+        ops.append({"q": None, "r": [], "w": keys(w), "kind": "arrive", "sig": (name, val)})
+
+    def ts(out, in0, s1, s2, o0, o1, r, w):
+        if o1 is None:
+            op("v", lambda: V.tensor_scalar(out, in0, s1, None, o0), r, w)
+        else:
+            op("v", lambda: V.tensor_scalar(out, in0, s1, s2, o0, o1), r, w)
+
+    def tt(out, a, b, o, r, w):
+        op("v", lambda: V.tensor_tensor(out, a, b, o), r, w)
+
+    def cp(out, a, r, w):
+        op("v", lambda: V.tensor_copy(out, a), r, w)
+
+    def ms(out, c, w):
+        op("v", lambda: V.memset(out, c), (), w)
+
+    def scan(out, d0, d1, r, w):
+        op("v", lambda: V.tensor_tensor_scan(out, d0, d1, 0.0, ALU.mult, ALU.add), r, w)
+
+    def act(out, a, r, w, scale=None):
+        if scale is None:
+            op("s", lambda: S.activation(out, a, ACT.Copy), r, w)
+        else:
+            op("s", lambda: S.activation(out, a, ACT.Copy, scale=scale), r, w)
+
+    def quant(q, s, a, r, w):
+        op("v", lambda: V.quantize_mx(q, s, a), r, w)
+
+    def mm(bank, n, lq, ls, rq, rs, r):
+        op("t", lambda: PE.matmul_mx(T.ps[:, 512 * bank:512 * bank + n], lq, ls, rq, rs, True, True), r, [("ps", bank)])
+
+    def dma(q, out, a, r, w):
+        e = {"y": g.sync, "s": S}[q]
+        op(q, lambda: e.dma_start(out, a), r, w, "dma")
+
+    def iota(out, pattern, base, w):
+        op("g", lambda: g.iota(out, pattern, base, 0, allow_small_or_imprecise_dtypes=True), (), w)
+
+    def send(to, out, a, name, r):
+        dst = T.cores[to]
+        rid, pid = topo.addr(dst)[:2]
+        sent[0] += len(topo.engines(core, dst))
+        op("g", lambda: g.remote_dma(out, a, sem[name], sem.sent, pid, rid, topo.mask(core, dst)), r, (), "remote")
+
+    def width(frm):
+        return len(topo.engines(T.cores[frm], core))
+
+    def ps(bank, a, b):
+        return T.ps[:, 512 * bank + a:512 * bank + b]
+
+    def u8(v):
+        return v.bitcast(dt.uint8)
+
+    def col(q, b):
+        return q[:, 128 * b:128 * b + 128]
+
+    dma("y", T.t0[:], T.x[:], (), ["t0"])
+    dma("s", T.ut[:], T.u[:], (), ["ut"])
+    dma("y", u8(T.wq[:]), T.wc[:], (), ["wq"])
+    dma("s", T.wsc[:], T.ws[:], (), ["wsc"])
+    dma("y", T.vt[:], T.v[:], (), ["vt"])
+
+    op("g", lambda: g.iota(T.pi[:, 0:1], [[0, 1]], 0, 1), (), [("pi", 0)])
+    iota(T.jm[:], [[0, 16], [1, 16]], 0, ["jm"])
+    iota(T.nw[:, 0:RG], [[1, RG]], 0, [("nw", 0)])
+    iota(T.z3[:, 0:576:3], [[1, C]], 1, [("z3", 0)])
+    ms(T.d3[:], 1.0, ["d3"])
+    ms(T.rp[:], 1.0, ["rp"])
+    ms(T.n1[:, 576:592], 0.0, [("n1", 1)])
+    ts(T.pi[:, 1:2], T.pi[:, 0:1], 15, None, ALU.bitwise_and, None, [("pi", 0)], [("pi", 1)])
+    ms(T.d3[:, 0:576:3], 0.0, ["d3"])
+    ms(T.rp[:, 0:256:16], 0.0, ["rp"])
+    cp(T.pf[:, 0:2], T.pi[:, 0:2], [("pi", 0), ("pi", 1)], [("pf", 0)])
+    for l in range(4):
+        ts(T.pi[:, 2 + l:3 + l], T.pi[:, 1:2], l, 1, ALU.logical_shift_right, ALU.bitwise_and, [("pi", 1)], [("pi", 2 + l)])
+    ts(T.uoff[:, 0:8], T.jm[:, 0:8], 16.0, None, ALU.mult, None, ["jm"], [("uoff", 0)])
+    ts(T.uoff[:, 8:16], T.jm[:, 0:8], 16.0, 1.0, ALU.mult, ALU.add, ["jm"], [("uoff", 1)])
+    ts(T.dm[:], T.jm[:], T.pf[:, 1:2], None, ALU.is_equal, None, ["jm", ("pf", 0)], ["dm"])
+    for e in range(4):
+        ts(T.off0[:, 12 + e:13 + e], T.pi[:, 2:3], float(2 * e - 586), float(588 + e), ALU.mult, ALU.add,
+           [("pi", 2)], [("off0", 1 + e)])
+    for l in range(1, 4):
+        ts(T.pf[:, 1 + l:2 + l], T.pi[:, 2 + l:3 + l], float(RG * l), None, ALU.mult, None, [("pi", 2 + l)], [("pf", l)])
+    ms(T.eall[:], 0.0, ["eall"])
+    cp(T.n1[:, 578:590:3], T.nw[:, C:C + 4], [("nw", 0)], [("n1", 1)])
+    cp(T.n1[:, 588:592], T.jm[:, 0:4], ["jm"], [("n1", 1)])
+    ts(T.eall[:, 3:515:4], T.nw[:, 0:128], T.pf[:, 0:1], None, ALU.is_equal, None, [("nw", 0), ("pf", 0)], ["eall"])
+    for l in range(1, 7):
+        act(T.nw[:, RG * l + C:RG * l + RG], T.nw[:, C:RG], [("nw", 0)], [("nw", 10 + l)])
+
+    def e_tile(b):
+        quant(col(T.eq, b), col(T.es, b), T.eall[:, 3 - b:515 - b], ["eall"], [("eq", b)])
+
+    def pad(t):
+        quant(T["lq%d" % t][:, A:176], T["ls%d" % t][:, A:176], T.zt[:], ["zt"], [("l%d" % t, "pad")])
+
+    soon = [lambda b=b: e_tile(b) for b in range(4)]
+    soon.append(lambda: ts(T.pf[:, 5:6], T.pf[:, 1:2], 3.0, None, ALU.min, None, [("pf", 0)], [("pf", 4)]))
+    shade = [lambda: ms(T.ft[:, 4 * A:], 0.0, [("ft", 9)]), lambda: ms(T.ht[:, 4 * A:], 0.0, [("ht", 9)])]
+    late = [lambda: ts(T.cb[:], T.jm[:, 0:12], 20.0, 16.0, ALU.mult, ALU.add, ["jm"], ["cb"]),
+            lambda: ts(T.kr[:], T.jm[:, 0:12], 16.0, 0.5, ALU.mult, ALU.add, ["jm"], ["kr"]),
+            lambda: ms(T.zt[:], 0.0, ["zt"]),
+            lambda: ts(T.jb[:], T.kr[:], T.pf[:, 1:2], None, ALU.add, None, ["kr", ("pf", 0)], ["jb"]),
+            lambda: ms(T.hw[:], 0.0, ["hw"]), lambda: pad(0)]
+    shade += late
+    late = [lambda: pad(1), lambda: pad(2), lambda: quant(T.vq[:], T.vs[:], T.vt[:], ["vt"], ["vq"])]
+
+    quant(T.uq[:], T.us[:], T.ut[:], ["ut"], ["uq"])
+    n64 = T.nw[:, 6 * RG:7 * RG]
+    N64 = [("nw", 6), ("nw", 16)]
+
+    for t in range(R):
+        def B(name):
+            return T["%s%d" % (name, t)]
+
+        def K(name):
+            return "%s%d" % (name, t)
+
+        helper, guest = (rank + HOP[t]) % N, (rank - HOP[t]) % N
+        tq, tsc = B("tq"), B("ts")
+        quant(tq[:], tsc[:], B("t")[:], [K("t")], [K("tq")])
+        send(helper, u8(B("gq")[:]), u8(tq[:]), K("aq"), [K("tq")])
+        send(helper, B("gs")[:], tsc[:], K("aq"), [K("tq")])
+        if t == 0:
+            cp(T.upq[:].bitcast(dt.uint32), T.uq[:].bitcast(dt.uint32).indirect(T.uoff[:]), ["uq", "uoff"], ["upq"])
+            act(T.ups[:], T.us[:].indirect(T.uoff[:]), ["uq", "uoff"], ["ups"])
+        for k in range(2):
+            mm(k, C, col(T.upq, k), col(T.ups, k), tq[:], tsc[:], ["upq", "ups", K("tq")])
+        ts(T.z3[:, 1:576:3], ps(0, 0, C), 0.0, None, ALU.is_gt, None, (), [("ps", 0), ("z3", 1)])
+        ts(T.z3[:, 2:576:3], ps(1, 0, C), 0.0, 2.0, ALU.is_gt, ALU.mult, (), [("ps", 1), ("z3", 2)])
+        scan(T.n1[:, 0:576], T.d3[:], T.z3[:], ["d3", "z3"], [("n1", 0)])
+        tt(T.gm[:, 0:C], T.n1[:, 2:576:3], T.dm[:, 0:C], ALU.mult, [("n1", 0), "dm"], ["gm"])
+        scan(T.sc[:, 0:C], T.rp[:, 0:C], T.gm[:, 0:C], ["rp", "gm"], ["sc"])
+        ts(T.off0[:, 0:12], T.sc[:, 15:C:16], 3.0, 2.0, ALU.mult, ALU.add, ["sc"], [("off0", 0)])
+        ts(B("loff")[:], T.sc[:, 15:C:16], -1.0, float(C - 1), ALU.add, ALU.min, ["sc"], [K("loff")])
+        send(helper, B("ll")[:], B("loff")[:], K("al"), [K("loff")])
+        cand = B("cand")
+        for l in range(5):
+            off, nxt = T["off%d" % l], T["off%d" % (l + 1)]
+            on, nn = "off%d" % l, "off%d" % (l + 1)
+            win = T.n1[:] if l == 0 else T.nw[:, 0:RG * (l + 1)]
+            wk = ["n1"] if l == 0 else [("nw", i) for i in range(l + 1)] + [("nw", 10 + i) for i in range(1, l + 1)]
+            act(T.nw[:, RG * (l + 1):RG * (l + 1) + C], win.indirect(off[:, 0:12]), wk + [on], [("nw", l + 1)])
+            tt(T.gm[:], win.indirect(off[:, 0:16]), T.dm[:], ALU.mult, wk + [on, "dm"], ["gm"])
+            if t == 0:
+                soon.pop(0)()
+            scan(T.sc[:], T.rp[:], T.gm[:], ["rp", "gm"], ["sc"])
+            base = float(RG * (l + 1))
+            if l < 3:
+                ts(nxt[:, 0:12], T.sc[:, 15:C:16], base, None, ALU.add, None, ["sc"], [(nn, 0)])
+                ts(nxt[:, 12:16], T.sc[:, C + 15:256:16], T.pf[:, 2 + l:3 + l], None, ALU.add, None, ["sc", ("pf", l + 1)], [(nn, 1)])
+            else:
+                ts(nxt[:, 0:16], T.sc[:, 15:256:16], base, None, ALU.add, None, ["sc"], [(nn, 0)])
+                cp(cand[:, l - 3:16:4], T.sc[:, C + 15:256:16], ["sc"], [(K("cand"), l - 3)])
+                if l == 3:
+                    ts(T.off5[:, 16:20], T.sc[:, C + 15:256:16], float(RG * 5), None, ALU.add, None, ["sc"], [("off5", 1)])
+        win = T.nw[:, 0:RG * 6]
+        wk = [("nw", i) for i in range(6)] + [("nw", 10 + i) for i in range(1, 6)]
+        act(T.nw[:, RG * 6:RG * 6 + C], win.indirect(T.off5[:, 0:12]), wk + [("off5", 0)], [("nw", 6)])
+        ex = B("ex")
+        if rank < N - 1:
+            cp(T.x0[:], win.indirect(T.off5[:, 0:1]), wk + [("off5", 0)], ["x0"])
+        tt(T.gm[:, 0:128], win.indirect(T.off5[:, 12:20]), T.dm[:, 0:128], ALU.mult, wk + ["off5", "dm"], ["gm"])
+        if rank == 0:
+            cp(T.x1[:, 0:16], n64.indirect(T.x0[:, 0:1]), N64 + ["x0"], ["x1"])
+        elif rank < N - 1:
+            cp(T.x1[:, 1:65], n64.indirect(T.x0[:, 0:4]), N64 + ["x0"], ["x1"])
+        scan(T.sc[:, 0:128], T.rp[:, 0:128], T.gm[:, 0:128], ["rp", "gm"], ["sc"])
+        if rank == 0:
+            ts(ex[:], n64.indirect(T.x1[:, 0:1]), -float(C), None, ALU.add, None, N64 + ["x1"], [K("ex")])
+        elif rank < N - 1:
+            for h in range(2):
+                ts(T.msg[:, 32 * h:32 * h + 32], n64.indirect(T.x1[:, 16 + 32 * h:18 + 32 * h]), -float(C), None,
+                   ALU.add, None, N64 + ["x1"], [("msg", h)])
+        cp(cand[:, 2:16:4], T.sc[:, 79:128:16], ["sc"], [(K("cand"), 2)])
+        if 0 < rank < N - 1:
+            cp(ex[:, 0:4], T.msg[:, 0:64:16], ["msg"], [K("ex")])
+        cp(cand[:, 3:16:4], T.sc[:, 15:64:16], ["sc"], [(K("cand"), 3)])
+        if rank < N - 1:
+            wd = 2 if rank == 0 else 4
+            to = [T.cores[r] for r in range(N) if r != rank and max(r, (r - HOP[t]) % N) > rank]
+            sent[0] += len(topo.engines(core, to[0]))
+            tr = RemoteDMATransfer(dst_ids=[DstId(rid=topo.addr(c)[0], pnc=topo.addr(c)[1]) for c in to],
+                                   dma_engine_mask=topo.mask(core, to[0]), remote_sem=sem[K("am%d_" % rank)],
+                                   srcs=[ex[:, 0:wd]], dsts=[B("lm%d_" % rank)[:, 0:wd] for c in to])
+            op("g", lambda tr=tr: g.remote_dma_fused([tr], local_sem=sem.sent), [K("ex")], (), "remote")
+        wd = 4 if rank == 0 else 16
+        send(helper, B("lc")[:, 0:wd], cand[:, 0:wd], K("ac"), [K("cand")])
+        arrive(K("aq"), 2 * width(guest), [K("gq")])
+        arrive(K("al"), width(guest), [K("ll")])
+        arrive(K("ac"), width(guest), [K("lc")])
+        for b in range(4):
+            mm(2 + b, C, col(T.eq, b), col(T.es, b), B("gq")[:], B("gs")[:], [("eq", b), K("gq")])
+        for b in range(4):
+            act(T.vh[:, C * b:C * b + C], ps(2 + b, 0, C), (), [("ps", 2 + b), ("vh", b)], 0.5)
+            act(T.vh2[:, C * b:C * b + C], ps(2 + b, 0, C), (), [("ps", 2 + b), ("vh2", b)], 0.5)
+        while shade:
+            shade.pop(0)()
+        for b in range(4):
+            tt(T.fa[:, C * b:C * b + C], T.vh[:, C * b:C * b + C].indirect(B("ll")[:]), T.vh2[:, C * b:C * b + C], ALU.add,
+               [("vh", b), ("vh2", b), K("ll")], [("fa", b)])
+        for r in range(max(rank, guest)):
+            if r != rank:
+                arrive(K("am%d_" % r), width(r), [K("lm%d_" % r)])
+        have = [0]
+
+        def exits(r):
+            name = "ex" if r == rank else "lm%d_" % r
+            if r == 0:
+                return B(name)[:, 0:2], [K(name)], 2
+            return B(name)[:, 0:4].indirect(T["ch%d" % r][:, 0:1]), [K(name), "ch%d" % r], 16
+
+        def pick(r, lists, ln, sel, out):
+            if r == 0:
+                cp(T[out][:, 0:4], lists[:, 0:4], [ln], [out])
+                return
+            while have[0] < r - 1:
+                src, rk, n = exits(have[0])
+                have[0] += 1
+                cp(T["ch%d" % have[0]][:, 0:n], src, rk, ["ch%d" % have[0]])
+            src, rk, n = exits(r - 1)
+            ts(T[sel][:, 0:n], src, 4.0, T.pf[:, 5:6], ALU.mult, ALU.add, rk + [("pf", 4)], [sel])
+            cp(T[out][:], lists[:].indirect(T[sel][:, 0:1]), [ln, sel], [out])
+
+        pick(guest, B("lc"), K("lc"), "gsel", "goff")
+        for b in range(4):
+            src = T.fa[:, C * b:C * b + C].indirect(T.goff[:, 0:3])
+            (cp if b % 2 == 0 else act)(T.ft[:, b:4 * A:4], src, [("fa", b), "goff"], [("ft", b)])
+        quant(T.fq[:], T.fs[:], T.ft[:], ["ft"], ["fq"])
+        for b in range(4):
+            mm(2 + b, 128, col(T.wq, b), col(T.wsc, b), T.fq[:], T.fs[:], ["wq", "wsc", "fq"])
+        pick(rank, cand, K("cand"), "osel", "soff")
+        for b in range(4):
+            if b % 2 == 0:
+                ts(T.ht[:, b:4 * A:4], ps(2 + b, 0, A), 0.03125, None, ALU.mult, None, (), [("ps", 2 + b), ("ht", b)])
+            else:
+                act(T.ht[:, b:4 * A:4], ps(2 + b, 0, A), (), [("ps", 2 + b), ("ht", b)], 0.03125)
+        quant(B("hq")[:], B("hs")[:], T.ht[:], ["ht"], [K("hq")])
+        send(guest, u8(B("lq")[:, 0:A]), u8(B("hq")[:, 0:A]), K("ah"), [K("hq")])
+        send(guest, B("ls")[:, 0:A], B("hs")[:, 0:A], K("ah"), [K("hq")])
+        act(T.sb[:, 0:64], T.nw[:, 0:RG].indirect(T.soff[:, 0:4]), [("nw", 0), "soff"], [("sb", 0)])
+        act(T.sb[:, 64:128], n64.indirect(T.soff[:, 0:4]), N64 + ["soff"], [("sb", 1)])
+        tt(T.gm[:, 0:64], n64.indirect(T.soff[:, 0:4]), T.dm[:, 0:64], ALU.mult, N64 + ["soff", "dm"], ["gm"])
+        scan(T.sc[:, 0:64], T.rp[:, 0:64], T.gm[:, 0:64], ["rp", "gm"], ["sc"])
+        cp(T.k2[:], T.sc[:, 15:64:16], ["sc"], ["k2"])
+        cp(T.sb[:, 128:192], n64.indirect(T.k2[:]), N64 + ["k2"], [("sb", 2)])
+        while late:
+            late.pop(0)()
+        for c in range(12):
+            lo, hi, at = 4 * c, 16 * c + 16, 6 * c * (c - 1) + 16 * c
+            op("s", lambda c=c, lo=lo, hi=hi, at=at: S.activation(
+                T.junk[:, at:at + hi - lo], T.sb[:, lo:hi], ACT.Sign, bias=T.jb[:, c:c + 1], scale=-1.0,
+                accum_out=T.acc[:, c:c + 1]), [("sb", i) for i in range((hi + 63) // 64)] + ["jb"], [("acc", c), ("junk", c)])
+        tt(T.kk[:], T.acc[:], T.cb[:], ALU.add, ["acc", "cb"], ["kk"])
+        ts(T.kq[:], T.kk[:], -49.0, 1.0 / 96.0, ALU.add, ALU.mult, ["kk"], ["kq"])
+        ts(T.kr[:], T.kq[:], 0.0, -96.0, ALU.max, ALU.mult, ["kq"], ["kr"])
+        tt(T.ks[:], T.kk[:], T.kr[:], ALU.add, ["kk", "kr"], ["ks"])
+        ts(T.koff[:], T.ks[:], 0.5, None, ALU.mult, None, ["ks"], ["koff"])
+        if t == R - 1:
+            dma("y", T.ol[:], T.sb[0:128:16, 0:A], [("sb", 0)], ())
+        arrive(K("ah"), 2 * width(helper), [(K("l"), "h")])
+        banks = [0, 1, 6, 7]
+        for b in range(4):
+            mm(banks[b], 128, col(T.eq, b), col(T.es, b), B("lq")[:, 0:128], B("ls")[:, 0:128], [("eq", b), K("l")])
+        for b in range(4):
+            act(T.hw[:, 64 * b + 1:64 * b + 1 + A], ps(banks[b], 0, A), (), [("ps", banks[b]), ("hw", b)])
+        new = "t%d" % (t + 1)
+        for b in range(4):
+            tt(T[new][:, b:4 * C:4], T.hw[:, 64 * b:64 * b + 64].indirect(T.koff[:]), B("t")[:, b:4 * C:4], ALU.add,
+               [("hw", b), "koff", K("t")], [(new, b)])
+
+    tq, tsc, qn = T["tq%d" % R], T["ts%d" % R], "tq%d" % R
+    quant(tq[:], tsc[:], T["t%d" % R][:], ["t%d" % R], [qn])
+    mm(2, C, T.vq[:], T.vs[:], tq[:], tsc[:], ["vq", qn])
+    dma("y", T.oc[:], u8(tq[:]), [qn], ())
+    cp(T.yt[:], ps(2, 0, C), (), [("ps", 2), "yt"])
+    for k in range(4):
+        dma("s", T.osc[4 * k:4 * k + 4, :], tsc[32 * k:32 * k + 4, :], [qn], ())
+    dma("y", T.y[:], T.yt[:], ["yt"], ())
+    emit(g, T, ops, sent)

@@ -1,11 +1,12 @@
 from concourse.bass import DstId, RemoteDMATransfer
-from concourse.mybir import dt, AluOpType, ActivationFunctionType
+from concourse.mybir import dt, AluOpType, ActivationFunctionType, AxisListType
 
 ALU = AluOpType
 ACT = ActivationFunctionType
 N, C, A, R = 4, 192, 48, 3
 HOP = [1, 2, 3]
 RG = 208
+SPLIT = 11
 X4, U8 = "float8_e4m3fn_x4", "uint8"
 BF, F32, U16 = "bfloat16", "float32", "uint16"
 
@@ -14,14 +15,14 @@ for _n, _w, _d in [
         ("ut", 512, BF), ("vt", 512, BF), ("uq", 128, X4), ("us", 128, U8), ("upq", 256, X4), ("ups", 256, U8),
         ("vq", 128, X4), ("vs", 128, U8), ("wq", 512, X4), ("wsc", 512, U8), ("fq", 128, X4), ("fs", 128, U8),
         ("eall", 516, BF), ("eq", 512, X4), ("es", 512, U8), ("zt", 512, BF), ("ft", 512, BF), ("ht", 512, BF),
-        ("jm", 256, BF), ("pi", 8, "int32"), ("pf", 8, F32), ("dm", 256, BF), ("rp", 256, BF),
-        ("d3", 576, BF), ("z3", 576, BF), ("n1", 592, BF), ("nw", 7 * RG, BF), ("gm", 256, BF), ("sc", 256, BF),
-        ("uoff", 16, U16), ("x0", 16, U16), ("x1", 66, U16), ("msg", 64, BF),
-        ("ch1", 16, U16), ("ch2", 16, U16), ("osel", 16, U16), ("gsel", 16, U16), ("soff", 16, U16), ("goff", 16, U16),
+        ("jm", 256, BF), ("pi", 8, "int32"), ("pf", 10, F32), ("dm", 256, BF), ("rp", 256, BF),
+        ("d3", 576, BF), ("d3m", 576, BF), ("z3", 576, BF), ("n1", 592, BF), ("n1m", 576, BF), ("nw", 7 * RG, BF),
+        ("gm", 256, BF), ("sc", 256, BF), ("uoff", 16, U16), ("x0", 16, U16), ("x1", 66, U16), ("msg", 64, BF),
+        ("ch2", 16, U16), ("osel", 16, U16), ("gsel", 16, U16), ("soff", 16, U16), ("goff", 16, U16),
         ("k2", 4, U16), ("koff", 12, U16),
-        ("sb", 192, F32), ("junk", 1024, BF), ("jb", 12, F32), ("cb", 12, F32), ("acc", 12, F32), ("kk", 12, F32),
-        ("kq", 12, "int32"), ("kr", 12, F32), ("ks", 12, F32), ("vh", 768, BF), ("vh2", 768, BF), ("fa", 768, BF),
-        ("hw", 256, BF), ("yt", 192, F32)]:
+        ("sb", 192, F32), ("junk", 1024, BF), ("jb", 12, F32), ("cb", 12, F32), ("acc", 12, F32), ("kr", 12, F32),
+        ("m0", 12, F32), ("m1", 12, F32), ("m2", 12, F32), ("m3", 12, F32), ("m4", 12, F32), ("m5", 12, F32),
+        ("ks", 12, F32), ("vh", 768, BF), ("vh2", 768, BF), ("fa", 768, BF), ("hw", 256, BF), ("yt", 192, F32)]:
     SCRATCH[_n] = ("sbuf", [128, _w], _d)
 for _l in range(6):
     SCRATCH["off%d" % _l] = ("sbuf", [128, 20], U16)
@@ -30,8 +31,8 @@ for _t in range(R + 1):
         SCRATCH["%s%d" % (_n, _t)] = ("sbuf", [128, _w], _d)
 for _t in range(R):
     for _n, _w, _d in [("hq", 128, X4), ("hs", 128, U8), ("lq", 176, X4), ("ls", 176, U8), ("gq", C, X4), ("gs", C, U8),
-                       ("ex", 16, BF), ("loff", 12, U16), ("ll", 12, U16), ("cand", 16, BF), ("lc", 16, BF),
-                       ("lm0_", 4, BF), ("lm1_", 4, BF), ("lm2_", 4, BF)]:
+                       ("ex", 4, BF), ("eu", 16, U16), ("loff", 12, U16), ("ll", 12, U16), ("cand", 16, BF), ("lc", 12, BF),
+                       ("lm0_", 2, U16), ("lm1_", 4, BF), ("lm2_", 4, BF)]:
         SCRATCH["%s%d" % (_n, _t)] = ("sbuf", [128, _w], _d)
 
 POOL = {"v": ["v%d" % i for i in range(56)], "s": ["s%d" % i for i in range(30)],
@@ -130,8 +131,8 @@ def rank_program(g, core, T, topo):
     def ms(out, c, w):
         op("v", lambda: V.memset(out, c), (), w)
 
-    def scan(out, d0, d1, r, w):
-        op("v", lambda: V.tensor_tensor_scan(out, d0, d1, 0.0, ALU.mult, ALU.add), r, w)
+    def scan(out, d0, d1, r, w, o1=ALU.add):
+        op("v", lambda: V.tensor_tensor_scan(out, d0, d1, 0.0, ALU.mult, o1), r, w)
 
     def act(out, a, r, w, scale=None):
         if scale is None:
@@ -153,10 +154,16 @@ def rank_program(g, core, T, topo):
         op("g", lambda: g.iota(out, pattern, base, 0, allow_small_or_imprecise_dtypes=True), (), w)
 
     def send(to, out, a, name, r):
-        dst = T.cores[to]
-        rid, pid = topo.addr(dst)[:2]
-        sent[0] += len(topo.engines(core, dst))
-        op("g", lambda: g.remote_dma(out, a, sem[name], sem.sent, pid, rid, topo.mask(core, dst)), r, (), "remote")
+        dst = [T.cores[k] for k in to]
+        sent[0] += len(topo.engines(core, dst[0]))
+        if len(dst) == 1:
+            rid, pid = topo.addr(dst[0])[:2]
+            op("g", lambda: g.remote_dma(out, a, sem[name], sem.sent, pid, rid, topo.mask(core, dst[0])), r, (), "remote")
+        else:
+            tr = RemoteDMATransfer(dst_ids=[DstId(rid=topo.addr(c)[0], pnc=topo.addr(c)[1]) for c in dst],
+                                   dma_engine_mask=topo.mask(core, dst[0]), remote_sem=sem[name], srcs=[a],
+                                   dsts=[out for c in dst])
+            op("g", lambda: g.remote_dma_fused([tr], local_sem=sem.sent), r, (), "remote")
 
     def width(frm):
         return len(topo.engines(T.cores[frm], core))
@@ -170,6 +177,17 @@ def rank_program(g, core, T, topo):
     def col(q, b):
         return q[:, 128 * b:128 * b + 128]
 
+    def table(l):
+        if l == 0:
+            return T.n1[:], ["n1"]
+        return T.nw[:, 0:RG * (l + 1)], [("nw", i) for i in range(l + 1)] + [("nw", 10 + i) for i in range(1, l + 1)]
+
+    def jump(win, wk, offs, on, n):
+        tt(T.gm[:, 0:n], win.indirect(offs), T.dm[:, 0:n], ALU.mult, wk + [on, "dm"], ["gm"])
+
+    def fold(n):
+        scan(T.sc[:, 0:n], T.rp[:, 0:n], T.gm[:, 0:n], ["rp", "gm"], ["sc"])
+
     dma("y", T.t0[:], T.x[:], (), ["t0"])
     dma("s", T.ut[:], T.u[:], (), ["ut"])
     dma("y", u8(T.wq[:]), T.wc[:], (), ["wq"])
@@ -181,6 +199,8 @@ def rank_program(g, core, T, topo):
     iota(T.nw[:, 0:RG], [[1, RG]], 0, [("nw", 0)])
     iota(T.z3[:, 0:576:3], [[1, C]], 1, [("z3", 0)])
     ms(T.d3[:], 1.0, ["d3"])
+    ms(T.d3m[:, 1:576:3], 1.0, [("d3m", 1)])
+    ms(T.d3m[:, 0:576:3], 0.0, [("d3m", 0)])
     ms(T.rp[:], 1.0, ["rp"])
     ms(T.n1[:, 576:592], 0.0, [("n1", 1)])
     ts(T.pi[:, 1:2], T.pi[:, 0:1], 15, None, ALU.bitwise_and, None, [("pi", 0)], [("pi", 1)])
@@ -198,6 +218,7 @@ def rank_program(g, core, T, topo):
     for l in range(1, 4):
         ts(T.pf[:, 1 + l:2 + l], T.pi[:, 2 + l:3 + l], float(RG * l), None, ALU.mult, None, [("pi", 2 + l)], [("pf", l)])
     ms(T.eall[:], 0.0, ["eall"])
+    ts(T.d3m[:, 2:576:3], T.dm[:, 0:C], 1001.0, -1000.0, ALU.mult, ALU.add, ["dm"], [("d3m", 2)])
     cp(T.n1[:, 578:590:3], T.nw[:, C:C + 4], [("nw", 0)], [("n1", 1)])
     cp(T.n1[:, 588:592], T.jm[:, 0:4], ["jm"], [("n1", 1)])
     ts(T.eall[:, 3:515:4], T.nw[:, 0:128], T.pf[:, 0:1], None, ALU.is_equal, None, [("nw", 0), ("pf", 0)], ["eall"])
@@ -210,16 +231,17 @@ def rank_program(g, core, T, topo):
     def pad(t):
         quant(T["lq%d" % t][:, A:176], T["ls%d" % t][:, A:176], T.zt[:], ["zt"], [("l%d" % t, "pad")])
 
-    soon = [lambda b=b: e_tile(b) for b in range(4)]
-    soon.append(lambda: ts(T.pf[:, 5:6], T.pf[:, 1:2], 3.0, None, ALU.min, None, [("pf", 0)], [("pf", 4)]))
-    shade = [lambda: ms(T.ft[:, 4 * A:], 0.0, [("ft", 9)]), lambda: ms(T.ht[:, 4 * A:], 0.0, [("ht", 9)])]
-    late = [lambda: ts(T.cb[:], T.jm[:, 0:12], 20.0, 16.0, ALU.mult, ALU.add, ["jm"], ["cb"]),
-            lambda: ts(T.kr[:], T.jm[:, 0:12], 16.0, 0.5, ALU.mult, ALU.add, ["jm"], ["kr"]),
-            lambda: ms(T.zt[:], 0.0, ["zt"]),
-            lambda: ts(T.jb[:], T.kr[:], T.pf[:, 1:2], None, ALU.add, None, ["kr", ("pf", 0)], ["jb"]),
-            lambda: ms(T.hw[:], 0.0, ["hw"]), lambda: pad(0)]
-    shade += late
-    late = [lambda: pad(1), lambda: pad(2), lambda: quant(T.vq[:], T.vs[:], T.vt[:], ["vt"], ["vq"])]
+    soon = [
+        lambda: e_tile(2),
+        lambda: ts(T.pf[:, 5:6], T.pf[:, 1:2], 2.0, None, ALU.min, None, [("pf", 0)], [("pf", 4)]),
+        lambda: e_tile(3),
+        lambda: ts(T.pf[:, 6:7], T.pf[:, 1:2], 3.0, None, ALU.is_ge, None, [("pf", 0)], [("pf", 5)]),
+        lambda: ts(T.pf[:, 7:8], T.pf[:, 6:7], -2.0, 3.0, ALU.mult, ALU.add, [("pf", 5)], [("pf", 6)]),
+        lambda: ts(T.pf[:, 8:9], T.pf[:, 6:7], 10.0, T.pf[:, 5:6], ALU.mult, ALU.add, [("pf", 5), ("pf", 4)], [("pf", 7)]),
+        lambda: ts(T.kr[:], T.jm[:, 0:12], 16.0, 0.5, ALU.mult, ALU.add, ["jm"], ["kr"]),
+        lambda: ts(T.cb[:, 0:SPLIT], T.jm[:, 0:SPLIT], 20.0, 16.0, ALU.mult, ALU.add, ["jm"], [("cb", 0)]),
+        lambda: ts(T.jb[:], T.kr[:], T.pf[:, 1:2], None, ALU.add, None, ["kr", ("pf", 0)], ["jb"]),
+        lambda: ts(T.cb[:, SPLIT:12], T.jm[:, SPLIT:12], 8.0, None, ALU.mult, None, ["jm"], [("cb", 1)])]
 
     quant(T.uq[:], T.us[:], T.ut[:], ["ut"], ["uq"])
     n64 = T.nw[:, 6 * RG:7 * RG]
@@ -232,145 +254,183 @@ def rank_program(g, core, T, topo):
         def K(name):
             return "%s%d" % (name, t)
 
+        def unpack(n):
+            b, name = n // 2, ("vh", "vh2")[n % 2]
+            act(T[name][:, C * b:C * b + C], ps(2 + b, 0, C), (), [("ps", 2 + b), (name, b)], 0.5)
+
         helper, guest = (rank + HOP[t]) % N, (rank - HOP[t]) % N
         tq, tsc = B("tq"), B("ts")
         quant(tq[:], tsc[:], B("t")[:], [K("t")], [K("tq")])
-        send(helper, u8(B("gq")[:]), u8(tq[:]), K("aq"), [K("tq")])
-        send(helper, B("gs")[:], tsc[:], K("aq"), [K("tq")])
+        send([helper], u8(B("gq")[:]), u8(tq[:]), K("aq"), [K("tq")])
+        send([helper], B("gs")[:], tsc[:], K("aq"), [K("tq")])
         if t == 0:
             cp(T.upq[:].bitcast(dt.uint32), T.uq[:].bitcast(dt.uint32).indirect(T.uoff[:]), ["uq", "uoff"], ["upq"])
             act(T.ups[:], T.us[:].indirect(T.uoff[:]), ["uq", "uoff"], ["ups"])
+            act(T.zt[:], T.d3[:, 0:512], ["d3"], ["zt"], 0.0)
+            act(T.ft[:, 4 * A:], T.d3[:, 4 * A:512], ["d3"], [("ft", 9)], 0.0)
+            act(T.ht[:, 4 * A:], T.d3[:, 4 * A:512], ["d3"], [("ht", 9)], 0.0)
+            e_tile(0)
+            e_tile(1)
+        else:
+            pad(t)
+            if t == 1:
+                quant(T.vq[:], T.vs[:], T.vt[:], ["vt"], ["vq"])
         for k in range(2):
             mm(k, C, col(T.upq, k), col(T.ups, k), tq[:], tsc[:], ["upq", "ups", K("tq")])
         ts(T.z3[:, 1:576:3], ps(0, 0, C), 0.0, None, ALU.is_gt, None, (), [("ps", 0), ("z3", 1)])
         ts(T.z3[:, 2:576:3], ps(1, 0, C), 0.0, 2.0, ALU.is_gt, ALU.mult, (), [("ps", 1), ("z3", 2)])
+        scan(T.n1m[:], T.d3m[:], T.z3[:], ["d3m", "z3"], ["n1m"])
         scan(T.n1[:, 0:576], T.d3[:], T.z3[:], ["d3", "z3"], [("n1", 0)])
-        tt(T.gm[:, 0:C], T.n1[:, 2:576:3], T.dm[:, 0:C], ALU.mult, [("n1", 0), "dm"], ["gm"])
-        scan(T.sc[:, 0:C], T.rp[:, 0:C], T.gm[:, 0:C], ["rp", "gm"], ["sc"])
+        scan(T.sc[:, 0:C], T.rp[:, 0:C], T.n1m[:, 2:576:3], ["rp", "n1m"], ["sc"], ALU.max)
         ts(T.off0[:, 0:12], T.sc[:, 15:C:16], 3.0, 2.0, ALU.mult, ALU.add, ["sc"], [("off0", 0)])
         ts(B("loff")[:], T.sc[:, 15:C:16], -1.0, float(C - 1), ALU.add, ALU.min, ["sc"], [K("loff")])
-        send(helper, B("ll")[:], B("loff")[:], K("al"), [K("loff")])
+        send([helper], B("ll")[:], B("loff")[:], K("al"), [K("loff")])
+        arrive(K("aq"), 2 * width(guest), [K("gq")])
+        arrive(K("al"), width(guest), [K("ll")])
+        arrive(K("ac"), width(guest), [K("lc")])
         cand = B("cand")
         for l in range(5):
             off, nxt = T["off%d" % l], T["off%d" % (l + 1)]
             on, nn = "off%d" % l, "off%d" % (l + 1)
-            win = T.n1[:] if l == 0 else T.nw[:, 0:RG * (l + 1)]
-            wk = ["n1"] if l == 0 else [("nw", i) for i in range(l + 1)] + [("nw", 10 + i) for i in range(1, l + 1)]
-            act(T.nw[:, RG * (l + 1):RG * (l + 1) + C], win.indirect(off[:, 0:12]), wk + [on], [("nw", l + 1)])
-            tt(T.gm[:], win.indirect(off[:, 0:16]), T.dm[:], ALU.mult, wk + [on, "dm"], ["gm"])
+            win, wk = table(l)
+            act(T.nw[:, RG * (l + 1):RG * (l + 1) + C], win.indirect(off[:, 0:12]), wk + [(on, 0)], [("nw", l + 1)])
+            jump(win, wk, off[:, 0:16], on, 256)
             if t == 0:
                 soon.pop(0)()
-            scan(T.sc[:], T.rp[:], T.gm[:], ["rp", "gm"], ["sc"])
+            if l == 2:
+                for b in range(4):
+                    mm(2 + b, C, col(T.eq, b), col(T.es, b), B("gq")[:], B("gs")[:], [("eq", b), K("gq")])
+            if l >= 2:
+                unpack(2 * l - 4)
+                unpack(2 * l - 3)
+            fold(256)
+            if t == 0:
+                soon.pop(0)()
             base = float(RG * (l + 1))
             if l < 3:
                 ts(nxt[:, 0:12], T.sc[:, 15:C:16], base, None, ALU.add, None, ["sc"], [(nn, 0)])
                 ts(nxt[:, 12:16], T.sc[:, C + 15:256:16], T.pf[:, 2 + l:3 + l], None, ALU.add, None, ["sc", ("pf", l + 1)], [(nn, 1)])
             else:
                 ts(nxt[:, 0:16], T.sc[:, 15:256:16], base, None, ALU.add, None, ["sc"], [(nn, 0)])
-                cp(cand[:, l - 3:16:4], T.sc[:, C + 15:256:16], ["sc"], [(K("cand"), l - 3)])
                 if l == 3:
+                    cp(cand[:, 0:12:3], T.sc[:, C + 15:256:16], ["sc"], [(K("cand"), 0)])
                     ts(T.off5[:, 16:20], T.sc[:, C + 15:256:16], float(RG * 5), None, ALU.add, None, ["sc"], [("off5", 1)])
-        win = T.nw[:, 0:RG * 6]
-        wk = [("nw", i) for i in range(6)] + [("nw", 10 + i) for i in range(1, 6)]
+        win, wk = table(5)
         act(T.nw[:, RG * 6:RG * 6 + C], win.indirect(T.off5[:, 0:12]), wk + [("off5", 0)], [("nw", 6)])
-        ex = B("ex")
+        unpack(6)
+        unpack(7)
+        if t == 0:
+            act(T.hw[:], T.d3[:, 0:256], ["d3"], ["hw"], 0.0)
+        ex, eu = B("ex"), B("eu")
         if rank < N - 1:
             cp(T.x0[:], win.indirect(T.off5[:, 0:1]), wk + [("off5", 0)], ["x0"])
-        tt(T.gm[:, 0:128], win.indirect(T.off5[:, 12:20]), T.dm[:, 0:128], ALU.mult, wk + ["off5", "dm"], ["gm"])
+        cp(cand[:, 1:12:3], T.sc[:, C + 15:256:16], ["sc"], [(K("cand"), 1)])
+        jump(win, wk, T.off5[:, 12:20], "off5", 128)
         if rank == 0:
             cp(T.x1[:, 0:16], n64.indirect(T.x0[:, 0:1]), N64 + ["x0"], ["x1"])
+            fold(128)
+            ts(eu[:], n64.indirect(T.x1[:, 0:1]), -float(C), None, ALU.add, None, N64 + ["x1"], [K("eu")])
         elif rank < N - 1:
             cp(T.x1[:, 1:65], n64.indirect(T.x0[:, 0:4]), N64 + ["x0"], ["x1"])
-        scan(T.sc[:, 0:128], T.rp[:, 0:128], T.gm[:, 0:128], ["rp", "gm"], ["sc"])
-        if rank == 0:
-            ts(ex[:], n64.indirect(T.x1[:, 0:1]), -float(C), None, ALU.add, None, N64 + ["x1"], [K("ex")])
-        elif rank < N - 1:
+            fold(128)
             for h in range(2):
                 ts(T.msg[:, 32 * h:32 * h + 32], n64.indirect(T.x1[:, 16 + 32 * h:18 + 32 * h]), -float(C), None,
                    ALU.add, None, N64 + ["x1"], [("msg", h)])
-        cp(cand[:, 2:16:4], T.sc[:, 79:128:16], ["sc"], [(K("cand"), 2)])
+        else:
+            fold(128)
+        cp(cand[:, 2:12:3], T.sc[:, 79:128:16], ["sc"], [(K("cand"), 2)])
         if 0 < rank < N - 1:
-            cp(ex[:, 0:4], T.msg[:, 0:64:16], ["msg"], [K("ex")])
-        cp(cand[:, 3:16:4], T.sc[:, 15:64:16], ["sc"], [(K("cand"), 3)])
+            cp(ex[:], T.msg[:, 0:64:16], ["msg"], [K("ex")])
         if rank < N - 1:
-            wd = 2 if rank == 0 else 4
-            to = [T.cores[r] for r in range(N) if r != rank and max(r, (r - HOP[t]) % N) > rank]
-            sent[0] += len(topo.engines(core, to[0]))
-            tr = RemoteDMATransfer(dst_ids=[DstId(rid=topo.addr(c)[0], pnc=topo.addr(c)[1]) for c in to],
-                                   dma_engine_mask=topo.mask(core, to[0]), remote_sem=sem[K("am%d_" % rank)],
-                                   srcs=[ex[:, 0:wd]], dsts=[B("lm%d_" % rank)[:, 0:wd] for c in to])
-            op("g", lambda tr=tr: g.remote_dma_fused([tr], local_sem=sem.sent), [K("ex")], (), "remote")
-        wd = 4 if rank == 0 else 16
-        send(helper, B("lc")[:, 0:wd], cand[:, 0:wd], K("ac"), [K("cand")])
-        arrive(K("aq"), 2 * width(guest), [K("gq")])
-        arrive(K("al"), width(guest), [K("ll")])
-        arrive(K("ac"), width(guest), [K("lc")])
-        for b in range(4):
-            mm(2 + b, C, col(T.eq, b), col(T.es, b), B("gq")[:], B("gs")[:], [("eq", b), K("gq")])
-        for b in range(4):
-            act(T.vh[:, C * b:C * b + C], ps(2 + b, 0, C), (), [("ps", 2 + b), ("vh", b)], 0.5)
-            act(T.vh2[:, C * b:C * b + C], ps(2 + b, 0, C), (), [("ps", 2 + b), ("vh2", b)], 0.5)
-        while shade:
-            shade.pop(0)()
+            src, sk = (eu[:, 0:2], K("eu")) if rank == 0 else (ex[:], K("ex"))
+            first = [r for r in range(N) if r != rank and (r - HOP[t]) % N > rank]
+            first.sort(key=lambda r: -((r - HOP[t]) % N))
+            send(first + [r for r in range(rank + 1, N) if r not in first], B("lm%d_" % rank)[:], src, K("am%d_" % rank), [sk])
+        wd = 4 if rank == 0 else 12
+        send([helper], B("lc")[:, 0:wd], cand[:, 0:wd], K("ac"), [(K("cand"), c) for c in range(3)])
+        cp(cand[:, 12:16], T.sc[:, 15:64:16], ["sc"], [(K("cand"), 3)])
         for b in range(4):
             tt(T.fa[:, C * b:C * b + C], T.vh[:, C * b:C * b + C].indirect(B("ll")[:]), T.vh2[:, C * b:C * b + C], ALU.add,
                [("vh", b), ("vh2", b), K("ll")], [("fa", b)])
+        if t == 0:
+            pad(0)
         for r in range(max(rank, guest)):
             if r != rank:
                 arrive(K("am%d_" % r), width(r), [K("lm%d_" % r)])
-        have = [0]
+        have = []
 
         def exits(r):
+            n0 = "eu" if rank == 0 else "lm0_"
+            if r == 0:
+                return B(n0)[:, 0:2], [K(n0)], 2
             name = "ex" if r == rank else "lm%d_" % r
-            if r == 0:
-                return B(name)[:, 0:2], [K(name)], 2
-            return B(name)[:, 0:4].indirect(T["ch%d" % r][:, 0:1]), [K(name), "ch%d" % r], 16
+            if r == 1:
+                return B(name)[:].indirect(B(n0)[:, 0:1]), [K(name), K(n0)], 16
+            if not have:
+                src, rk, n = exits(1)
+                cp(T.ch2[:], src, rk, ["ch2"])
+                have.append(1)
+            return B(name)[:].indirect(T.ch2[:, 0:1]), [K(name), "ch2"], 16
 
-        def pick(r, lists, ln, sel, out):
-            if r == 0:
-                cp(T[out][:, 0:4], lists[:, 0:4], [ln], [out])
-                return
-            while have[0] < r - 1:
-                src, rk, n = exits(have[0])
-                have[0] += 1
-                cp(T["ch%d" % have[0]][:, 0:n], src, rk, ["ch%d" % have[0]])
-            src, rk, n = exits(r - 1)
-            ts(T[sel][:, 0:n], src, 4.0, T.pf[:, 5:6], ALU.mult, ALU.add, rk + [("pf", 4)], [sel])
-            cp(T[out][:], lists[:].indirect(T[sel][:, 0:1]), [ln, sel], [out])
+        def pick(r, lists, ln, a, b, sel, out):
+            if r == 0 and out == "goff":
+                cp(T.goff[:, 0:4], lists[:, 0:4], [ln], [out])
+            elif r == 0:
+                cp(T.soff[:, 0:3], lists[:, 0:3], [ln], [(out, 0)])
+                cp(T.soff[:, 3:4], lists[:, 12:13], [ln], [(out, 1)])
+            else:
+                src, rk, n = exits(r - 1)
+                ts(T[sel][:, 0:n], src, a, b, ALU.mult, ALU.add, rk + ["pf"], [sel])
+                cp(T[out][:], lists[:].indirect(T[sel][:, 0:1]), [ln, sel], [out])
 
-        pick(guest, B("lc"), K("lc"), "gsel", "goff")
+        def own():
+            pick(rank, cand, K("cand"), T.pf[:, 7:8], T.pf[:, 8:9], "osel", "soff")
+
+        if rank == 0:
+            own()
+        pick(guest, B("lc"), K("lc"), 3.0, T.pf[:, 5:6], "gsel", "goff")
         for b in range(4):
             src = T.fa[:, C * b:C * b + C].indirect(T.goff[:, 0:3])
             (cp if b % 2 == 0 else act)(T.ft[:, b:4 * A:4], src, [("fa", b), "goff"], [("ft", b)])
         quant(T.fq[:], T.fs[:], T.ft[:], ["ft"], ["fq"])
         for b in range(4):
             mm(2 + b, 128, col(T.wq, b), col(T.wsc, b), T.fq[:], T.fs[:], ["wq", "wsc", "fq"])
-        pick(rank, cand, K("cand"), "osel", "soff")
+        if rank > 0:
+            own()
         for b in range(4):
-            if b % 2 == 0:
-                ts(T.ht[:, b:4 * A:4], ps(2 + b, 0, A), 0.03125, None, ALU.mult, None, (), [("ps", 2 + b), ("ht", b)])
-            else:
-                act(T.ht[:, b:4 * A:4], ps(2 + b, 0, A), (), [("ps", 2 + b), ("ht", b)], 0.03125)
+            ts(T.ht[:, b:4 * A:4], ps(2 + b, 0, A), 0.03125, None, ALU.mult, None, (), [("ps", 2 + b), ("ht", b)])
         quant(B("hq")[:], B("hs")[:], T.ht[:], ["ht"], [K("hq")])
-        send(guest, u8(B("lq")[:, 0:A]), u8(B("hq")[:, 0:A]), K("ah"), [K("hq")])
-        send(guest, B("ls")[:, 0:A], B("hs")[:, 0:A], K("ah"), [K("hq")])
+        send([guest], u8(B("lq")[:, 0:A]), u8(B("hq")[:, 0:A]), K("ah"), [K("hq")])
+        send([guest], B("ls")[:, 0:A], B("hs")[:, 0:A], K("ah"), [K("hq")])
         act(T.sb[:, 0:64], T.nw[:, 0:RG].indirect(T.soff[:, 0:4]), [("nw", 0), "soff"], [("sb", 0)])
         act(T.sb[:, 64:128], n64.indirect(T.soff[:, 0:4]), N64 + ["soff"], [("sb", 1)])
-        tt(T.gm[:, 0:64], n64.indirect(T.soff[:, 0:4]), T.dm[:, 0:64], ALU.mult, N64 + ["soff", "dm"], ["gm"])
-        scan(T.sc[:, 0:64], T.rp[:, 0:64], T.gm[:, 0:64], ["rp", "gm"], ["sc"])
+        jump(n64, N64, T.soff[:, 0:4], "soff", 64)
+        ts(T.m0[:], T.jb[:], T.sb[:, A:A + 1], -96.0, ALU.is_gt, ALU.mult, ["jb", ("sb", 0)], ["m0"])
+        fold(64)
+        ts(T.m1[:], T.jb[:], T.sb[:, 2 * A:2 * A + 1], -96.0, ALU.is_gt, ALU.mult, ["jb", ("sb", 1)], ["m1"])
         cp(T.k2[:], T.sc[:, 15:64:16], ["sc"], ["k2"])
+        tt(T.m3[:], T.m0[:], T.cb[:], ALU.add, ["m0", "cb"], ["m3"])
         cp(T.sb[:, 128:192], n64.indirect(T.k2[:]), N64 + ["k2"], [("sb", 2)])
-        while late:
-            late.pop(0)()
-        for c in range(12):
-            lo, hi, at = 4 * c, 16 * c + 16, 6 * c * (c - 1) + 16 * c
+        tt(T.m4[:], T.m1[:], T.m3[:], ALU.add, ["m1", "m3"], ["m4"])
+        ts(T.m2[:], T.jb[:], T.sb[:, 3 * A:3 * A + 1], -96.0, ALU.is_gt, ALU.mult, ["jb", ("sb", 2)], ["m2"])
+
+        def span(c):
+            return 4 * c, 16 * c + 16, 6 * c * (c - 1) + 16 * c
+
+        for c in range(SPLIT):
+            lo, hi, at = span(c)
             op("s", lambda c=c, lo=lo, hi=hi, at=at: S.activation(
                 T.junk[:, at:at + hi - lo], T.sb[:, lo:hi], ACT.Sign, bias=T.jb[:, c:c + 1], scale=-1.0,
                 accum_out=T.acc[:, c:c + 1]), [("sb", i) for i in range((hi + 63) // 64)] + ["jb"], [("acc", c), ("junk", c)])
-        tt(T.kk[:], T.acc[:], T.cb[:], ALU.add, ["acc", "cb"], ["kk"])
-        ts(T.kq[:], T.kk[:], -49.0, 1.0 / 96.0, ALU.add, ALU.mult, ["kk"], ["kq"])
-        ts(T.kr[:], T.kq[:], 0.0, -96.0, ALU.max, ALU.mult, ["kq"], ["kr"])
-        tt(T.ks[:], T.kk[:], T.kr[:], ALU.add, ["kk", "kr"], ["ks"])
+        for c in range(SPLIT, 12):
+            lo, hi, at = span(c)
+            ts(T.junk[:, at:at + hi - lo], T.sb[:, lo:hi], T.jb[:, c:c + 1], 2.0, ALU.is_lt, ALU.mult, ["sb", "jb"], [("junk", c)])
+        tt(T.m5[:], T.m2[:], T.m4[:], ALU.add, ["m2", "m4"], ["m5"])
+        for c in range(SPLIT, 12):
+            lo, hi, at = span(c)
+            op("v", lambda c=c, lo=lo, hi=hi, at=at: V.tensor_reduce(
+                T.acc[:, c:c + 1], T.junk[:, at:at + hi - lo], AxisListType.X, ALU.add), [("junk", c)], [("acc", c)])
+        tt(T.ks[:], T.acc[:], T.m5[:], ALU.add, ["acc", "m5"], ["ks"])
         ts(T.koff[:], T.ks[:], 0.5, None, ALU.mult, None, ["ks"], ["koff"])
         if t == R - 1:
             dma("y", T.ol[:], T.sb[0:128:16, 0:A], [("sb", 0)], ())

@@ -17,7 +17,8 @@ for _n, _w, _d in [
         ("eall", 516, BF), ("eq", 512, X4), ("es", 512, U8), ("zt", 512, BF), ("ft", 512, BF), ("ht", 512, BF),
         ("jm", 256, BF), ("pi", 8, "int32"), ("pf", 10, F32), ("dm", 256, BF), ("rp", 256, BF),
         ("d3", 576, BF), ("d3m", 576, BF), ("z3", 576, BF), ("n1", 592, BF), ("n1m", 576, BF), ("nw", 7 * RG, BF),
-        ("gm", 256, BF), ("sc", 256, BF), ("uoff", 16, U16), ("x0", 16, U16), ("x1", 66, U16), ("msg", 64, BF),
+        ("gm", C, BF), ("sc", C, BF), ("gl", 64, BF), ("sl", 64, BF),
+        ("uoff", 16, U16), ("x0", 16, U16), ("x1", 66, U16), ("msg", 64, BF),
         ("ch2", 16, U16), ("osel", 16, U16), ("gsel", 16, U16), ("soff", 16, U16), ("goff", 16, U16),
         ("k2", 4, U16), ("koff", 12, U16),
         ("sb", 192, F32), ("junk", 1024, BF), ("jb", 12, F32), ("cb", 12, F32), ("acc", 12, F32), ("kr", 12, F32),
@@ -53,6 +54,10 @@ def keys(xs):
 def emit(g, T, ops, sent):
     queues = {"v": g.vector, "s": g.scalar, "t": g.tensor, "g": g, "y": g.sync}
     known = {q: set() for q in queues}
+    groups = {}
+    for n, o in enumerate(ops):
+        if o.get("grp"):
+            groups.setdefault(o["grp"], []).append(n)
     for n, o in enumerate(ops):
         if o["q"] is None:
             o["known"] = set()
@@ -66,6 +71,10 @@ def emit(g, T, ops, sent):
                     or any(clash(a, b) for a in o["w"] for b in p["r"])):
                 deps.add(m)
         deps = {m for m in deps if not any(m in ops[k]["known"] for k in deps)}
+        for m in list(deps):
+            if ops[m].get("grp"):
+                assert groups[ops[m]["grp"]][-1] < n
+                deps |= set(groups[ops[m]["grp"]])
         o["waits"] = sorted(deps)
         for m in deps:
             ops[m]["need"] = True
@@ -79,8 +88,11 @@ def emit(g, T, ops, sent):
                 tail.append(o["sig"])
             continue
         q = queues[o["q"]]
+        done = []
         for m in o["waits"]:
-            q.wait_ge(T.sem[ops[m]["sig"][0]], ops[m]["sig"][1])
+            if ops[m]["sig"] not in done:
+                done.append(ops[m]["sig"])
+                q.wait_ge(T.sem[ops[m]["sig"][0]], ops[m]["sig"][1])
         ins = o["fn"]()
         if o["kind"] == "remote":
             continue
@@ -92,10 +104,14 @@ def emit(g, T, ops, sent):
             if not o.get("need"):
                 tail.append(o["sig"])
         elif o.get("need"):
-            name = [s for s in POOL[o["q"]] if s not in last or last[s] in o["known"]][0]
-            o["sig"] = (name, ops[last[name]]["sig"][1] + 1 if name in last else 1)
-            last[name] = n
-            ins.then_inc(T.sem[name], 1)
+            if "sig" not in o:
+                mates = groups[o["grp"]] if o.get("grp") else [n]
+                name = [s for s in POOL[o["q"]] if s not in last or last[s] in o["known"]][0]
+                sig = (name, (ops[last[name]]["sig"][1] if name in last else 0) + len(mates))
+                last[name] = mates[-1]
+                for m in mates:
+                    ops[m]["sig"] = sig
+            ins.then_inc(T.sem[o["sig"][0]], 1)
     tail.insert(0, ("sent", sent[0]))
     for name, val in tail:
         g.wait_ge(T.sem[name], val)
@@ -112,6 +128,9 @@ def rank_program(g, core, T, topo):
 
     def op(q, fn, r=(), w=(), kind="compute"):
         ops.append({"q": q, "fn": fn, "r": keys(r), "w": keys(w), "kind": kind})
+
+    def together(name):
+        ops[-1]["grp"] = name
 
     def arrive(name, val, w):
         ops.append({"q": None, "r": [], "w": keys(w), "kind": "arrive", "sig": (name, val)})
@@ -182,17 +201,14 @@ def rank_program(g, core, T, topo):
             return T.n1[:], ["n1"]
         return T.nw[:, 0:RG * (l + 1)], [("nw", i) for i in range(l + 1)] + [("nw", 10 + i) for i in range(1, l + 1)]
 
-    def jump(win, wk, offs, on, n):
-        tt(T.gm[:, 0:n], win.indirect(offs), T.dm[:, 0:n], ALU.mult, wk + [on, "dm"], ["gm"])
+    def jump(tab, offs, on):
+        tt(T.gl[:], tab[0].indirect(offs), T.dm[:, 0:64], ALU.mult, tab[1] + [on, "dm"], ["gl"])
 
-    def fold(n):
-        scan(T.sc[:, 0:n], T.rp[:, 0:n], T.gm[:, 0:n], ["rp", "gm"], ["sc"])
+    def fold():
+        scan(T.sl[:], T.rp[:, 0:64], T.gl[:], ["rp", "gl"], ["sl"])
 
     dma("y", T.t0[:], T.x[:], (), ["t0"])
     dma("s", T.ut[:], T.u[:], (), ["ut"])
-    dma("y", u8(T.wq[:]), T.wc[:], (), ["wq"])
-    dma("s", T.wsc[:], T.ws[:], (), ["wsc"])
-    dma("y", T.vt[:], T.v[:], (), ["vt"])
 
     op("g", lambda: g.iota(T.pi[:, 0:1], [[0, 1]], 0, 1), (), [("pi", 0)])
     iota(T.jm[:], [[0, 16], [1, 16]], 0, ["jm"])
@@ -206,24 +222,30 @@ def rank_program(g, core, T, topo):
     ts(T.pi[:, 1:2], T.pi[:, 0:1], 15, None, ALU.bitwise_and, None, [("pi", 0)], [("pi", 1)])
     ms(T.d3[:, 0:576:3], 0.0, ["d3"])
     ms(T.rp[:, 0:256:16], 0.0, ["rp"])
+    act(T.eall[:], T.d3[:, 0:516], ["d3"], ["eall"], 0.0)
     cp(T.pf[:, 0:2], T.pi[:, 0:2], [("pi", 0), ("pi", 1)], [("pf", 0)])
     for l in range(4):
         ts(T.pi[:, 2 + l:3 + l], T.pi[:, 1:2], l, 1, ALU.logical_shift_right, ALU.bitwise_and, [("pi", 1)], [("pi", 2 + l)])
+        together("bits")
     ts(T.uoff[:, 0:8], T.jm[:, 0:8], 16.0, None, ALU.mult, None, ["jm"], [("uoff", 0)])
+    together("uoff")
     ts(T.uoff[:, 8:16], T.jm[:, 0:8], 16.0, 1.0, ALU.mult, ALU.add, ["jm"], [("uoff", 1)])
+    together("uoff")
     ts(T.dm[:], T.jm[:], T.pf[:, 1:2], None, ALU.is_equal, None, ["jm", ("pf", 0)], ["dm"])
     for e in range(4):
         ts(T.off0[:, 12 + e:13 + e], T.pi[:, 2:3], float(2 * e - 586), float(588 + e), ALU.mult, ALU.add,
            [("pi", 2)], [("off0", 1 + e)])
+        together("off0")
     for l in range(1, 4):
         ts(T.pf[:, 1 + l:2 + l], T.pi[:, 2 + l:3 + l], float(RG * l), None, ALU.mult, None, [("pi", 2 + l)], [("pf", l)])
-    ms(T.eall[:], 0.0, ["eall"])
+        together("base")
     ts(T.d3m[:, 2:576:3], T.dm[:, 0:C], 1001.0, -1000.0, ALU.mult, ALU.add, ["dm"], [("d3m", 2)])
     cp(T.n1[:, 578:590:3], T.nw[:, C:C + 4], [("nw", 0)], [("n1", 1)])
-    cp(T.n1[:, 588:592], T.jm[:, 0:4], ["jm"], [("n1", 1)])
     ts(T.eall[:, 3:515:4], T.nw[:, 0:128], T.pf[:, 0:1], None, ALU.is_equal, None, [("nw", 0), ("pf", 0)], ["eall"])
+    cp(T.n1[:, 588:592], T.jm[:, 0:4], ["jm"], [("n1", 1)])
     for l in range(1, 7):
         act(T.nw[:, RG * l + C:RG * l + RG], T.nw[:, C:RG], [("nw", 0)], [("nw", 10 + l)])
+        together("stay")
 
     def e_tile(b):
         quant(col(T.eq, b), col(T.es, b), T.eall[:, 3 - b:515 - b], ["eall"], [("eq", b)])
@@ -231,21 +253,18 @@ def rank_program(g, core, T, topo):
     def pad(t):
         quant(T["lq%d" % t][:, A:176], T["ls%d" % t][:, A:176], T.zt[:], ["zt"], [("l%d" % t, "pad")])
 
-    soon = [
-        lambda: e_tile(2),
-        lambda: ts(T.pf[:, 5:6], T.pf[:, 1:2], 2.0, None, ALU.min, None, [("pf", 0)], [("pf", 4)]),
-        lambda: e_tile(3),
-        lambda: ts(T.pf[:, 6:7], T.pf[:, 1:2], 3.0, None, ALU.is_ge, None, [("pf", 0)], [("pf", 5)]),
-        lambda: ts(T.pf[:, 7:8], T.pf[:, 6:7], -2.0, 3.0, ALU.mult, ALU.add, [("pf", 5)], [("pf", 6)]),
-        lambda: ts(T.pf[:, 8:9], T.pf[:, 6:7], 10.0, T.pf[:, 5:6], ALU.mult, ALU.add, [("pf", 5), ("pf", 4)], [("pf", 7)]),
-        lambda: ts(T.kr[:], T.jm[:, 0:12], 16.0, 0.5, ALU.mult, ALU.add, ["jm"], ["kr"]),
-        lambda: ts(T.cb[:, 0:SPLIT], T.jm[:, 0:SPLIT], 20.0, 16.0, ALU.mult, ALU.add, ["jm"], [("cb", 0)]),
-        lambda: ts(T.jb[:], T.kr[:], T.pf[:, 1:2], None, ALU.add, None, ["kr", ("pf", 0)], ["jb"]),
-        lambda: ts(T.cb[:, SPLIT:12], T.jm[:, SPLIT:12], 8.0, None, ALU.mult, None, ["jm"], [("cb", 1)])]
+    def pick_constants():
+        ts(T.pf[:, 6:7], T.pf[:, 1:2], 3.0, None, ALU.is_ge, None, [("pf", 0)], [("pf", 5)])
+        ts(T.pf[:, 5:6], T.pf[:, 1:2], 2.0, None, ALU.min, None, [("pf", 0)], [("pf", 4)])
+        ts(T.kr[:], T.jm[:, 0:12], 16.0, 0.5, ALU.mult, ALU.add, ["jm"], ["kr"])
+        ts(T.pf[:, 7:8], T.pf[:, 6:7], -2.0, 3.0, ALU.mult, ALU.add, [("pf", 5)], [("pf", 6)])
+        ts(T.pf[:, 8:9], T.pf[:, 6:7], 10.0, T.pf[:, 5:6], ALU.mult, ALU.add, [("pf", 5), ("pf", 4)], [("pf", 7)])
+        ts(T.jb[:], T.kr[:], T.pf[:, 1:2], None, ALU.add, None, ["kr", ("pf", 0)], ["jb"])
 
     quant(T.uq[:], T.us[:], T.ut[:], ["ut"], ["uq"])
     n64 = T.nw[:, 6 * RG:7 * RG]
     N64 = [("nw", 6), ("nw", 16)]
+    ends = T.sl[:, 15:64:16]
 
     for t in range(R):
         def B(name):
@@ -260,12 +279,13 @@ def rank_program(g, core, T, topo):
 
         helper, guest = (rank + HOP[t]) % N, (rank - HOP[t]) % N
         tq, tsc = B("tq"), B("ts")
+        if t == 0:
+            cp(T.upq[:].bitcast(dt.uint32), T.uq[:].bitcast(dt.uint32).indirect(T.uoff[:]), ["uq", "uoff"], ["upq"])
+            act(T.ups[:], T.us[:].indirect(T.uoff[:]), ["uq", "uoff"], ["ups"])
         quant(tq[:], tsc[:], B("t")[:], [K("t")], [K("tq")])
         send([helper], u8(B("gq")[:]), u8(tq[:]), K("aq"), [K("tq")])
         send([helper], B("gs")[:], tsc[:], K("aq"), [K("tq")])
         if t == 0:
-            cp(T.upq[:].bitcast(dt.uint32), T.uq[:].bitcast(dt.uint32).indirect(T.uoff[:]), ["uq", "uoff"], ["upq"])
-            act(T.ups[:], T.us[:].indirect(T.uoff[:]), ["uq", "uoff"], ["ups"])
             act(T.zt[:], T.d3[:, 0:512], ["d3"], ["zt"], 0.0)
             act(T.ft[:, 4 * A:], T.d3[:, 4 * A:512], ["d3"], [("ft", 9)], 0.0)
             act(T.ht[:, 4 * A:], T.d3[:, 4 * A:512], ["d3"], [("ht", 9)], 0.0)
@@ -278,13 +298,21 @@ def rank_program(g, core, T, topo):
         for k in range(2):
             mm(k, C, col(T.upq, k), col(T.ups, k), tq[:], tsc[:], ["upq", "ups", K("tq")])
         ts(T.z3[:, 1:576:3], ps(0, 0, C), 0.0, None, ALU.is_gt, None, (), [("ps", 0), ("z3", 1)])
+        together(K("signs"))
         ts(T.z3[:, 2:576:3], ps(1, 0, C), 0.0, 2.0, ALU.is_gt, ALU.mult, (), [("ps", 1), ("z3", 2)])
+        together(K("signs"))
         scan(T.n1m[:], T.d3m[:], T.z3[:], ["d3m", "z3"], ["n1m"])
         scan(T.n1[:, 0:576], T.d3[:], T.z3[:], ["d3", "z3"], [("n1", 0)])
-        scan(T.sc[:, 0:C], T.rp[:, 0:C], T.n1m[:, 2:576:3], ["rp", "n1m"], ["sc"], ALU.max)
+        scan(T.sc[:], T.rp[:, 0:C], T.n1m[:, 2:576:3], ["rp", "n1m"], ["sc"], ALU.max)
+        jump(table(0), T.off0[:, 12:16], ("off0", 1))
         ts(T.off0[:, 0:12], T.sc[:, 15:C:16], 3.0, 2.0, ALU.mult, ALU.add, ["sc"], [("off0", 0)])
         ts(B("loff")[:], T.sc[:, 15:C:16], -1.0, float(C - 1), ALU.add, ALU.min, ["sc"], [K("loff")])
+        fold()
         send([helper], B("ll")[:], B("loff")[:], K("al"), [K("loff")])
+        if t == 0:
+            dma("y", u8(T.wq[:]), T.wc[:], [K("loff")], ["wq"])
+            dma("y", T.wsc[:], T.ws[:], (), ["wsc"])
+            dma("y", T.vt[:], T.v[:], (), ["vt"])
         arrive(K("aq"), 2 * width(guest), [K("gq")])
         arrive(K("al"), width(guest), [K("ll")])
         arrive(K("ac"), width(guest), [K("lc")])
@@ -294,51 +322,55 @@ def rank_program(g, core, T, topo):
             on, nn = "off%d" % l, "off%d" % (l + 1)
             win, wk = table(l)
             act(T.nw[:, RG * (l + 1):RG * (l + 1) + C], win.indirect(off[:, 0:12]), wk + [(on, 0)], [("nw", l + 1)])
-            jump(win, wk, off[:, 0:16], on, 256)
-            if t == 0:
-                soon.pop(0)()
-            if l == 2:
+            tt(T.gm[:], win.indirect(off[:, 0:12]), T.dm[:, 0:C], ALU.mult, wk + [(on, 0), "dm"], ["gm"])
+            if l < 3:
+                ts(nxt[:, 12:16], ends, T.pf[:, 2 + l:3 + l], None, ALU.add, None, ["sl", ("pf", l + 1)], [(nn, 1)])
+            elif l == 3:
+                ts(nxt[:, 12:16], ends, float(RG * 4), None, ALU.add, None, ["sl"], [(nn, 1)])
+                ts(T.off5[:, 12:16], ends, float(RG * 5), None, ALU.add, None, ["sl"], [("off5", 1)])
+            else:
+                cp(cand[:, 1:12:3], ends, ["sl"], [(K("cand"), 1)])
+                ts(T.off5[:, 16:20], ends, float(RG * 5), None, ALU.add, None, ["sl"], [("off5", 2)])
+            if l == 3:
                 for b in range(4):
                     mm(2 + b, C, col(T.eq, b), col(T.es, b), B("gq")[:], B("gs")[:], [("eq", b), K("gq")])
-            if l >= 2:
-                unpack(2 * l - 4)
-                unpack(2 * l - 3)
-            fold(256)
-            if t == 0:
-                soon.pop(0)()
-            base = float(RG * (l + 1))
-            if l < 3:
-                ts(nxt[:, 0:12], T.sc[:, 15:C:16], base, None, ALU.add, None, ["sc"], [(nn, 0)])
-                ts(nxt[:, 12:16], T.sc[:, C + 15:256:16], T.pf[:, 2 + l:3 + l], None, ALU.add, None, ["sc", ("pf", l + 1)], [(nn, 1)])
-            else:
-                ts(nxt[:, 0:16], T.sc[:, 15:256:16], base, None, ALU.add, None, ["sc"], [(nn, 0)])
-                if l == 3:
-                    cp(cand[:, 0:12:3], T.sc[:, C + 15:256:16], ["sc"], [(K("cand"), 0)])
-                    ts(T.off5[:, 16:20], T.sc[:, C + 15:256:16], float(RG * 5), None, ALU.add, None, ["sc"], [("off5", 1)])
+            if l >= 3:
+                unpack(l - 3)
+            scan(T.sc[:], T.rp[:, 0:C], T.gm[:], ["rp", "gm"], ["sc"])
+            if l == 3:
+                cp(cand[:, 0:12:3], ends, ["sl"], [(K("cand"), 0)])
+            jump(table(l + 1), nxt[:, 12:16], (nn, 1))
+            ts(nxt[:, 0:12], T.sc[:, 15:C:16], float(RG * (l + 1)), None, ALU.add, None, ["sc"], [(nn, 0)])
+            fold()
+            if t == 0 and l < 2:
+                e_tile(2 + l)
         win, wk = table(5)
         act(T.nw[:, RG * 6:RG * 6 + C], win.indirect(T.off5[:, 0:12]), wk + [("off5", 0)], [("nw", 6)])
-        unpack(6)
-        unpack(7)
+        for n in range(2, 8):
+            unpack(n)
         if t == 0:
             act(T.hw[:], T.d3[:, 0:256], ["d3"], ["hw"], 0.0)
         ex, eu = B("ex"), B("eu")
         if rank < N - 1:
             cp(T.x0[:], win.indirect(T.off5[:, 0:1]), wk + [("off5", 0)], ["x0"])
-        cp(cand[:, 1:12:3], T.sc[:, C + 15:256:16], ["sc"], [(K("cand"), 1)])
-        jump(win, wk, T.off5[:, 12:20], "off5", 128)
+        cp(cand[:, 2:12:3], ends, ["sl"], [(K("cand"), 2)])
+        wd = 4 if rank == 0 else 12
+        send([helper], B("lc")[:, 0:wd], cand[:, 0:wd], K("ac"), [(K("cand"), c) for c in range(3)])
+        jump(table(5), T.off5[:, 16:20], ("off5", 2))
         if rank == 0:
             cp(T.x1[:, 0:16], n64.indirect(T.x0[:, 0:1]), N64 + ["x0"], ["x1"])
-            fold(128)
+            fold()
             ts(eu[:], n64.indirect(T.x1[:, 0:1]), -float(C), None, ALU.add, None, N64 + ["x1"], [K("eu")])
         elif rank < N - 1:
             cp(T.x1[:, 1:65], n64.indirect(T.x0[:, 0:4]), N64 + ["x0"], ["x1"])
-            fold(128)
+            fold()
             for h in range(2):
                 ts(T.msg[:, 32 * h:32 * h + 32], n64.indirect(T.x1[:, 16 + 32 * h:18 + 32 * h]), -float(C), None,
                    ALU.add, None, N64 + ["x1"], [("msg", h)])
+                together(K("msg"))
         else:
-            fold(128)
-        cp(cand[:, 2:12:3], T.sc[:, 79:128:16], ["sc"], [(K("cand"), 2)])
+            fold()
+        cp(cand[:, 12:16], ends, ["sl"], [(K("cand"), 3)])
         if 0 < rank < N - 1:
             cp(ex[:], T.msg[:, 0:64:16], ["msg"], [K("ex")])
         if rank < N - 1:
@@ -346,14 +378,12 @@ def rank_program(g, core, T, topo):
             first = [r for r in range(N) if r != rank and (r - HOP[t]) % N > rank]
             first.sort(key=lambda r: -((r - HOP[t]) % N))
             send(first + [r for r in range(rank + 1, N) if r not in first], B("lm%d_" % rank)[:], src, K("am%d_" % rank), [sk])
-        wd = 4 if rank == 0 else 12
-        send([helper], B("lc")[:, 0:wd], cand[:, 0:wd], K("ac"), [(K("cand"), c) for c in range(3)])
-        cp(cand[:, 12:16], T.sc[:, 15:64:16], ["sc"], [(K("cand"), 3)])
+        if t == 0:
+            pick_constants()
         for b in range(4):
             tt(T.fa[:, C * b:C * b + C], T.vh[:, C * b:C * b + C].indirect(B("ll")[:]), T.vh2[:, C * b:C * b + C], ALU.add,
                [("vh", b), ("vh2", b), K("ll")], [("fa", b)])
-        if t == 0:
-            pad(0)
+            together(K("fa"))
         for r in range(max(rank, guest)):
             if r != rank:
                 arrive(K("am%d_" % r), width(r), [K("lm%d_" % r)])
@@ -372,43 +402,59 @@ def rank_program(g, core, T, topo):
                 have.append(1)
             return B(name)[:].indirect(T.ch2[:, 0:1]), [K(name), "ch2"], 16
 
-        def pick(r, lists, ln, a, b, sel, out):
+        def choose(r, a, b, sel):
+            if r > 0:
+                src, rk, n = exits(r - 1)
+                ts(T[sel][:, 0:n], src, a, b, ALU.mult, ALU.add, rk + ["pf"], [sel])
+
+        def pick(r, lists, ln, sel, out):
             if r == 0 and out == "goff":
                 cp(T.goff[:, 0:4], lists[:, 0:4], [ln], [out])
             elif r == 0:
                 cp(T.soff[:, 0:3], lists[:, 0:3], [ln], [(out, 0)])
                 cp(T.soff[:, 3:4], lists[:, 12:13], [ln], [(out, 1)])
             else:
-                src, rk, n = exits(r - 1)
-                ts(T[sel][:, 0:n], src, a, b, ALU.mult, ALU.add, rk + ["pf"], [sel])
                 cp(T[out][:], lists[:].indirect(T[sel][:, 0:1]), [ln, sel], [out])
 
-        def own():
-            pick(rank, cand, K("cand"), T.pf[:, 7:8], T.pf[:, 8:9], "osel", "soff")
-
         if rank == 0:
-            own()
-        pick(guest, B("lc"), K("lc"), 3.0, T.pf[:, 5:6], "gsel", "goff")
+            pick(rank, cand, K("cand"), "osel", "soff")
+        choose(guest, 3.0, T.pf[:, 5:6], "gsel")
+        if 0 < rank < guest:
+            choose(rank, T.pf[:, 7:8], T.pf[:, 8:9], "osel")
+        pick(guest, B("lc"), K("lc"), "gsel", "goff")
+        if 0 < rank < guest:
+            pick(rank, cand, K("cand"), "osel", "soff")
         for b in range(4):
             src = T.fa[:, C * b:C * b + C].indirect(T.goff[:, 0:3])
             (cp if b % 2 == 0 else act)(T.ft[:, b:4 * A:4], src, [("fa", b), "goff"], [("ft", b)])
+            together(K("ft%d_" % (b % 2)))
         quant(T.fq[:], T.fs[:], T.ft[:], ["ft"], ["fq"])
         for b in range(4):
             mm(2 + b, 128, col(T.wq, b), col(T.wsc, b), T.fq[:], T.fs[:], ["wq", "wsc", "fq"])
-        if rank > 0:
-            own()
+        if t == 0:
+            ts(T.cb[:, 0:SPLIT], T.jm[:, 0:SPLIT], 20.0, 16.0, ALU.mult, ALU.add, ["jm"], [("cb", 0)])
+            ts(T.cb[:, SPLIT:12], T.jm[:, SPLIT:12], 8.0, None, ALU.mult, None, ["jm"], [("cb", 1)])
+        if rank > guest:
+            choose(rank, T.pf[:, 7:8], T.pf[:, 8:9], "osel")
+            pick(rank, cand, K("cand"), "osel", "soff")
+        else:
+            jump((n64, N64), T.soff[:, 0:4], "soff")
+            fold()
         for b in range(4):
             ts(T.ht[:, b:4 * A:4], ps(2 + b, 0, A), 0.03125, None, ALU.mult, None, (), [("ps", 2 + b), ("ht", b)])
+            together(K("ht"))
         quant(B("hq")[:], B("hs")[:], T.ht[:], ["ht"], [K("hq")])
         send([guest], u8(B("lq")[:, 0:A]), u8(B("hq")[:, 0:A]), K("ah"), [K("hq")])
         send([guest], B("ls")[:, 0:A], B("hs")[:, 0:A], K("ah"), [K("hq")])
         act(T.sb[:, 0:64], T.nw[:, 0:RG].indirect(T.soff[:, 0:4]), [("nw", 0), "soff"], [("sb", 0)])
         act(T.sb[:, 64:128], n64.indirect(T.soff[:, 0:4]), N64 + ["soff"], [("sb", 1)])
-        jump(n64, N64, T.soff[:, 0:4], "soff", 64)
+        if rank > guest:
+            jump((n64, N64), T.soff[:, 0:4], "soff")
         ts(T.m0[:], T.jb[:], T.sb[:, A:A + 1], -96.0, ALU.is_gt, ALU.mult, ["jb", ("sb", 0)], ["m0"])
-        fold(64)
+        if rank > guest:
+            fold()
         ts(T.m1[:], T.jb[:], T.sb[:, 2 * A:2 * A + 1], -96.0, ALU.is_gt, ALU.mult, ["jb", ("sb", 1)], ["m1"])
-        cp(T.k2[:], T.sc[:, 15:64:16], ["sc"], ["k2"])
+        cp(T.k2[:], ends, ["sl"], ["k2"])
         tt(T.m3[:], T.m0[:], T.cb[:], ALU.add, ["m0", "cb"], ["m3"])
         cp(T.sb[:, 128:192], n64.indirect(T.k2[:]), N64 + ["k2"], [("sb", 2)])
         tt(T.m4[:], T.m1[:], T.m3[:], ALU.add, ["m1", "m3"], ["m4"])
@@ -422,6 +468,7 @@ def rank_program(g, core, T, topo):
             op("s", lambda c=c, lo=lo, hi=hi, at=at: S.activation(
                 T.junk[:, at:at + hi - lo], T.sb[:, lo:hi], ACT.Sign, bias=T.jb[:, c:c + 1], scale=-1.0,
                 accum_out=T.acc[:, c:c + 1]), [("sb", i) for i in range((hi + 63) // 64)] + ["jb"], [("acc", c), ("junk", c)])
+            together(K("count"))
         for c in range(SPLIT, 12):
             lo, hi, at = span(c)
             ts(T.junk[:, at:at + hi - lo], T.sb[:, lo:hi], T.jb[:, c:c + 1], 2.0, ALU.is_lt, ALU.mult, ["sb", "jb"], [("junk", c)])
@@ -430,6 +477,8 @@ def rank_program(g, core, T, topo):
             lo, hi, at = span(c)
             op("v", lambda c=c, lo=lo, hi=hi, at=at: V.tensor_reduce(
                 T.acc[:, c:c + 1], T.junk[:, at:at + hi - lo], AxisListType.X, ALU.add), [("junk", c)], [("acc", c)])
+        if t == 0:
+            pad(0)
         tt(T.ks[:], T.acc[:], T.m5[:], ALU.add, ["acc", "m5"], ["ks"])
         ts(T.koff[:], T.ks[:], 0.5, None, ALU.mult, None, ["ks"], ["koff"])
         if t == R - 1:
@@ -444,6 +493,7 @@ def rank_program(g, core, T, topo):
         for b in range(4):
             tt(T[new][:, b:4 * C:4], T.hw[:, 64 * b:64 * b + 64].indirect(T.koff[:]), B("t")[:, b:4 * C:4], ALU.add,
                [("hw", b), "koff", K("t")], [(new, b)])
+            together(K("new"))
 
     tq, tsc, qn = T["tq%d" % R], T["ts%d" % R], "tq%d" % R
     quant(tq[:], tsc[:], T["t%d" % R][:], ["t%d" % R], [qn])

@@ -6,7 +6,11 @@ ACT = ActivationFunctionType
 N, C, A, R = 4, 192, 48, 3
 HOP = [1, 2, 3]
 RG = 208
-SPLIT = 11
+NEAR = [0, 2, 3, 5, 7, 12, 17, 29, 41, 53]
+FAR = [82, 123, 164]
+STEP = 41
+SPLIT = 6
+ORDER = 0
 X4, U8 = "float8_e4m3fn_x4", "uint8"
 BF, F32, U16 = "bfloat16", "float32", "uint16"
 
@@ -15,29 +19,31 @@ for _n, _w, _d in [
         ("ut", 512, BF), ("vt", 512, BF), ("uq", 128, X4), ("us", 128, U8), ("upq", 256, X4), ("ups", 256, U8),
         ("vq", 128, X4), ("vs", 128, U8), ("wq", 512, X4), ("wsc", 512, U8), ("fq", 128, X4), ("fs", 128, U8),
         ("eall", 516, BF), ("eq", 512, X4), ("es", 512, U8), ("zt", 512, BF), ("ft", 512, BF), ("ht", 512, BF),
-        ("jm", 256, BF), ("pi", 8, "int32"), ("pf", 10, F32), ("dm", 256, BF), ("rp", 256, BF),
-        ("d3", 576, BF), ("d3m", 576, BF), ("z3", 576, BF), ("n1", 592, BF), ("n1m", 576, BF), ("nw", 7 * RG, BF),
-        ("gm", C, BF), ("sc", C, BF), ("gl", 64, BF), ("sl", 64, BF),
-        ("uoff", 16, U16), ("x0", 16, U16), ("x1", 66, U16), ("msg", 64, BF),
-        ("ch2", 16, U16), ("osel", 16, U16), ("gsel", 16, U16), ("soff", 16, U16), ("goff", 16, U16),
-        ("k2", 4, U16), ("koff", 12, U16),
-        ("sb", 192, F32), ("junk", 1024, BF), ("jb", 12, F32), ("cb", 12, F32), ("acc", 12, F32), ("kr", 12, F32),
-        ("m0", 12, F32), ("m1", 12, F32), ("m2", 12, F32), ("m3", 12, F32), ("m4", 12, F32), ("m5", 12, F32),
-        ("ks", 12, F32), ("vh", 768, BF), ("vh2", 768, BF), ("fa", 768, BF), ("hw", 256, BF), ("yt", 192, F32)]:
+        ("jm", C, BF), ("pi", 2, "int32"), ("pf", 10, F32), ("md", C, BF), ("oh", 32, BF),
+        ("sq", 16, F32), ("zd", 576, BF), ("zc", 576, BF), ("zo", 576, BF), ("so", 576, BF), ("n1", 592, BF),
+        ("nw", RG * len(NEAR), BF), ("nx", RG * len(FAR), BF), ("fl", 224, BF), ("sf", A, BF),
+        ("sc", C, BF), ("ro", C, BF), ("sr", C, BF), ("vh2", 4 * C, BF), ("via", 64, BF),
+        ("uoff", 16, U16), ("off1", 24, U16), ("off2", 12, U16), ("off5", 12, U16), ("off12", 12, U16),
+        ("off41", 8, U16), ("ta", 2, U16), ("tb", 4, U16), ("roff", 4, U16),
+        ("x0", 16, U16), ("x1", 66, U16), ("x2", 66, U16), ("x3", 66, U16),
+        ("osel", 16, U16), ("gsel", 16, U16), ("soff", 16, U16), ("sofb", 4, U16), ("goff", 16, U16),
+        ("koff", 12, U16), ("lq", 272, X4), ("ls", 272, U8),
+        ("sb", 5 * A, BF), ("olf", A, F32), ("junk", 1248, BF), ("jb", 12, F32),
+        ("ca", 60, F32), ("cr", 60, F32), ("cs", 60, F32),
+        ("vh", 4 * RG, BF), ("fa", 4 * RG, BF), ("hw", 256, BF), ("yt", 192, F32)]:
     SCRATCH[_n] = ("sbuf", [128, _w], _d)
-for _l in range(6):
-    SCRATCH["off%d" % _l] = ("sbuf", [128, 20], U16)
 for _t in range(R + 1):
     for _n, _w, _d in [("t", 768, BF), ("tq", C, X4), ("ts", C, U8)]:
         SCRATCH["%s%d" % (_n, _t)] = ("sbuf", [128, _w], _d)
 for _t in range(R):
-    for _n, _w, _d in [("hq", 128, X4), ("hs", 128, U8), ("lq", 176, X4), ("ls", 176, U8), ("gq", C, X4), ("gs", C, U8),
-                       ("ex", 4, BF), ("eu", 16, U16), ("loff", 12, U16), ("ll", 12, U16), ("cand", 16, BF), ("lc", 12, BF),
-                       ("lm0_", 2, U16), ("lm1_", 4, BF), ("lm2_", 4, BF)]:
+    for _n, _w, _d in [("hq", 128, X4), ("hs", 128, U8), ("gq", C, X4), ("gs", C, U8),
+                       ("exb", 68, BF), ("exu", 68, U16), ("loff", 12, U16), ("ll", 12, U16),
+                       ("cand", 12, BF), ("lc", 12, BF), ("cu", 4, U16), ("lu", 4, U16),
+                       ("lm0_", 4, U16), ("lm1_", 4, BF), ("lm2_", 4, U16)]:
         SCRATCH["%s%d" % (_n, _t)] = ("sbuf", [128, _w], _d)
 
-POOL = {"v": ["v%d" % i for i in range(56)], "s": ["s%d" % i for i in range(30)],
-        "t": ["t%d" % i for i in range(18)], "g": ["g%d" % i for i in range(5)],
+POOL = {"v": ["v%d" % i for i in range(60)], "s": ["s%d" % i for i in range(28)],
+        "t": ["t%d" % i for i in range(18)], "g": ["g%d" % i for i in range(4)],
         "d": ["d%d" % i for i in range(14)]}
 SEMAPHORES = ([n for k in "vstgd" for n in POOL[k]] + ["sent"]
               + ["%s%d" % (n, t) for t in range(R) for n in ("aq", "al", "ac", "ah", "am0_", "am1_", "am2_")])
@@ -150,14 +156,11 @@ def rank_program(g, core, T, topo):
     def ms(out, c, w):
         op("v", lambda: V.memset(out, c), (), w)
 
-    def scan(out, d0, d1, r, w, o1=ALU.add):
-        op("v", lambda: V.tensor_tensor_scan(out, d0, d1, 0.0, ALU.mult, o1), r, w)
+    def scan(out, d0, d1, o0, o1, r, w):
+        op("v", lambda: V.tensor_tensor_scan(out, d0, d1, 0.0, o0, o1), r, w)
 
-    def act(out, a, r, w, scale=None):
-        if scale is None:
-            op("s", lambda: S.activation(out, a, ACT.Copy), r, w)
-        else:
-            op("s", lambda: S.activation(out, a, ACT.Copy, scale=scale), r, w)
+    def act(out, a, r, w, func=ACT.Copy, **how):
+        op("s", lambda: S.activation(out, a, func, **how), r, w)
 
     def quant(q, s, a, r, w):
         op("v", lambda: V.quantize_mx(q, s, a), r, w)
@@ -173,6 +176,8 @@ def rank_program(g, core, T, topo):
         op("g", lambda: g.iota(out, pattern, base, 0, allow_small_or_imprecise_dtypes=True), (), w)
 
     def send(to, out, a, name, r):
+        if not to:
+            return
         dst = [T.cores[k] for k in to]
         sent[0] += len(topo.engines(core, dst[0]))
         if len(dst) == 1:
@@ -196,75 +201,116 @@ def rank_program(g, core, T, topo):
     def col(q, b):
         return q[:, 128 * b:128 * b + 128]
 
-    def table(l):
-        if l == 0:
+    def pf(k):
+        return T.pf[:, k:k + 1]
+
+    def home(m):
+        return (T.nw, "nw", RG * NEAR.index(m)) if m in NEAR else (T.nx, "nx", RG * FAR.index(m))
+
+    def made(m):
+        return [(home(m)[1], "a%d" % m), (home(m)[1], "b%d" % m)]
+
+    def table(m, first=0):
+        if m == 1:
             return T.n1[:], ["n1"]
-        return T.nw[:, 0:RG * (l + 1)], [("nw", i) for i in range(l + 1)] + [("nw", 10 + i) for i in range(1, l + 1)]
+        buf, name, at = home(m)
+        return buf[:, at + first:at + C + 5], made(m) + [(name, "stay")]
 
-    def jump(tab, offs, on):
-        tt(T.gl[:], tab[0].indirect(offs), T.dm[:, 0:64], ALU.mult, tab[1] + [on, "dm"], ["gl"])
+    def places(m, a, b):
+        buf, name, at = home(m)
+        return buf[:, at + a:at + b]
 
-    def fold():
-        scan(T.sl[:], T.rp[:, 0:64], T.gl[:], ["rp", "gl"], ["sl"])
+    def grow(call, m, have, by, a, b):
+        win, wk = table(have)
+        at = 12 if have == 1 else 0
+        call(places(m, 16 * a + 1, 16 * b + 1), win.indirect(T["off%d" % by][:, at + a:at + b]),
+             wk + [("off%d" % by, at)], [made(m)[0 if call is act else 1]])
+
+    def own(out, src, n, r, w):
+        scan(out, T.md[:, 0:n], src, ALU.mult, ALU.max, r + ["md"], w)
+
+    def ends(out, src, n, r, w):
+        ts(out, src[:, 15:n:16], T.sq[:, 15:16], None, ALU.mult, None, r + ["sq"], w)
+
+    ne = 1 if rank == 0 else 4
 
     dma("y", T.t0[:], T.x[:], (), ["t0"])
     dma("s", T.ut[:], T.u[:], (), ["ut"])
 
     op("g", lambda: g.iota(T.pi[:, 0:1], [[0, 1]], 0, 1), (), [("pi", 0)])
-    iota(T.jm[:], [[0, 16], [1, 16]], 0, ["jm"])
-    iota(T.nw[:, 0:RG], [[1, RG]], 0, [("nw", 0)])
-    iota(T.z3[:, 0:576:3], [[1, C]], 1, [("z3", 0)])
-    ms(T.d3[:], 1.0, ["d3"])
-    ms(T.d3m[:, 1:576:3], 1.0, [("d3m", 1)])
-    ms(T.d3m[:, 0:576:3], 0.0, [("d3m", 0)])
-    ms(T.rp[:], 1.0, ["rp"])
+    iota(T.jm[:], [[0, 12], [1, 16]], 0, ["jm"])
+    iota(T.nw[:, 0:C + 5], [[1, C + 5]], 0, [("nw", "a0")])
+    ms(T.eall[:], 0.0, ["eall"])
     ms(T.n1[:, 576:592], 0.0, [("n1", 1)])
     ts(T.pi[:, 1:2], T.pi[:, 0:1], 15, None, ALU.bitwise_and, None, [("pi", 0)], [("pi", 1)])
-    ms(T.d3[:, 0:576:3], 0.0, ["d3"])
-    ms(T.rp[:, 0:256:16], 0.0, ["rp"])
-    act(T.eall[:], T.d3[:, 0:516], ["d3"], ["eall"], 0.0)
-    cp(T.pf[:, 0:2], T.pi[:, 0:2], [("pi", 0), ("pi", 1)], [("pf", 0)])
-    for l in range(4):
-        ts(T.pi[:, 2 + l:3 + l], T.pi[:, 1:2], l, 1, ALU.logical_shift_right, ALU.bitwise_and, [("pi", 1)], [("pi", 2 + l)])
-        together("bits")
+    for k, c in enumerate((0.0, 4.0, 0.5)):
+        ms(T.zc[:, k:576:3], c, [("zc", k)])
+        together("zc")
+    cp(T.pf[:, 0:2], T.pi[:], ["pi"], [("pf", 0)])
+    for p in (0, C + 1, C + 2, C + 3, C + 4):
+        ms(T.nw[:, RG + p::RG], float(p), [("nw", "stay%d" % p)])
+        together("stay")
+    ms(places(53, 128, 129), 0.0, [("nw", "stay")])
+    together("stay")
+    ts(pf(9), pf(1), 1.0, None, ALU.add, None, [("pf", 0)], [("pf", 9)])
     ts(T.uoff[:, 0:8], T.jm[:, 0:8], 16.0, None, ALU.mult, None, ["jm"], [("uoff", 0)])
     together("uoff")
     ts(T.uoff[:, 8:16], T.jm[:, 0:8], 16.0, 1.0, ALU.mult, ALU.add, ["jm"], [("uoff", 1)])
     together("uoff")
-    ts(T.dm[:], T.jm[:], T.pf[:, 1:2], None, ALU.is_equal, None, ["jm", ("pf", 0)], ["dm"])
-    for e in range(4):
-        ts(T.off0[:, 12 + e:13 + e], T.pi[:, 2:3], float(2 * e - 586), float(588 + e), ALU.mult, ALU.add,
-           [("pi", 2)], [("off0", 1 + e)])
-        together("off0")
-    for l in range(1, 4):
-        ts(T.pf[:, 1 + l:2 + l], T.pi[:, 2 + l:3 + l], float(RG * l), None, ALU.mult, None, [("pi", 2 + l)], [("pf", l)])
-        together("base")
-    ts(T.d3m[:, 2:576:3], T.dm[:, 0:C], 1001.0, -1000.0, ALU.mult, ALU.add, ["dm"], [("d3m", 2)])
-    cp(T.n1[:, 578:590:3], T.nw[:, C:C + 4], [("nw", 0)], [("n1", 1)])
-    ts(T.eall[:, 3:515:4], T.nw[:, 0:128], T.pf[:, 0:1], None, ALU.is_equal, None, [("nw", 0), ("pf", 0)], ["eall"])
-    cp(T.n1[:, 588:592], T.jm[:, 0:4], ["jm"], [("n1", 1)])
-    for l in range(1, 7):
-        act(T.nw[:, RG * l + C:RG * l + RG], T.nw[:, C:RG], [("nw", 0)], [("nw", 10 + l)])
-        together("stay")
+    ts(T.sc[:], T.jm[:], pf(1), None, ALU.not_equal, None, ["jm", ("pf", 0)], ["sc"])
+    ts(T.sr[:], T.jm[:], pf(9), 2.0 ** 30, ALU.is_equal, ALU.mult, ["jm", ("pf", 9)], ["sr"])
+    ts(pf(3), pf(1), 15.0, 2.0 ** -30, ALU.is_equal, ALU.max, [("pf", 0)], [("pf", 3)])
+    quant(T.uq[:], T.us[:], T.ut[:], ["ut"], ["uq"])
+    act(T.zd[:, 2:576:3], T.nw[:, 0:C], [("nw", "a0")], [("zd", 2)], ACT.Identity, bias=2.0)
+    ts(T.oh[:, 0:16], T.jm[:, 0:16], pf(1), None, ALU.is_equal, None, ["jm", ("pf", 0)], [("oh", 0)])
+    together("sq")
+    ts(T.oh[:, 16:32], T.jm[:, 0:16], pf(1), 2.0 ** -8, ALU.not_equal, ALU.mult, ["jm", ("pf", 0)], [("oh", 1)])
+    together("sq")
+    ts(pf(8), pf(3), 3.0, None, ALU.mult, None, [("pf", 3)], [("pf", 8)])
+    cp(T.upq[:].bitcast(dt.uint32), T.uq[:].bitcast(dt.uint32).indirect(T.uoff[:]), ["uq", "uoff"], ["upq"])
+    act(T.ups[:], T.us[:].indirect(T.uoff[:]), ["uq", "uoff"], ["ups"])
+    act(T.zo[:, 1:576:3], T.sc[:], ["sc"], [("zo", 1)], ACT.Identity, scale=-3.0, bias=4.0)
+    together("zo")
+    act(T.zo[:, 2:576:3], T.sc[:], ["sc"], [("zo", 2)], ACT.Identity, scale=0.5, bias=0.5)
+    together("zo")
+
+    def masks():
+        tt(T.zo[:, 0:576:3], T.sc[:], T.sr[:], ALU.max, ["sc", "sr"], [("zo", 0)])
+        cp(T.n1[:, 578:590:3], T.nw[:, C + 1:C + 5], [("nw", "a0")], [("n1", 1)])
+        ms(T.fl[:], 1.0, ["fl"])
+
+    def more_masks():
+        ts(T.md[:], T.sc[:], 256.0, None, ALU.mult, None, ["sc"], ["md"])
+        scan(T.sq[:], T.oh[:, 16:32], T.oh[:, 0:16], ALU.mult, ALU.add, ["oh"], ["sq"])
+        cp(T.fl[:, 0:4], T.nw[:, 1:5], [("nw", "a0")], [("fl", 0)])
 
     def e_tile(b):
         quant(col(T.eq, b), col(T.es, b), T.eall[:, 3 - b:515 - b], ["eall"], [("eq", b)])
 
-    def pad(t):
-        quant(T["lq%d" % t][:, A:176], T["ls%d" % t][:, A:176], T.zt[:], ["zt"], [("l%d" % t, "pad")])
+    later = [
+        lambda: ts(T.eall[:, 3:515:4], T.nw[:, 0:128], pf(0), None, ALU.is_equal, None, [("nw", "a0"), ("pf", 0)], ["eall"]),
+        lambda: e_tile(0),
+        lambda: e_tile(1),
+        lambda: e_tile(2),
+        lambda: e_tile(3),
+        lambda: ts(pf(2), pf(1), 4.0, None, ALU.mult, None, [("pf", 0)], [("pf", 2)]),
+        lambda: ts(pf(5), pf(1), 2.0, 4.0, ALU.min, ALU.mult, [("pf", 0)], [("pf", 5)]),
+        lambda: ts(T.roff[:], T.jm[:, 0:4], pf(2), None, ALU.add, None, ["jm", ("pf", 2)], ["roff"]),
+        lambda: ts(pf(6), pf(5), -float(C + 1), None, ALU.add, None, [("pf", 5)], [("pf", 6)]),
+        lambda: ts(pf(7), pf(1), float(A - STEP), float(C + 1), ALU.is_lt, ALU.mult, [("pf", 0)], [("pf", 7)]),
+    ]
 
-    def pick_constants():
-        ts(T.pf[:, 6:7], T.pf[:, 1:2], 3.0, None, ALU.is_ge, None, [("pf", 0)], [("pf", 5)])
-        ts(T.pf[:, 5:6], T.pf[:, 1:2], 2.0, None, ALU.min, None, [("pf", 0)], [("pf", 4)])
-        ts(T.kr[:], T.jm[:, 0:12], 16.0, 0.5, ALU.mult, ALU.add, ["jm"], ["kr"])
-        ts(T.pf[:, 7:8], T.pf[:, 6:7], -2.0, 3.0, ALU.mult, ALU.add, [("pf", 5)], [("pf", 6)])
-        ts(T.pf[:, 8:9], T.pf[:, 6:7], 10.0, T.pf[:, 5:6], ALU.mult, ALU.add, [("pf", 5), ("pf", 4)], [("pf", 7)])
-        ts(T.jb[:], T.kr[:], T.pf[:, 1:2], None, ALU.add, None, ["kr", ("pf", 0)], ["jb"])
+    def fill(n):
+        for k in range(min(n, len(later))):
+            later.pop(0)()
 
-    quant(T.uq[:], T.us[:], T.ut[:], ["ut"], ["uq"])
-    n64 = T.nw[:, 6 * RG:7 * RG]
-    N64 = [("nw", 6), ("nw", 16)]
-    ends = T.sl[:, 15:64:16]
+    def count_constants():
+        ts(T.cs[:, 0:12], T.jm[:, 0:12], 16.0, 1.5, ALU.mult, ALU.add, ["jm"], ["cs"])
+        ms(T.cr[:], 1.0, ["cr"])
+        ts(T.ca[:, 0:5 * SPLIT:5], T.jm[:, 0:SPLIT], 8.0, None, ALU.mult, None, ["jm"], [("ca", "c0")])
+        ts(T.jb[:], T.cs[:, 0:12], pf(1), None, ALU.add, None, ["cs", ("pf", 0)], ["jb"])
+        ms(T.cr[:, 0:60:5], 0.0, ["cr"])
+        ts(T.ca[:, 5 * SPLIT:60:5], T.jm[:, SPLIT:12], 24.0, 16.0, ALU.mult, ALU.add, ["jm"], [("ca", "c1")])
 
     for t in range(R):
         def B(name):
@@ -273,41 +319,46 @@ def rank_program(g, core, T, topo):
         def K(name):
             return "%s%d" % (name, t)
 
-        def unpack(n):
-            b, name = n // 2, ("vh", "vh2")[n % 2]
-            act(T[name][:, C * b:C * b + C], ps(2 + b, 0, C), (), [("ps", 2 + b), (name, b)], 0.5)
+        def both(m, have, by, cut=6):
+            grow(act, m, have, by, 0, cut)
+            grow(cp, m, have, by, cut, 12)
+
+        def turn_a(m, n=C):
+            own(T.sc[:, 0:n], places(m, 1, n + 1), n, made(m), ["sc"])
+
+        def turn_b(m, n=C):
+            ends(T["off%d" % m][:, 0:n // 16], T.sc, n, ["sc"], ["off%d" % m])
+
+        def starts(call, m, on, n, r=(), w=()):
+            win, wk = table(m)
+            call(T.fl[:, 4 * m:4 * m + 16 * n], win.indirect(T[on][:, 0:n]), wk + [on] + list(r), [("fl", m)] + list(w))
+
+        def first(m):
+            src, rk = (T.n1[:, 2:12:3], [("n1", 0)]) if m == 1 else (places(m, 1, 5), made(m))
+            cp(T.fl[:, 4 * m:4 * m + 4], src, rk, [("fl", m)])
+
+        def order(call, c, have):
+            call(T.ro[:, 16 * ne * c:16 * ne * (c + 1)], T.fl[:, 64 * c:64 * c + 64].indirect(T.roff[:, 0:ne]),
+                 [("fl", k) for k in have] + ["roff"], [("ro", c)])
 
         helper, guest = (rank + HOP[t]) % N, (rank - HOP[t]) % N
         tq, tsc = B("tq"), B("ts")
-        if t == 0:
-            cp(T.upq[:].bitcast(dt.uint32), T.uq[:].bitcast(dt.uint32).indirect(T.uoff[:]), ["uq", "uoff"], ["upq"])
-            act(T.ups[:], T.us[:].indirect(T.uoff[:]), ["uq", "uoff"], ["ups"])
         quant(tq[:], tsc[:], B("t")[:], [K("t")], [K("tq")])
         send([helper], u8(B("gq")[:]), u8(tq[:]), K("aq"), [K("tq")])
         send([helper], B("gs")[:], tsc[:], K("aq"), [K("tq")])
         if t == 0:
-            act(T.zt[:], T.d3[:, 0:512], ["d3"], ["zt"], 0.0)
-            act(T.ft[:, 4 * A:], T.d3[:, 4 * A:512], ["d3"], [("ft", 9)], 0.0)
-            act(T.ht[:, 4 * A:], T.d3[:, 4 * A:512], ["d3"], [("ht", 9)], 0.0)
-            e_tile(0)
-            e_tile(1)
-        else:
-            pad(t)
-            if t == 1:
-                quant(T.vq[:], T.vs[:], T.vt[:], ["vt"], ["vq"])
-        for k in range(2):
+            masks()
+        for k in (1, 0):
             mm(k, C, col(T.upq, k), col(T.ups, k), tq[:], tsc[:], ["upq", "ups", K("tq")])
-        ts(T.z3[:, 1:576:3], ps(0, 0, C), 0.0, None, ALU.is_gt, None, (), [("ps", 0), ("z3", 1)])
-        together(K("signs"))
-        ts(T.z3[:, 2:576:3], ps(1, 0, C), 0.0, 2.0, ALU.is_gt, ALU.mult, (), [("ps", 1), ("z3", 2)])
-        together(K("signs"))
-        scan(T.n1m[:], T.d3m[:], T.z3[:], ["d3m", "z3"], ["n1m"])
-        scan(T.n1[:, 0:576], T.d3[:], T.z3[:], ["d3", "z3"], [("n1", 0)])
-        scan(T.sc[:], T.rp[:, 0:C], T.n1m[:, 2:576:3], ["rp", "n1m"], ["sc"], ALU.max)
-        jump(table(0), T.off0[:, 12:16], ("off0", 1))
-        ts(T.off0[:, 0:12], T.sc[:, 15:C:16], 3.0, 2.0, ALU.mult, ALU.add, ["sc"], [("off0", 0)])
-        ts(B("loff")[:], T.sc[:, 15:C:16], -1.0, float(C - 1), ALU.add, ALU.min, ["sc"], [K("loff")])
-        fold()
+        ts(T.zd[:, 0:576:3], ps(1, 0, C), 0.0, 0.25, ALU.is_gt, ALU.add, (), [("ps", 1), ("zd", 0)])
+        act(T.zd[:, 1:576:3], ps(0, 0, C), (), [("ps", 0), ("zd", 1)], ACT.Sign, bias=-1e-37)
+        if t == 0:
+            more_masks()
+        scan(T.so[:], T.zo[:], T.zd[:], ALU.mult, ALU.add, ["zd", "zo"], ["so"])
+        scan(T.n1[:, 0:576], T.zc[:], T.zd[:], ALU.mult, ALU.add, ["zd", "zc"], [("n1", 0)])
+        ts(T.off1[:, 12:24], T.so[:, 47:576:48], pf(8), -1.0, ALU.mult, ALU.add, ["so", ("pf", 8)], [("off1", 12)])
+        ts(B("loff")[:], T.so[:, 47:576:48], pf(3), float(C + 1), ALU.mult, ALU.min, ["so", ("pf", 3)], [K("loff")])
+        ts(T.off1[:, 0:12], T.so[:, 47:576:48], pf(3), None, ALU.mult, None, ["so", ("pf", 3)], [("off1", 0)])
         send([helper], B("ll")[:], B("loff")[:], K("al"), [K("loff")])
         if t == 0:
             dma("y", u8(T.wq[:]), T.wc[:], [K("loff")], ["wq"])
@@ -316,183 +367,247 @@ def rank_program(g, core, T, topo):
         arrive(K("aq"), 2 * width(guest), [K("gq")])
         arrive(K("al"), width(guest), [K("ll")])
         arrive(K("ac"), width(guest), [K("lc")])
-        cand = B("cand")
-        for l in range(5):
-            off, nxt = T["off%d" % l], T["off%d" % (l + 1)]
-            on, nn = "off%d" % l, "off%d" % (l + 1)
-            win, wk = table(l)
-            act(T.nw[:, RG * (l + 1):RG * (l + 1) + C], win.indirect(off[:, 0:12]), wk + [(on, 0)], [("nw", l + 1)])
-            tt(T.gm[:], win.indirect(off[:, 0:12]), T.dm[:, 0:C], ALU.mult, wk + [(on, 0), "dm"], ["gm"])
-            if l < 3:
-                ts(nxt[:, 12:16], ends, T.pf[:, 2 + l:3 + l], None, ALU.add, None, ["sl", ("pf", l + 1)], [(nn, 1)])
-            elif l == 3:
-                ts(nxt[:, 12:16], ends, float(RG * 4), None, ALU.add, None, ["sl"], [(nn, 1)])
-                ts(T.off5[:, 12:16], ends, float(RG * 5), None, ALU.add, None, ["sl"], [("off5", 1)])
+        both(2, 1, 1)
+        grow(act, 3, 2, 1, 0, 12)
+        first(1)
+        fill(1)
+        turn_a(2)
+        first(2)
+        fill(1)
+        turn_b(2)
+        fill(1)
+        both(5, 3, 2)
+        grow(act, 7, 5, 2, 0, 12)
+        first(3)
+        cp(T.fl[:, 16:32], table(2)[0].indirect(T.off2[:, 0:1]), table(2)[1] + ["off2"], [("fl", 4), ("fl", 5), ("fl", 7)])
+        turn_a(5)
+        own(T.sf[:, 0:32], T.fl[:, 0:32], 32, [("fl", k) for k in (0, 1, 2, 3, 4)], ["sf"])
+        fill(1)
+        turn_b(5)
+        ends(T.ta[:], T.sf, 32, ["sf"], ["ta"])
+        fill(1)
+        both(12, 7, 5)
+        grow(act, 17, 12, 5, 0, 12)
+        starts(cp, 5, "ta", 1, w=[("fl", 4), ("fl", 7)])
+        fill(1)
+        turn_a(12)
+        starts(cp, 7, "ta", 2, w=[("fl", 4), ("fl", 12)])
+        fill(1)
+        turn_b(12)
+        own(T.sf[:], T.fl[:, 0:A], A, [("fl", k) for k in (0, 1, 2, 3, 4, 5, 7)], ["sf"])
+        fill(3)
+        last = rank == N - 1
+        both(29, 17, 12, 6 if last else 8)
+        grow(act, 41, 29, 12, 0, 12)
+        ends(T.tb[:, 0:3], T.sf, A, ["sf"], ["tb"])
+        xn = K("exb" if rank == 1 else "exu")
+        ex, cand, cu = T[xn], B("cand"), B("cu")
+
+        def jump(step):
+            m = (29, 41, 41, 53)[step]
+            win, wk = table(m, 128 if step == 3 else 0)
+            src, on = T["x%d" % step], "x%d" % step
+            out, nn = (T["x%d" % (step + 1)], "x%d" % (step + 1)) if step < 3 else (ex, xn)
+            add = (0.0, 0.0, -128.0, -float(C + 1))[step]
+            if last:
+                return
+            if rank == 0:
+                ts(out[:, 0:16], win.indirect(src[:, 0:1]), add, None, ALU.add, None, wk + [on], [(nn, 0)])
+                if step == 3:
+                    together(K("ex"))
+                    ts(out[:, 16:32], win.indirect(src[:, 0:1]), pf(6), None, ALU.add, None, wk + [on, ("pf", 6)], [(nn, 1)])
+                    together(K("ex"))
+            elif step % 2 == 0:
+                a = 0 if step == 0 else 30
+                ts(out[:, 1:65], win.indirect(src[:, a:a + 4]), add, None, ALU.add, None, wk + [on], [nn])
             else:
-                cp(cand[:, 1:12:3], ends, ["sl"], [(K("cand"), 1)])
-                ts(T.off5[:, 16:20], ends, float(RG * 5), None, ALU.add, None, ["sl"], [("off5", 2)])
-            if l == 3:
-                for b in range(4):
-                    mm(2 + b, C, col(T.eq, b), col(T.es, b), B("gq")[:], B("gs")[:], [("eq", b), K("gq")])
-            if l >= 3:
-                unpack(l - 3)
-            scan(T.sc[:], T.rp[:, 0:C], T.gm[:], ["rp", "gm"], ["sc"])
-            if l == 3:
-                cp(cand[:, 0:12:3], ends, ["sl"], [(K("cand"), 0)])
-            jump(table(l + 1), nxt[:, 12:16], (nn, 1))
-            ts(nxt[:, 0:12], T.sc[:, 15:C:16], float(RG * (l + 1)), None, ALU.add, None, ["sc"], [(nn, 0)])
-            fold()
-            if t == 0 and l < 2:
-                e_tile(2 + l)
-        win, wk = table(5)
-        act(T.nw[:, RG * 6:RG * 6 + C], win.indirect(T.off5[:, 0:12]), wk + [("off5", 0)], [("nw", 6)])
-        for n in range(2, 8):
-            unpack(n)
-        if t == 0:
-            act(T.hw[:], T.d3[:, 0:256], ["d3"], ["hw"], 0.0)
-        ex, eu = B("ex"), B("eu")
-        if rank < N - 1:
-            cp(T.x0[:], win.indirect(T.off5[:, 0:1]), wk + [("off5", 0)], ["x0"])
-        cp(cand[:, 2:12:3], ends, ["sl"], [(K("cand"), 2)])
-        wd = 4 if rank == 0 else 12
-        send([helper], B("lc")[:, 0:wd], cand[:, 0:wd], K("ac"), [(K("cand"), c) for c in range(3)])
-        jump(table(5), T.off5[:, 16:20], ("off5", 2))
-        if rank == 0:
-            cp(T.x1[:, 0:16], n64.indirect(T.x0[:, 0:1]), N64 + ["x0"], ["x1"])
-            fold()
-            ts(eu[:], n64.indirect(T.x1[:, 0:1]), -float(C), None, ALU.add, None, N64 + ["x1"], [K("eu")])
-        elif rank < N - 1:
-            cp(T.x1[:, 1:65], n64.indirect(T.x0[:, 0:4]), N64 + ["x0"], ["x1"])
-            fold()
-            for h in range(2):
-                ts(T.msg[:, 32 * h:32 * h + 32], n64.indirect(T.x1[:, 16 + 32 * h:18 + 32 * h]), -float(C), None,
-                   ALU.add, None, N64 + ["x1"], [("msg", h)])
-                together(K("msg"))
-        else:
-            fold()
-        cp(cand[:, 12:16], ends, ["sl"], [(K("cand"), 3)])
-        if 0 < rank < N - 1:
-            cp(ex[:], T.msg[:, 0:64:16], ["msg"], [K("ex")])
-        if rank < N - 1:
-            src, sk = (eu[:, 0:2], K("eu")) if rank == 0 else (ex[:], K("ex"))
-            first = [r for r in range(N) if r != rank and (r - HOP[t]) % N > rank]
-            first.sort(key=lambda r: -((r - HOP[t]) % N))
-            send(first + [r for r in range(rank + 1, N) if r not in first], B("lm%d_" % rank)[:], src, K("am%d_" % rank), [sk])
-        if t == 0:
-            pick_constants()
+                for h in range(2):
+                    a = h if step == 1 else 2 + h
+                    ts(out[:, a:a + 64:2], win.indirect(src[:, 16 + 32 * h:18 + 32 * h]),
+                       pf(6) if step == 3 and rank == 2 else add, None, ALU.add, None, wk + [on, ("pf", 6)], [(nn, h)])
+                    together(K("j%d_" % step))
+
+        if not last:
+            cp(T.x0[:], table(17)[0].indirect(T.off12[:, 0:1]), table(17)[1] + ["off12"], ["x0"])
+        starts(cp, 12, "tb", 2, w=[("fl", 7), ("fl", 17)])
+        jump(0)
+        starts(cp, 29, "tb", 3)
+        starts(cp, 17, "tb", 3, w=[("fl", 12)])
+        starts(act, 41, "tb", 2)
+        if not last:
+            grow(act, 53, 41, 12, 8, 12)
+        order(act, 2, (29, 41))
+        jump(1)
+        order(cp, 0, (0, 1, 2, 3, 4, 5, 7, 12))
+        jump(2)
+        order(cp, 1, (12, 17, 29))
+        jump(3)
+        own(T.sr[:, 0:A * ne], T.ro[:, 0:A * ne], A * ne, ["ro"], ["sr"])
         for b in range(4):
-            tt(T.fa[:, C * b:C * b + C], T.vh[:, C * b:C * b + C].indirect(B("ll")[:]), T.vh2[:, C * b:C * b + C], ALU.add,
-               [("vh", b), ("vh2", b), K("ll")], [("fa", b)])
+            mm(2 + b, C, col(T.eq, b), col(T.es, b), B("gq")[:], B("gs")[:], [("eq", b), K("gq")])
+        if t == 0:
+            ms(T.vh[:, 0:4 * RG:RG], 0.0, [("vh", 8)])
+            ms(T.vh[:, 1:4 * RG:RG], 0.0, [("vh", 9)])
+        else:
+            turn_a(41, 112)
+        if rank == 0:
+            ends(cu[:, 0:3], T.sr, A, ["sr"], [K("cu")])
+        else:
+            ends(cand[:], T.sr, C, ["sr"], [K("cand")])
+        for b in range(4):
+            act(T.vh[:, RG * b + 2:RG * b + 2 + C], ps(2 + b, 0, C), [("ps", 2 + b)], [("vh", b)], scale=0.5)
+            together(K("vh%d_" % b))
+            act(T.vh2[:, C * b:C * b + C], ps(2 + b, 0, C), [("ps", 2 + b)], [("vh2", b)], scale=0.5)
+            together(K("vh%d_" % b))
+        helpers = [r for r in range(N) if r != rank and (r - HOP[t]) % N > rank]
+        helpers.sort(key=lambda r: -((r - HOP[t]) % N))
+        src = ex[:, 14:18] if rank == 0 else ex[:, 32:36]
+        homes = [r for r in range(rank + 1, N) if r not in helpers]
+        if not last:
+            send(helpers + (homes if ORDER == 1 else []), B("lm%d_" % rank)[:], src, K("am%d_" % rank), [xn])
+        if rank == 0:
+            send([helper], B("lu")[:, 0:3], cu[:, 0:3], K("ac"), [K("cu")])
+        else:
+            send([helper], B("lc")[:], cand[:], K("ac"), [K("cand")])
+        if not last and ORDER == 0:
+            send(homes, B("lm%d_" % rank)[:], src, K("am%d_" % rank), [xn])
+
+        def pack(b):
+            tt(T.fa[:, RG * b + 1:RG * b + 1 + C], T.vh[:, RG * b:RG * b + 2 + C].indirect(B("ll")[:]),
+               T.vh2[:, C * b:C * b + C], ALU.add, [("vh", b), ("vh2", b), ("vh", 8), ("vh", 9), K("ll")], [("fa", b)])
             together(K("fa"))
+
+        if t == 0:
+            ms(T.nx[:], 200.0, ["nx"])
+            turn_a(41, 112)
+            ms(T.fa[:, 0:4 * RG:RG], 0.0, [("fa", 9)])
+            ms(T.ft[:, 4 * A:], 0.0, [("ft", 9)])
+            ms(T.ht[:, 4 * A:], 0.0, [("ht", 9)])
+        turn_b(41, 112)
+        pack(0)
+        grow(cp, 82, 41, 41, 0, 7)
+        pack(1)
+        grow(cp, 123, 82, 41, 0, 5)
+        pack(2)
+        grow(cp, 164, 123, 41, 0, 2)
+        pack(3)
         for r in range(max(rank, guest)):
             if r != rank:
                 arrive(K("am%d_" % r), width(r), [K("lm%d_" % r)])
-        have = []
 
-        def exits(r):
-            n0 = "eu" if rank == 0 else "lm0_"
-            if r == 0:
-                return B(n0)[:, 0:2], [K(n0)], 2
-            name = "ex" if r == rank else "lm%d_" % r
-            if r == 1:
-                return B(name)[:].indirect(B(n0)[:, 0:1]), [K(name), K(n0)], 16
-            if not have:
-                src, rk, n = exits(1)
-                cp(T.ch2[:], src, rk, ["ch2"])
-                have.append(1)
-            return B(name)[:].indirect(T.ch2[:, 0:1]), [K(name), "ch2"], 16
+        def told(r, a=0, n=4):
+            if r == rank:
+                at = 14 if r == 0 else 32
+                return ex[:, at + a:at + a + n], xn
+            return B("lm%d_" % r)[:, a:a + n], K("lm%d_" % r)
 
-        def choose(r, a, b, sel):
-            if r > 0:
-                src, rk, n = exits(r - 1)
-                ts(T[sel][:, 0:n], src, a, b, ALU.mult, ALU.add, rk + ["pf"], [sel])
+        def choose(r, lists, ln, sel):
+            if r >= 2:
+                (win, wn), (v0, vn) = told(1), told(0, 0, 1)
+                if r == 2:
+                    ts(T[sel][:], win.indirect(v0), pf(5), None, ALU.add, None, [wn, vn, ("pf", 5)], [sel])
+                else:
+                    ts(T[sel][:], win.indirect(v0), 16.0, pf(1), ALU.mult, ALU.add, [wn, vn, ("pf", 0)], [sel])
+                    cp(T.via[:], lists[:].indirect(told(2)[0]), [ln, told(2)[1]], ["via"])
 
         def pick(r, lists, ln, sel, out):
-            if r == 0 and out == "goff":
-                cp(T.goff[:, 0:4], lists[:, 0:4], [ln], [out])
-            elif r == 0:
-                cp(T.soff[:, 0:3], lists[:, 0:3], [ln], [(out, 0)])
-                cp(T.soff[:, 3:4], lists[:, 12:13], [ln], [(out, 1)])
-            else:
+            if r == 1:
+                cp(T[out][:], lists[:].indirect(told(0, 2, 1)[0]), [ln, told(0)[1]], [out])
+            elif r == 2:
                 cp(T[out][:], lists[:].indirect(T[sel][:, 0:1]), [ln, sel], [out])
+            elif r == 3:
+                cp(T[out][:], T.via[:].indirect(T[sel][:, 0:1]), ["via", sel], [out])
 
-        if rank == 0:
-            pick(rank, cand, K("cand"), "osel", "soff")
-        choose(guest, 3.0, T.pf[:, 5:6], "gsel")
-        if 0 < rank < guest:
-            choose(rank, T.pf[:, 7:8], T.pf[:, 8:9], "osel")
+        goff, gn = (T.goff, "goff") if guest > 0 else (B("lu"), K("lc"))
+        soff, sn = (T.soff, "soff") if rank > 0 else (cu, K("cu"))
+
+        def blocks():
+            ts(T.sofb[:, 0:1], soff[:, 0:1], pf(7), None, ALU.max, None, [sn, ("pf", 7)], [("sofb", 0)])
+            together(K("sofb"))
+            cp(T.sofb[:, 1:3], soff[:, 1:3], [sn], [("sofb", 1)])
+            together(K("sofb"))
+
+        choose(guest, B("lc"), K("lc"), "gsel")
+        if rank < guest:
+            choose(rank, cand, K("cand"), "osel")
         pick(guest, B("lc"), K("lc"), "gsel", "goff")
-        if 0 < rank < guest:
+        if rank < guest:
             pick(rank, cand, K("cand"), "osel", "soff")
         for b in range(4):
-            src = T.fa[:, C * b:C * b + C].indirect(T.goff[:, 0:3])
-            (cp if b % 2 == 0 else act)(T.ft[:, b:4 * A:4], src, [("fa", b), "goff"], [("ft", b)])
+            src = T.fa[:, RG * b:RG * b + 1 + C].indirect(goff[:, 0:3])
+            (cp if b % 2 == 0 else act)(T.ft[:, b:4 * A:4], src, [("fa", b), ("fa", 9), gn], [("ft", b)])
             together(K("ft%d_" % (b % 2)))
+        if rank < guest:
+            blocks()
         quant(T.fq[:], T.fs[:], T.ft[:], ["ft"], ["fq"])
         for b in range(4):
             mm(2 + b, 128, col(T.wq, b), col(T.wsc, b), T.fq[:], T.fs[:], ["wq", "wsc", "fq"])
-        if t == 0:
-            ts(T.cb[:, 0:SPLIT], T.jm[:, 0:SPLIT], 20.0, 16.0, ALU.mult, ALU.add, ["jm"], [("cb", 0)])
-            ts(T.cb[:, SPLIT:12], T.jm[:, SPLIT:12], 8.0, None, ALU.mult, None, ["jm"], [("cb", 1)])
         if rank > guest:
-            choose(rank, T.pf[:, 7:8], T.pf[:, 8:9], "osel")
+            choose(rank, cand, K("cand"), "osel")
             pick(rank, cand, K("cand"), "osel", "soff")
-        else:
-            jump((n64, N64), T.soff[:, 0:4], "soff")
-            fold()
+        elif t == 0:
+            count_constants()
         for b in range(4):
             ts(T.ht[:, b:4 * A:4], ps(2 + b, 0, A), 0.03125, None, ALU.mult, None, (), [("ps", 2 + b), ("ht", b)])
             together(K("ht"))
+        if rank > guest:
+            blocks()
+        for m in range(5):
+            win, wk = table(STEP * m)
+            offs, on = (soff, sn) if m == 0 else (T.sofb, "sofb")
+            act(T.sb[:, A * m:A * m + A], win.indirect(offs[:, 0:3]), wk + [on], [("sb", m)])
+            together(K("sb%d_" % (m // 3)))
         quant(B("hq")[:], B("hs")[:], T.ht[:], ["ht"], [K("hq")])
-        send([guest], u8(B("lq")[:, 0:A]), u8(B("hq")[:, 0:A]), K("ah"), [K("hq")])
-        send([guest], B("ls")[:, 0:A], B("hs")[:, 0:A], K("ah"), [K("hq")])
-        act(T.sb[:, 0:64], T.nw[:, 0:RG].indirect(T.soff[:, 0:4]), [("nw", 0), "soff"], [("sb", 0)])
-        act(T.sb[:, 64:128], n64.indirect(T.soff[:, 0:4]), N64 + ["soff"], [("sb", 1)])
-        if rank > guest:
-            jump((n64, N64), T.soff[:, 0:4], "soff")
-        ts(T.m0[:], T.jb[:], T.sb[:, A:A + 1], -96.0, ALU.is_gt, ALU.mult, ["jb", ("sb", 0)], ["m0"])
-        if rank > guest:
-            fold()
-        ts(T.m1[:], T.jb[:], T.sb[:, 2 * A:2 * A + 1], -96.0, ALU.is_gt, ALU.mult, ["jb", ("sb", 1)], ["m1"])
-        cp(T.k2[:], ends, ["sl"], ["k2"])
-        tt(T.m3[:], T.m0[:], T.cb[:], ALU.add, ["m0", "cb"], ["m3"])
-        cp(T.sb[:, 128:192], n64.indirect(T.k2[:]), N64 + ["k2"], [("sb", 2)])
-        tt(T.m4[:], T.m1[:], T.m3[:], ALU.add, ["m1", "m3"], ["m4"])
-        ts(T.m2[:], T.jb[:], T.sb[:, 3 * A:3 * A + 1], -96.0, ALU.is_gt, ALU.mult, ["jb", ("sb", 2)], ["m2"])
+        land = A * (R - 1 - t)
+        send([guest], u8(T.lq[:, land:land + A]), u8(B("hq")[:, 0:A]), K("ah"), [K("hq")])
+        send([guest], T.ls[:, land:land + A], B("hs")[:, 0:A], K("ah"), [K("hq")])
 
         def span(c):
-            return 4 * c, 16 * c + 16, 6 * c * (c - 1) + 16 * c
+            return 4 * c, 20 * c + 16, 8 * c * (c + 1), [("sb", i) for i in range((20 * c + 15) // A + 1)] + ["jb"]
 
-        for c in range(SPLIT):
-            lo, hi, at = span(c)
-            op("s", lambda c=c, lo=lo, hi=hi, at=at: S.activation(
-                T.junk[:, at:at + hi - lo], T.sb[:, lo:hi], ACT.Sign, bias=T.jb[:, c:c + 1], scale=-1.0,
-                accum_out=T.acc[:, c:c + 1]), [("sb", i) for i in range((hi + 63) // 64)] + ["jb"], [("acc", c), ("junk", c)])
+        if t == 0 and rank > guest:
+            count_constants()
+        for c in range(SPLIT, 12):
+            lo, hi, at, rk = span(c)
+            act(T.junk[:, at:at + hi - lo], T.sb[:, lo:hi], rk, [("ca", c), ("junk", c)], ACT.Sign,
+                bias=T.jb[:, c:c + 1], scale=-1.0, accum_out=T.ca[:, 5 * c + 4:5 * c + 5])
             together(K("count"))
-        for c in range(SPLIT, 12):
-            lo, hi, at = span(c)
-            ts(T.junk[:, at:at + hi - lo], T.sb[:, lo:hi], T.jb[:, c:c + 1], 2.0, ALU.is_lt, ALU.mult, ["sb", "jb"], [("junk", c)])
-        tt(T.m5[:], T.m2[:], T.m4[:], ALU.add, ["m2", "m4"], ["m5"])
-        for c in range(SPLIT, 12):
-            lo, hi, at = span(c)
+        for c in range(SPLIT):
+            lo, hi, at, rk = span(c)
+            ts(T.junk[:, at:at + hi - lo], T.sb[:, lo:hi], T.jb[:, c:c + 1], 2.0, ALU.is_lt, ALU.mult, rk, [("junk", c)])
+            together(K("less"))
+        for m in range(1, 4):
+            at = m * (2 * A - STEP)
+            ts(T.ca[:, m:60:5], T.jb[:], T.sb[:, at:at + 1], -96.0, ALU.is_gt, ALU.mult, ["jb", ("sb", m)], [("ca", "m%d" % m)])
+            together(K("sums"))
+        for c in range(SPLIT):
+            lo, hi, at, rk = span(c)
             op("v", lambda c=c, lo=lo, hi=hi, at=at: V.tensor_reduce(
-                T.acc[:, c:c + 1], T.junk[:, at:at + hi - lo], AxisListType.X, ALU.add), [("junk", c)], [("acc", c)])
+                T.ca[:, 5 * c + 4:5 * c + 5], T.junk[:, at:at + hi - lo], AxisListType.X, ALU.add), [("junk", c)], [("ca", c)])
+            together(K("sums"))
         if t == 0:
-            pad(0)
-        tt(T.ks[:], T.acc[:], T.m5[:], ALU.add, ["acc", "m5"], ["ks"])
-        ts(T.koff[:], T.ks[:], 0.5, None, ALU.mult, None, ["ks"], ["koff"])
+            ms(T.zt[:], 0.0, ["zt"])
+            ms(T.hw[:, 0:256:64], 0.0, [("hw", 9)])
+        if t == 1:
+            quant(T.vq[:], T.vs[:], T.vt[:], ["vt"], ["vq"])
+        scan(T.cs[:], T.cr[:], T.ca[:], ALU.mult, ALU.add, ["cr", "ca"], ["cs"])
+        if t == 0:
+            quant(T.lq[:, R * A:], T.ls[:, R * A:], T.zt[:], ["zt"], [("lq", "pad")])
+        ts(T.koff[:], T.cs[:, 4:60:5], 0.5, None, ALU.mult, None, ["cs"], ["koff"])
         if t == R - 1:
-            dma("y", T.ol[:], T.sb[0:128:16, 0:A], [("sb", 0)], ())
-        arrive(K("ah"), 2 * width(helper), [(K("l"), "h")])
+            act(T.olf[:], T.sb[:, 0:A], [("sb", 0)], ["olf"], ACT.Identity, bias=-1.0)
+            dma("y", T.ol[:], T.olf[0:128:16, :], ["olf"], ())
+        arrive(K("ah"), 2 * width(helper), [("lq", t)])
         banks = [0, 1, 6, 7]
         for b in range(4):
-            mm(banks[b], 128, col(T.eq, b), col(T.es, b), B("lq")[:, 0:128], B("ls")[:, 0:128], [("eq", b), K("l")])
+            mm(banks[b], 128, col(T.eq, b), col(T.es, b), T.lq[:, land:land + 128], T.ls[:, land:land + 128],
+               [("eq", b), ("lq", "pad")] + [("lq", k) for k in range(t + 1)])
         for b in range(4):
-            act(T.hw[:, 64 * b + 1:64 * b + 1 + A], ps(banks[b], 0, A), (), [("ps", banks[b]), ("hw", b)])
+            (cp if b == 0 else act)(T.hw[:, 64 * b + 1:64 * b + 1 + A], ps(banks[b], 0, A), (), [("ps", banks[b]), ("hw", b)])
         new = "t%d" % (t + 1)
         for b in range(4):
-            tt(T[new][:, b:4 * C:4], T.hw[:, 64 * b:64 * b + 64].indirect(T.koff[:]), B("t")[:, b:4 * C:4], ALU.add,
-               [("hw", b), "koff", K("t")], [(new, b)])
+            tt(T[new][:, b:4 * C:4], T.hw[:, 64 * b:64 * b + 1 + A].indirect(T.koff[:]), B("t")[:, b:4 * C:4], ALU.add,
+               [("hw", b), ("hw", 9), "koff", K("t")], [(new, b)])
             together(K("new"))
 
     tq, tsc, qn = T["tq%d" % R], T["ts%d" % R], "tq%d" % R

@@ -10,7 +10,14 @@ NEAR = [0, 2, 3, 5, 7, 12, 17, 29, 41, 53]
 FAR = [82, 123, 164]
 STEP = 41
 SPLIT = 6
-ORDER = 0
+ORD = [[1, 1, 1, 1], [1, 1, 1, 1], [1, 1, 1, 1]]
+EU = [-1, 0, 0]
+VIA = [1, 0, 0]
+SGN = [1, 1, 1]
+SG0 = [1, 1, -1]
+CC = 0
+APART = 1
+EARLY = 1
 X4, U8 = "float8_e4m3fn_x4", "uint8"
 BF, F32, U16 = "bfloat16", "float32", "uint16"
 
@@ -19,14 +26,14 @@ for _n, _w, _d in [
         ("ut", 512, BF), ("vt", 512, BF), ("uq", 128, X4), ("us", 128, U8), ("upq", 256, X4), ("ups", 256, U8),
         ("vq", 128, X4), ("vs", 128, U8), ("wq", 512, X4), ("wsc", 512, U8), ("fq", 128, X4), ("fs", 128, U8),
         ("eall", 516, BF), ("eq", 512, X4), ("es", 512, U8), ("zt", 512, BF), ("ft", 512, BF), ("ht", 512, BF),
-        ("jm", C, BF), ("pi", 2, "int32"), ("pf", 10, F32), ("md", C, BF), ("oh", 32, BF),
+        ("jm", C, BF), ("pi", 2, "int32"), ("pf", 14, F32), ("md", C, BF), ("oh", 32, BF),
         ("sq", 16, F32), ("zd", 576, BF), ("zc", 576, BF), ("zo", 576, BF), ("so", 576, BF), ("n1", 592, BF),
-        ("nw", RG * len(NEAR), BF), ("nx", RG * len(FAR), BF), ("fl", 224, BF), ("sf", A, BF),
-        ("sc", C, BF), ("ro", C, BF), ("sr", C, BF), ("vh2", 4 * C, BF), ("via", 64, BF),
+        ("nw", RG * len(NEAR), BF), ("nx", RG * len(FAR), BF), ("fl", 240, BF), ("sf", 96, BF),
+        ("sc", C, BF), ("me", 52, BF), ("sr", 256, BF), ("vh2", 4 * C, BF), ("via", 64, BF),
         ("uoff", 16, U16), ("off1", 24, U16), ("off2", 12, U16), ("off5", 12, U16), ("off12", 12, U16),
-        ("off41", 8, U16), ("ta", 2, U16), ("tb", 4, U16), ("roff", 4, U16),
+        ("off41", 8, U16), ("ta", 2, U16), ("tb", 6, U16),
         ("x0", 16, U16), ("x1", 66, U16), ("x2", 66, U16), ("x3", 66, U16),
-        ("osel", 16, U16), ("gsel", 16, U16), ("soff", 16, U16), ("sofb", 4, U16), ("goff", 16, U16),
+        ("ch", 16, U16), ("osel", 16, U16), ("gsel", 16, U16), ("soff", 16, U16), ("sofb", 4, U16), ("goff", 16, U16),
         ("koff", 12, U16), ("lq", 272, X4), ("ls", 272, U8),
         ("sb", 5 * A, BF), ("olf", A, F32), ("junk", 1248, BF), ("jb", 12, F32),
         ("ca", 60, F32), ("cr", 60, F32), ("cs", 60, F32),
@@ -38,8 +45,8 @@ for _t in range(R + 1):
 for _t in range(R):
     for _n, _w, _d in [("hq", 128, X4), ("hs", 128, U8), ("gq", C, X4), ("gs", C, U8),
                        ("exb", 68, BF), ("exu", 68, U16), ("loff", 12, U16), ("ll", 12, U16),
-                       ("cand", 12, BF), ("lc", 12, BF), ("cu", 4, U16), ("lu", 4, U16),
-                       ("lm0_", 4, U16), ("lm1_", 4, BF), ("lm2_", 4, U16)]:
+                       ("cand", 15, BF), ("lc", 15, BF), ("cu", 4, U16), ("lu", 4, U16),
+                       ("lm0_", 4, U16), ("lm1_", 4, BF), ("lm2_", 4, U16 if VIA[_t] else BF)]:
         SCRATCH["%s%d" % (_n, _t)] = ("sbuf", [128, _w], _d)
 
 POOL = {"v": ["v%d" % i for i in range(60)], "s": ["s%d" % i for i in range(28)],
@@ -112,7 +119,7 @@ def emit(g, T, ops, sent):
         elif o.get("need"):
             if "sig" not in o:
                 mates = groups[o["grp"]] if o.get("grp") else [n]
-                name = [s for s in POOL[o["q"]] if s not in last or last[s] in o["known"]][0]
+                name = [s for s in POOL[o["q"]] if s not in last or all(last[s] in ops[m]["known"] for m in mates)][0]
                 sig = (name, (ops[last[name]]["sig"][1] if name in last else 0) + len(mates))
                 last[name] = mates[-1]
                 for m in mates:
@@ -234,8 +241,8 @@ def rank_program(g, core, T, topo):
 
     ne = 1 if rank == 0 else 4
 
+    dma("y", T.ut[:], T.u[:], (), ["ut"])
     dma("y", T.t0[:], T.x[:], (), ["t0"])
-    dma("s", T.ut[:], T.u[:], (), ["ut"])
 
     op("g", lambda: g.iota(T.pi[:, 0:1], [[0, 1]], 0, 1), (), [("pi", 0)])
     iota(T.jm[:], [[0, 12], [1, 16]], 0, ["jm"])
@@ -250,16 +257,26 @@ def rank_program(g, core, T, topo):
     for p in (0, C + 1, C + 2, C + 3, C + 4):
         ms(T.nw[:, RG + p::RG], float(p), [("nw", "stay%d" % p)])
         together("stay")
+    ts(pf(9), pf(1), 1.0, None, ALU.add, None, [("pf", 0)], [("pf", 9)])
     ms(places(53, 128, 129), 0.0, [("nw", "stay")])
     together("stay")
-    ts(pf(9), pf(1), 1.0, None, ALU.add, None, [("pf", 0)], [("pf", 9)])
     ts(T.uoff[:, 0:8], T.jm[:, 0:8], 16.0, None, ALU.mult, None, ["jm"], [("uoff", 0)])
     together("uoff")
     ts(T.uoff[:, 8:16], T.jm[:, 0:8], 16.0, 1.0, ALU.mult, ALU.add, ["jm"], [("uoff", 1)])
     together("uoff")
     ts(T.sc[:], T.jm[:], pf(1), None, ALU.not_equal, None, ["jm", ("pf", 0)], ["sc"])
-    ts(T.sr[:], T.jm[:], pf(9), 2.0 ** 30, ALU.is_equal, ALU.mult, ["jm", ("pf", 9)], ["sr"])
     ts(pf(3), pf(1), 15.0, 2.0 ** -30, ALU.is_equal, ALU.max, [("pf", 0)], [("pf", 3)])
+    ts(T.sr[:, 0:C], T.jm[:], pf(9), 2.0 ** 30, ALU.is_equal, ALU.mult, ["jm", ("pf", 9)], ["sr"])
+    ts(pf(5), pf(1), 2.0, None, ALU.min, None, [("pf", 0)], [("pf", 5)])
+    together("pf")
+    ts(pf(6), pf(1), 2.0, -4.0 * (C + 1), ALU.min, ALU.add, [("pf", 0)], [("pf", 6)])
+    together("pf")
+    ms(T.me[:, 13:16], 1.0, [("me", 1)])
+    together("pf")
+    ms(T.me[:, 12:13], 256.0, [("me", 3)])
+    together("pf")
+    iota(T.nx[:], [[0, RG * len(FAR)]], 200, ["nx"])
+    act(T.zt[:], T.eall[:, 0:512], ["eall"], ["zt"])
     quant(T.uq[:], T.us[:], T.ut[:], ["ut"], ["uq"])
     act(T.zd[:, 2:576:3], T.nw[:, 0:C], [("nw", "a0")], [("zd", 2)], ACT.Identity, bias=2.0)
     ts(T.oh[:, 0:16], T.jm[:, 0:16], pf(1), None, ALU.is_equal, None, ["jm", ("pf", 0)], [("oh", 0)])
@@ -267,15 +284,25 @@ def rank_program(g, core, T, topo):
     ts(T.oh[:, 16:32], T.jm[:, 0:16], pf(1), 2.0 ** -8, ALU.not_equal, ALU.mult, ["jm", ("pf", 0)], [("oh", 1)])
     together("sq")
     ts(pf(8), pf(3), 3.0, None, ALU.mult, None, [("pf", 3)], [("pf", 8)])
-    cp(T.upq[:].bitcast(dt.uint32), T.uq[:].bitcast(dt.uint32).indirect(T.uoff[:]), ["uq", "uoff"], ["upq"])
-    act(T.ups[:], T.us[:].indirect(T.uoff[:]), ["uq", "uoff"], ["ups"])
-    act(T.zo[:, 1:576:3], T.sc[:], ["sc"], [("zo", 1)], ACT.Identity, scale=-3.0, bias=4.0)
-    together("zo")
-    act(T.zo[:, 2:576:3], T.sc[:], ["sc"], [("zo", 2)], ACT.Identity, scale=0.5, bias=0.5)
-    together("zo")
+    ts(pf(2), pf(1), 1.5, None, ALU.add, None, [("pf", 0)], [("pf", 2)])
+
+    def u_pick(k):
+        offs = T.uoff[:, 8 * k:8 * k + 8]
+        cp(col(T.upq, k).bitcast(dt.uint32), T.uq[:].bitcast(dt.uint32).indirect(offs), ["uq", "uoff"], [("upq", k)])
+        together("up%d" % k)
+        act(col(T.ups, k), T.us[:].indirect(offs), ["uq", "uoff"], [("ups", k)])
+        together("up%d" % k)
+
+    u_pick(0)
 
     def masks():
-        tt(T.zo[:, 0:576:3], T.sc[:], T.sr[:], ALU.max, ["sc", "sr"], [("zo", 0)])
+        u_pick(1)
+        act(T.zo[:, 1:576:3], T.sc[:], ["sc"], [("zo", 1)], ACT.Identity, scale=-3.0, bias=4.0)
+        together("zo")
+        act(T.zo[:, 2:576:3], T.sc[:], ["sc"], [("zo", 2)], ACT.Identity, scale=0.5, bias=0.5)
+        together("zo")
+        dma("s", T.wsc[:], T.ws[:], ["t0"], ["wsc"])
+        tt(T.zo[:, 0:576:3], T.sc[:], T.sr[:, 0:C], ALU.max, ["sc", "sr"], [("zo", 0)])
         cp(T.n1[:, 578:590:3], T.nw[:, C + 1:C + 5], [("nw", "a0")], [("n1", 1)])
         ms(T.fl[:], 1.0, ["fl"])
 
@@ -289,28 +316,35 @@ def rank_program(g, core, T, topo):
 
     later = [
         lambda: ts(T.eall[:, 3:515:4], T.nw[:, 0:128], pf(0), None, ALU.is_equal, None, [("nw", "a0"), ("pf", 0)], ["eall"]),
+        lambda: cp(T.me[:, 0:12], T.md[:, 0:12], ["md"], [("me", 0)]),
         lambda: e_tile(0),
         lambda: e_tile(1),
+        lambda: cp(T.me[:, 17:52], T.md[:, 13:48], ["md"], [("me", 2)]),
         lambda: e_tile(2),
         lambda: e_tile(3),
-        lambda: ts(pf(2), pf(1), 4.0, None, ALU.mult, None, [("pf", 0)], [("pf", 2)]),
-        lambda: ts(pf(5), pf(1), 2.0, 4.0, ALU.min, ALU.mult, [("pf", 0)], [("pf", 5)]),
-        lambda: ts(T.roff[:], T.jm[:, 0:4], pf(2), None, ALU.add, None, ["jm", ("pf", 2)], ["roff"]),
-        lambda: ts(pf(6), pf(5), -float(C + 1), None, ALU.add, None, [("pf", 5)], [("pf", 6)]),
+        lambda: ts(T.me[:, 16:17], T.md[:, 12:13], 2.0 ** -8, None, ALU.mult, None, ["md"], [("me", 4)]),
         lambda: ts(pf(7), pf(1), float(A - STEP), float(C + 1), ALU.is_lt, ALU.mult, [("pf", 0)], [("pf", 7)]),
+        lambda: ts(T.jb[:], T.jm[:, 0:12], 16.0, pf(2), ALU.mult, ALU.add, ["jm", ("pf", 2)], ["jb"]),
     ]
 
     def fill(n):
         for k in range(min(n, len(later))):
             later.pop(0)()
 
-    def count_constants():
-        ts(T.cs[:, 0:12], T.jm[:, 0:12], 16.0, 1.5, ALU.mult, ALU.add, ["jm"], ["cs"])
-        ms(T.cr[:], 1.0, ["cr"])
-        ts(T.ca[:, 0:5 * SPLIT:5], T.jm[:, 0:SPLIT], 8.0, None, ALU.mult, None, ["jm"], [("ca", "c0")])
-        ts(T.jb[:], T.cs[:, 0:12], pf(1), None, ALU.add, None, ["cs", ("pf", 0)], ["jb"])
-        ms(T.cr[:, 0:60:5], 0.0, ["cr"])
-        ts(T.ca[:, 5 * SPLIT:60:5], T.jm[:, SPLIT:12], 24.0, 16.0, ALU.mult, ALU.add, ["jm"], [("ca", "c1")])
+    def borders():
+        for out, n, on in [(T.vh[:, 0:4 * RG:RG], 4, ("vh", 8)), (T.vh[:, 1:4 * RG:RG], 4, ("vh", 9)),
+                           (T.fa[:, 0:4 * RG:RG], 4, ("fa", 9)), (T.ft[:, 4 * A:], 320, ("ft", 9)),
+                           (T.ht[:, 4 * A:], 320, ("ht", 9)), (T.hw[:, 0:256:64], 4, ("hw", 9)),
+                           (T.cr[:, 0:60:5], 12, ("cr", 0))]:
+            iota(out, [[0, n]], 0, [on])
+            together("borders")
+        for k in range(1, 5):
+            iota(T.cr[:, k:60:5], [[0, 12]], 1, [("cr", k)])
+            together("borders")
+        iota(T.ca[:, 0:5 * SPLIT:5], [[8, SPLIT]], 0, [("ca", "c0")])
+        together("borders")
+        iota(T.ca[:, 5 * SPLIT:60:5], [[24, 12 - SPLIT]], 24 * SPLIT + 16, [("ca", "c1")])
+        together("borders")
 
     for t in range(R):
         def B(name):
@@ -321,86 +355,133 @@ def rank_program(g, core, T, topo):
 
         def both(m, have, by, cut=6):
             grow(act, m, have, by, 0, cut)
+            together(K("n%d_" % m))
             grow(cp, m, have, by, cut, 12)
+            together(K("n%d_" % m))
+
+        def alone(m, have, by, a=0):
+            grow(act, m, have, by, a, 12)
+            together(K("n%d_" % m))
 
         def turn_a(m, n=C):
             own(T.sc[:, 0:n], places(m, 1, n + 1), n, made(m), ["sc"])
 
-        def turn_b(m, n=C):
+        def turn_b(m, n=C, mate=None):
             ends(T["off%d" % m][:, 0:n // 16], T.sc, n, ["sc"], ["off%d" % m])
+            if mate:
+                together(K("n%d_" % mate))
 
-        def starts(call, m, on, n, r=(), w=()):
-            win, wk = table(m)
-            call(T.fl[:, 4 * m:4 * m + 16 * n], win.indirect(T[on][:, 0:n]), wk + [on] + list(r), [("fl", m)] + list(w))
+        def starts(call, m, on, n, by=None, a=0, w=()):
+            win, wk = table(by or m)
+            at = 4 * m + (16 if m >= 12 else 0)
+            call(T.fl[:, at:at + 16 * n], win.indirect(T[on][:, a:a + n]), wk + [on], [("fl", m)] + list(w))
 
         def first(m):
             src, rk = (T.n1[:, 2:12:3], [("n1", 0)]) if m == 1 else (places(m, 1, 5), made(m))
             cp(T.fl[:, 4 * m:4 * m + 4], src, rk, [("fl", m)])
 
-        def order(call, c, have):
-            call(T.ro[:, 16 * ne * c:16 * ne * (c + 1)], T.fl[:, 64 * c:64 * c + 64].indirect(T.roff[:, 0:ne]),
-                 [("fl", k) for k in have] + ["roff"], [("ro", c)])
-
         helper, guest = (rank + HOP[t]) % N, (rank - HOP[t]) % N
+        ahead = t > 0 and guest < rank and EU[0] >= 0
+        copies, planes = list(range(8)), list(range(4))
+
+        def unpack(n):
+            if n and len(copies) == 8:
+                for b in range(4):
+                    mm(2 + b, C, col(T.eq, b), col(T.es, b), B("gq")[:], B("gs")[:], [("eq", b), K("gq")])
+            for k in copies[:n]:
+                b = k // 2
+                out, on = (T.vh2[:, C * b:C * b + C], "vh2") if k % 2 else (T.vh[:, RG * b + 2:RG * b + 2 + C], "vh")
+                act(out, ps(2 + b, 0, C), [("ps", 2 + b)], [(on, b)], scale=0.5)
+                together(K("vh%d_" % b))
+            del copies[:n]
+
+        def pack():
+            for b in planes[:1]:
+                tt(T.fa[:, RG * b + 1:RG * b + 1 + C], T.vh[:, RG * b:RG * b + 2 + C].indirect(B("ll")[:]),
+                   T.vh2[:, C * b:C * b + C], ALU.add, [("vh", b), ("vh2", b), ("vh", 8), ("vh", 9), K("ll")], [("fa", b)])
+                together(K("fa"))
+            del planes[:1]
+
         tq, tsc = B("tq"), B("ts")
         quant(tq[:], tsc[:], B("t")[:], [K("t")], [K("tq")])
         send([helper], u8(B("gq")[:]), u8(tq[:]), K("aq"), [K("tq")])
         send([helper], B("gs")[:], tsc[:], K("aq"), [K("tq")])
         if t == 0:
             masks()
-        for k in (1, 0):
-            mm(k, C, col(T.upq, k), col(T.ups, k), tq[:], tsc[:], ["upq", "ups", K("tq")])
+        for k in (0, 1):
+            mm(k, C, col(T.upq, k), col(T.ups, k), tq[:], tsc[:], [("upq", k), ("ups", k), K("tq")])
         ts(T.zd[:, 0:576:3], ps(1, 0, C), 0.0, 0.25, ALU.is_gt, ALU.add, (), [("ps", 1), ("zd", 0)])
+        together(K("signs"))
         act(T.zd[:, 1:576:3], ps(0, 0, C), (), [("ps", 0), ("zd", 1)], ACT.Sign, bias=-1e-37)
+        together(K("signs"))
         if t == 0:
             more_masks()
         scan(T.so[:], T.zo[:], T.zd[:], ALU.mult, ALU.add, ["zd", "zo"], ["so"])
         scan(T.n1[:, 0:576], T.zc[:], T.zd[:], ALU.mult, ALU.add, ["zd", "zc"], [("n1", 0)])
+        together(K("n1_"))
         ts(T.off1[:, 12:24], T.so[:, 47:576:48], pf(8), -1.0, ALU.mult, ALU.add, ["so", ("pf", 8)], [("off1", 12)])
-        ts(B("loff")[:], T.so[:, 47:576:48], pf(3), float(C + 1), ALU.mult, ALU.min, ["so", ("pf", 3)], [K("loff")])
+        together(K("n1_"))
         ts(T.off1[:, 0:12], T.so[:, 47:576:48], pf(3), None, ALU.mult, None, ["so", ("pf", 3)], [("off1", 0)])
+        together(K("n2_"))
+        both(2, 1, 1)
+        ts(B("loff")[:], T.so[:, 47:576:48], pf(3), float(C + 1), ALU.mult, ALU.min, ["so", ("pf", 3)], [K("loff")])
         send([helper], B("ll")[:], B("loff")[:], K("al"), [K("loff")])
         if t == 0:
             dma("y", u8(T.wq[:]), T.wc[:], [K("loff")], ["wq"])
-            dma("y", T.wsc[:], T.ws[:], (), ["wsc"])
-            dma("y", T.vt[:], T.v[:], (), ["vt"])
+            borders()
+        if t == 1:
+            dma("y", T.vt[:], T.v[:], [K("loff")], ["vt"])
         arrive(K("aq"), 2 * width(guest), [K("gq")])
         arrive(K("al"), width(guest), [K("ll")])
         arrive(K("ac"), width(guest), [K("lc")])
-        both(2, 1, 1)
-        grow(act, 3, 2, 1, 0, 12)
+        alone(3, 2, 1)
         first(1)
+        together(K("fla"))
         fill(1)
         turn_a(2)
         first(2)
+        together(K("fla"))
         fill(1)
-        turn_b(2)
+        turn_b(2, C, 3)
         fill(1)
         both(5, 3, 2)
-        grow(act, 7, 5, 2, 0, 12)
+        alone(7, 5, 2)
+        cp(T.fl[:, 16:32], table(2)[0].indirect(T.off2[:, 0:1]), table(2)[1] + ["off2"],
+           [("fl", k) for k in (4, 5, 6, 7)])
+        together(K("fla"))
         first(3)
-        cp(T.fl[:, 16:32], table(2)[0].indirect(T.off2[:, 0:1]), table(2)[1] + ["off2"], [("fl", 4), ("fl", 5), ("fl", 7)])
+        together(K("fla"))
         turn_a(5)
-        own(T.sf[:, 0:32], T.fl[:, 0:32], 32, [("fl", k) for k in (0, 1, 2, 3, 4)], ["sf"])
-        fill(1)
-        turn_b(5)
+        first(5)
+        together(K("flb"))
+        cp(T.fl[:, 24:40], table(5)[0].indirect(T.off1[:, 0:1]), table(5)[1] + [("off1", 0)], [("fl", 6), ("fl", 7)])
+        together(K("flb"))
+        turn_b(5, C, 7)
+        fill(2)
+        own(T.sf[:, 0:32], T.fl[:, 0:32], 32, [("fl", k) for k in range(8)], ["sf"])
+        both(12, 7, 5)
+        unpack(EU[0] if ahead else 0)
+        alone(17, 12, 5)
+        unpack(EU[1] if ahead else 0)
         ends(T.ta[:], T.sf, 32, ["sf"], ["ta"])
         fill(1)
-        both(12, 7, 5)
-        grow(act, 17, 12, 5, 0, 12)
-        starts(cp, 5, "ta", 1, w=[("fl", 4), ("fl", 7)])
-        fill(1)
         turn_a(12)
-        starts(cp, 7, "ta", 2, w=[("fl", 4), ("fl", 12)])
-        fill(1)
-        turn_b(12)
-        own(T.sf[:], T.fl[:, 0:A], A, [("fl", k) for k in (0, 1, 2, 3, 4, 5, 7)], ["sf"])
-        fill(3)
+        starts(cp, 7, "ta", 2)
+        together(K("flc"))
+        starts(cp, 12, "ta", 2, w=[("fl", 17)])
+        together(K("flc"))
+        turn_b(12, C, 17)
+        fill(2)
+        own(T.sf[:], T.fl[:, 0:96], 96, [("fl", k) for k in (0, 1, 2, 3, 4, 5, 6, 7, 12)], ["sf"])
         last = rank == N - 1
         both(29, 17, 12, 6 if last else 8)
-        grow(act, 41, 29, 12, 0, 12)
-        ends(T.tb[:, 0:3], T.sf, A, ["sf"], ["tb"])
-        xn = K("exb" if rank == 1 else "exu")
+        if not last:
+            cp(T.x0[:], table(17)[0].indirect(T.off12[:, 0:1]), table(17)[1] + ["off12"], ["x0"])
+            together(K("n29_"))
+        unpack(EU[2] if ahead else 0)
+        if not last:
+            alone(41, 29, 12)
+        xn = K("exb" if rank == 1 or (rank == 2 and not VIA[t]) else "exu")
         ex, cand, cu = T[xn], B("cand"), B("cu")
 
         def jump(step):
@@ -415,7 +496,7 @@ def rank_program(g, core, T, topo):
                 ts(out[:, 0:16], win.indirect(src[:, 0:1]), add, None, ALU.add, None, wk + [on], [(nn, 0)])
                 if step == 3:
                     together(K("ex"))
-                    ts(out[:, 16:32], win.indirect(src[:, 0:1]), pf(6), None, ALU.add, None, wk + [on, ("pf", 6)], [(nn, 1)])
+                    ts(out[:, 16:32], win.indirect(src[:, 0:1]), 4.0, pf(6), ALU.mult, ALU.add, wk + [on, ("pf", 6)], [(nn, 1)])
                     together(K("ex"))
             elif step % 2 == 0:
                 a = 0 if step == 0 else 30
@@ -423,74 +504,68 @@ def rank_program(g, core, T, topo):
             else:
                 for h in range(2):
                     a = h if step == 1 else 2 + h
-                    ts(out[:, a:a + 64:2], win.indirect(src[:, 16 + 32 * h:18 + 32 * h]),
-                       pf(6) if step == 3 and rank == 2 else add, None, ALU.add, None, wk + [on, ("pf", 6)], [(nn, h)])
+                    two = win.indirect(src[:, 16 + 32 * h:18 + 32 * h])
+                    if step == 3 and rank == 2 and VIA[t]:
+                        ts(out[:, a:a + 64:2], two, 4.0, pf(6), ALU.mult, ALU.add, wk + [on, ("pf", 6)], [(nn, h)])
+                    else:
+                        ts(out[:, a:a + 64:2], two, add, None, ALU.add, None, wk + [on], [(nn, h)])
                     together(K("j%d_" % step))
 
-        if not last:
-            cp(T.x0[:], table(17)[0].indirect(T.off12[:, 0:1]), table(17)[1] + ["off12"], ["x0"])
-        starts(cp, 12, "tb", 2, w=[("fl", 7), ("fl", 17)])
+        ends(T.tb[:], T.sf, 96, ["sf"], ["tb"])
+        fill(9)
         jump(0)
-        starts(cp, 29, "tb", 3)
-        starts(cp, 17, "tb", 3, w=[("fl", 12)])
-        starts(act, 41, "tb", 2)
         if not last:
-            grow(act, 53, 41, 12, 8, 12)
-        order(act, 2, (29, 41))
+            together(K("n41_"))
+        starts(cp, 29, "tb", 3)
+        together(K("fld"))
+        starts(cp, 41, "tb", 2, 29, 4)
+        together(K("fld"))
+        starts(act, 17, "tb", 3, w=[("fl", 12)])
+        together(K("fld"))
+        if not last:
+            alone(53, 41, 12, 8)
+        unpack(8)
+        if last:
+            alone(41, 29, 12)
+            if ahead:
+                pack()
         jump(1)
-        order(cp, 0, (0, 1, 2, 3, 4, 5, 7, 12))
+        for e in range(ne):
+            scan(T.sr[:, 64 * e:64 * e + 52], T.me[:], T.fl[:, e:208:4], ALU.mult, ALU.max, ["fl", "me"], [("sr", e)])
+            together(K("sr"))
+        if last and ahead:
+            pack()
         jump(2)
-        order(cp, 1, (12, 17, 29))
+        if not last:
+            together(K("n53_"))
+        out, on = (cu[:, 0:3], K("cu")) if rank == 0 else (cand[:, 0:15], K("cand"))
+        ts(out, T.sr[:, 19:64 * ne:16], T.sq[:, 15:16], None, ALU.mult, None, ["sr", "sq"], [on])
         jump(3)
-        own(T.sr[:, 0:A * ne], T.ro[:, 0:A * ne], A * ne, ["ro"], ["sr"])
-        for b in range(4):
-            mm(2 + b, C, col(T.eq, b), col(T.es, b), B("gq")[:], B("gs")[:], [("eq", b), K("gq")])
-        if t == 0:
-            ms(T.vh[:, 0:4 * RG:RG], 0.0, [("vh", 8)])
-            ms(T.vh[:, 1:4 * RG:RG], 0.0, [("vh", 9)])
-        else:
+        if not last:
             turn_a(41, 112)
-        if rank == 0:
-            ends(cu[:, 0:3], T.sr, A, ["sr"], [K("cu")])
-        else:
-            ends(cand[:], T.sr, C, ["sr"], [K("cand")])
-        for b in range(4):
-            act(T.vh[:, RG * b + 2:RG * b + 2 + C], ps(2 + b, 0, C), [("ps", 2 + b)], [("vh", b)], scale=0.5)
-            together(K("vh%d_" % b))
-            act(T.vh2[:, C * b:C * b + C], ps(2 + b, 0, C), [("ps", 2 + b)], [("vh2", b)], scale=0.5)
-            together(K("vh%d_" % b))
         helpers = [r for r in range(N) if r != rank and (r - HOP[t]) % N > rank]
-        helpers.sort(key=lambda r: -((r - HOP[t]) % N))
+        helpers.sort(key=lambda r: ((r - HOP[t]) % N) * (SGN[t] if rank == 1 else SG0[t]))
         src = ex[:, 14:18] if rank == 0 else ex[:, 32:36]
         homes = [r for r in range(rank + 1, N) if r not in helpers]
-        if not last:
-            send(helpers + (homes if ORDER == 1 else []), B("lm%d_" % rank)[:], src, K("am%d_" % rank), [xn])
+        ORDER = ORD[t][rank]
+        if not last and ORDER != 1:
+            send(helpers, B("lm%d_" % rank)[:], src, K("am%d_" % rank), [xn])
         if rank == 0:
             send([helper], B("lu")[:, 0:3], cu[:, 0:3], K("ac"), [K("cu")])
         else:
             send([helper], B("lc")[:], cand[:], K("ac"), [K("cand")])
-        if not last and ORDER == 0:
-            send(homes, B("lm%d_" % rank)[:], src, K("am%d_" % rank), [xn])
+        if not last:
+            send((helpers if ORDER == 1 else []) + homes, B("lm%d_" % rank)[:], src, K("am%d_" % rank), [xn])
+        assert APART
 
-        def pack(b):
-            tt(T.fa[:, RG * b + 1:RG * b + 1 + C], T.vh[:, RG * b:RG * b + 2 + C].indirect(B("ll")[:]),
-               T.vh2[:, C * b:C * b + C], ALU.add, [("vh", b), ("vh2", b), ("vh", 8), ("vh", 9), K("ll")], [("fa", b)])
-            together(K("fa"))
-
-        if t == 0:
-            ms(T.nx[:], 200.0, ["nx"])
-            turn_a(41, 112)
-            ms(T.fa[:, 0:4 * RG:RG], 0.0, [("fa", 9)])
-            ms(T.ft[:, 4 * A:], 0.0, [("ft", 9)])
-            ms(T.ht[:, 4 * A:], 0.0, [("ht", 9)])
-        turn_b(41, 112)
-        pack(0)
-        grow(cp, 82, 41, 41, 0, 7)
-        pack(1)
-        grow(cp, 123, 82, 41, 0, 5)
-        pack(2)
-        grow(cp, 164, 123, 41, 0, 2)
-        pack(3)
+        pack()
+        if not last:
+            turn_b(41, 112)
+        if rank < guest:
+            grow(act, 82, 41, 41, 0, 7)
+            grow(act, 123, 82, 41, 0, 5)
+        for b in range(3):
+            pack()
         for r in range(max(rank, guest)):
             if r != rank:
                 arrive(K("am%d_" % r), width(r), [K("lm%d_" % r)])
@@ -505,95 +580,144 @@ def rank_program(g, core, T, topo):
             if r >= 2:
                 (win, wn), (v0, vn) = told(1), told(0, 0, 1)
                 if r == 2:
-                    ts(T[sel][:], win.indirect(v0), pf(5), None, ALU.add, None, [wn, vn, ("pf", 5)], [sel])
-                else:
+                    ts(T[sel][:], win.indirect(v0), 4.0, pf(5), ALU.mult, ALU.add, [wn, vn, ("pf", 5)], [sel])
+                elif VIA[t]:
                     ts(T[sel][:], win.indirect(v0), 16.0, pf(1), ALU.mult, ALU.add, [wn, vn, ("pf", 0)], [sel])
+                    together(K("via"))
                     cp(T.via[:], lists[:].indirect(told(2)[0]), [ln, told(2)[1]], ["via"])
+                    together(K("via"))
+                else:
+                    cp(T.ch[:], win.indirect(v0), [wn, vn], ["ch"])
+                    ts(T[sel][:], told(2)[0].indirect(T.ch[:, 0:1]), 4.0, pf(5), ALU.mult, ALU.add,
+                       [told(2)[1], "ch", ("pf", 5)], [sel])
 
         def pick(r, lists, ln, sel, out):
             if r == 1:
                 cp(T[out][:], lists[:].indirect(told(0, 2, 1)[0]), [ln, told(0)[1]], [out])
-            elif r == 2:
-                cp(T[out][:], lists[:].indirect(T[sel][:, 0:1]), [ln, sel], [out])
-            elif r == 3:
+            elif r == 3 and VIA[t]:
                 cp(T[out][:], T.via[:].indirect(T[sel][:, 0:1]), ["via", sel], [out])
+            elif r >= 2:
+                cp(T[out][:], lists[:].indirect(T[sel][:, 0:1]), [ln, sel], [out])
 
         goff, gn = (T.goff, "goff") if guest > 0 else (B("lu"), K("lc"))
         soff, sn = (T.soff, "soff") if rank > 0 else (cu, K("cu"))
 
-        def blocks():
+        def shared():
             ts(T.sofb[:, 0:1], soff[:, 0:1], pf(7), None, ALU.max, None, [sn, ("pf", 7)], [("sofb", 0)])
             together(K("sofb"))
             cp(T.sofb[:, 1:3], soff[:, 1:3], [sn], [("sofb", 1)])
             together(K("sofb"))
 
-        choose(guest, B("lc"), K("lc"), "gsel")
-        if rank < guest:
-            choose(rank, cand, K("cand"), "osel")
-        pick(guest, B("lc"), K("lc"), "gsel", "goff")
-        if rank < guest:
-            pick(rank, cand, K("cand"), "osel", "soff")
-        for b in range(4):
-            src = T.fa[:, RG * b:RG * b + 1 + C].indirect(goff[:, 0:3])
-            (cp if b % 2 == 0 else act)(T.ft[:, b:4 * A:4], src, [("fa", b), ("fa", 9), gn], [("ft", b)])
-            together(K("ft%d_" % (b % 2)))
-        if rank < guest:
-            blocks()
-        quant(T.fq[:], T.fs[:], T.ft[:], ["ft"], ["fq"])
-        for b in range(4):
-            mm(2 + b, 128, col(T.wq, b), col(T.wsc, b), T.fq[:], T.fs[:], ["wq", "wsc", "fq"])
-        if rank > guest:
-            choose(rank, cand, K("cand"), "osel")
-            pick(rank, cand, K("cand"), "osel", "soff")
-        elif t == 0:
-            count_constants()
-        for b in range(4):
-            ts(T.ht[:, b:4 * A:4], ps(2 + b, 0, A), 0.03125, None, ALU.mult, None, (), [("ps", 2 + b), ("ht", b)])
-            together(K("ht"))
-        if rank > guest:
-            blocks()
-        for m in range(5):
-            win, wk = table(STEP * m)
-            offs, on = (soff, sn) if m == 0 else (T.sofb, "sofb")
-            act(T.sb[:, A * m:A * m + A], win.indirect(offs[:, 0:3]), wk + [on], [("sb", m)])
-            together(K("sb%d_" % (m // 3)))
-        quant(B("hq")[:], B("hs")[:], T.ht[:], ["ht"], [K("hq")])
-        land = A * (R - 1 - t)
-        send([guest], u8(T.lq[:, land:land + A]), u8(B("hq")[:, 0:A]), K("ah"), [K("hq")])
-        send([guest], T.ls[:, land:land + A], B("hs")[:, 0:A], K("ah"), [K("hq")])
+        def blocks():
+            for m in range(5):
+                win, wk = table(STEP * m)
+                offs, on = (soff, sn) if m == 0 else (T.sofb, "sofb")
+                mine = m < 3 if rank == 0 else m in (1, 2) and rank > guest
+                (cp if mine else act)(T.sb[:, A * m:A * m + A], win.indirect(offs[:, 0:3]), wk + [on], [("sb", m)])
+                if m > 0:
+                    together(K("sb%d_" % (0 if m < 3 else 1)))
 
         def span(c):
             return 4 * c, 20 * c + 16, 8 * c * (c + 1), [("sb", i) for i in range((20 * c + 15) // A + 1)] + ["jb"]
 
-        if t == 0 and rank > guest:
-            count_constants()
-        for c in range(SPLIT, 12):
-            lo, hi, at, rk = span(c)
-            act(T.junk[:, at:at + hi - lo], T.sb[:, lo:hi], rk, [("ca", c), ("junk", c)], ACT.Sign,
-                bias=T.jb[:, c:c + 1], scale=-1.0, accum_out=T.ca[:, 5 * c + 4:5 * c + 5])
-            together(K("count"))
-        for c in range(SPLIT):
-            lo, hi, at, rk = span(c)
-            ts(T.junk[:, at:at + hi - lo], T.sb[:, lo:hi], T.jb[:, c:c + 1], 2.0, ALU.is_lt, ALU.mult, rk, [("junk", c)])
-            together(K("less"))
-        for m in range(1, 4):
-            at = m * (2 * A - STEP)
-            ts(T.ca[:, m:60:5], T.jb[:], T.sb[:, at:at + 1], -96.0, ALU.is_gt, ALU.mult, ["jb", ("sb", m)], [("ca", "m%d" % m)])
-            together(K("sums"))
-        for c in range(SPLIT):
-            lo, hi, at, rk = span(c)
-            op("v", lambda c=c, lo=lo, hi=hi, at=at: V.tensor_reduce(
-                T.ca[:, 5 * c + 4:5 * c + 5], T.junk[:, at:at + hi - lo], AxisListType.X, ALU.add), [("junk", c)], [("ca", c)])
-            together(K("sums"))
-        if t == 0:
-            ms(T.zt[:], 0.0, ["zt"])
-            ms(T.hw[:, 0:256:64], 0.0, [("hw", 9)])
-        if t == 1:
-            quant(T.vq[:], T.vs[:], T.vt[:], ["vt"], ["vq"])
-        scan(T.cs[:], T.cr[:], T.ca[:], ALU.mult, ALU.add, ["cr", "ca"], ["cs"])
+        def count_scalar():
+            for c in range(SPLIT, 12):
+                lo, hi, at, rk = span(c)
+                act(T.junk[:, at:at + hi - lo], T.sb[:, lo:hi], rk, [("ca", c), ("junk", c)], ACT.Sign,
+                    bias=T.jb[:, c:c + 1], scale=-1.0, accum_out=T.ca[:, 5 * c + 4:5 * c + 5])
+                together(K("sums"))
+
+        def count_compare():
+            for c in range(SPLIT):
+                lo, hi, at, rk = span(c)
+                ts(T.junk[:, at:at + hi - lo], T.sb[:, lo:hi], T.jb[:, c:c + 1], 2.0, ALU.is_lt, ALU.mult, rk, [("junk", c)])
+                together(K("less"))
+            for m in range(1, 4):
+                at = m * (2 * A - STEP)
+                ts(T.ca[:, m:60:5], T.jb[:], T.sb[:, at:at + 1], -96.0, ALU.is_gt, ALU.mult, ["jb", ("sb", m)],
+                   [("ca", "m%d" % m)])
+                together(K("sums"))
+
+        def count_add(cs):
+            for c in cs:
+                lo, hi, at, rk = span(c)
+                op("v", lambda c=c, lo=lo, hi=hi, at=at: V.tensor_reduce(
+                    T.ca[:, 5 * c + 4:5 * c + 5], T.junk[:, at:at + hi - lo], AxisListType.X, ALU.add),
+                   [("junk", c)], [("ca", c)])
+                together(K("sums"))
+
+        if rank == 0:
+            shared()
+            grow(act, 164, 123, 41, 0, 2)
+            blocks()
         if t == 0:
             quant(T.lq[:, R * A:], T.ls[:, R * A:], T.zt[:], ["zt"], [("lq", "pad")])
+        choose(guest, B("lc"), K("lc"), "gsel")
+        if rank < guest:
+            choose(rank, cand, K("cand"), "osel")
+        pick(guest, B("lc"), K("lc"), "gsel", "goff")
+        if guest > 0:
+            together(K("fa"))
+        if last:
+            turn_a(41, 112)
+        for b in range(4):
+            src = T.fa[:, RG * b:RG * b + 1 + C].indirect(goff[:, 0:3])
+            (cp if b % 2 == 0 else act)(T.ft[:, b:4 * A:4], src, [("fa", b), ("fa", 9), gn], [("ft", b)])
+            together(K("ft"))
+        if last:
+            turn_b(41, 112)
+        if rank > guest:
+            grow(act, 82, 41, 41, 0, 7)
+            grow(act, 123, 82, 41, 0, 5)
+        if rank > 0:
+            grow(act, 164, 123, 41, 0, 2)
+        if rank < guest:
+            pick(rank, cand, K("cand"), "osel", "soff")
+        quant(T.fq[:], T.fs[:], T.ft[:], ["ft"], ["fq"])
+        if rank == 0:
+            count_scalar()
+            count_compare()
+        elif rank < guest:
+            shared()
+            blocks()
+        for b in range(4):
+            mm(2 + b, 128, col(T.wq, b), col(T.wsc, b), T.fq[:], T.fs[:], ["wq", "wsc", "fq"])
+        if rank > guest and EARLY >= 2:
+            choose(rank, cand, K("cand"), "osel")
+        if rank > guest and EARLY == 3:
+            pick(rank, cand, K("cand"), "osel", "soff")
+        for b in range(4):
+            ts(T.ht[:, b:4 * A:4], ps(2 + b, 0, A), 0.03125, None, ALU.mult, None, (), [("ps", 2 + b), ("ht", b)])
+            together(K("ht"))
+        if rank > guest and EARLY == 1:
+            choose(rank, cand, K("cand"), "osel")
+        if rank > guest and EARLY == 2:
+            pick(rank, cand, K("cand"), "osel", "soff")
+        if rank > guest and EARLY == 3:
+            shared()
+        if rank == 0:
+            count_add(range(3))
+        quant(B("hq")[:], B("hs")[:], T.ht[:], ["ht"], [K("hq")])
+        if rank > guest:
+            if EARLY == 0:
+                choose(rank, cand, K("cand"), "osel")
+            if EARLY < 2:
+                pick(rank, cand, K("cand"), "osel", "soff")
+            if EARLY < 3:
+                shared()
+            blocks()
+        land = A * (R - 1 - t)
+        send([guest], u8(T.lq[:, land:land + A]), u8(B("hq")[:, 0:A]), K("ah"), [K("hq")])
+        send([guest], T.ls[:, land:land + A], B("hs")[:, 0:A], K("ah"), [K("hq")])
+        if rank > 0:
+            count_scalar()
+            count_compare()
+        count_add(range(3 if rank == 0 else 0, SPLIT))
+        scan(T.cs[:], T.cr[:], T.ca[:], ALU.mult, ALU.add, ["cr", "ca"], ["cs"])
+        if t == 1:
+            quant(T.vq[:], T.vs[:], T.vt[:], ["vt"], ["vq"])
         ts(T.koff[:], T.cs[:, 4:60:5], 0.5, None, ALU.mult, None, ["cs"], ["koff"])
+        together(K("hw"))
         if t == R - 1:
             act(T.olf[:], T.sb[:, 0:A], [("sb", 0)], ["olf"], ACT.Identity, bias=-1.0)
             dma("y", T.ol[:], T.olf[0:128:16, :], ["olf"], ())
@@ -604,6 +728,8 @@ def rank_program(g, core, T, topo):
                [("eq", b), ("lq", "pad")] + [("lq", k) for k in range(t + 1)])
         for b in range(4):
             (cp if b == 0 else act)(T.hw[:, 64 * b + 1:64 * b + 1 + A], ps(banks[b], 0, A), (), [("ps", banks[b]), ("hw", b)])
+            if b == 0:
+                together(K("hw"))
         new = "t%d" % (t + 1)
         for b in range(4):
             tt(T[new][:, b:4 * C:4], T.hw[:, 64 * b:64 * b + 1 + A].indirect(T.koff[:]), B("t")[:, b:4 * C:4], ALU.add,

from concourse.bass import DstId, RemoteDMATransfer
from concourse.mybir import dt, AluOpType, ActivationFunctionType, AxisListType

ALU = AluOpType
ACT = ActivationFunctionType
N, C, A, R = 4, 192, 48, 3
HOP = [1, 2, 3]
RG = 208
NEAR = [0, 2, 3, 5, 7, 12, 17, 29, 41, 53]
FAR = [82, 123, 164]
STEP = 41
SPLIT = 6
ORD = [[1, 1, 1, 1], [1, 1, 1, 1], [1, 1, 1, 1]]
EU = [-1, 0, 0]
VIA = [1, 0, 0]
SGN = [1, 1, 1]
SG0 = [1, 1, -1]
CC = 0
APART = 1
EARLY = 1
X4, U8 = "float8_e4m3fn_x4", "uint8"
BF, F32, U16 = "bfloat16", "float32", "uint16"

SCRATCH = {"ps": ("psum", [128, 4096], F32)}
for _n, _w, _d in [
        ("ut", 512, BF), ("vt", 512, BF), ("uq", 128, X4), ("us", 128, U8), ("upq", 256, X4), ("ups", 256, U8),
        ("vq", 128, X4), ("vs", 128, U8), ("wq", 512, X4), ("wsc", 512, U8), ("fq", 128, X4), ("fs", 128, U8),
        ("eall", 516, BF), ("eq", 512, X4), ("es", 512, U8), ("zt", 512, BF), ("ft", 512, BF), ("ht", 512, BF),
        ("jm", C, BF), ("pi", 2, "int32"), ("pf", 14, F32), ("md", C, BF), ("oh", 32, BF),
        ("sq", 16, F32), ("zd", 576, BF), ("zc", 576, BF), ("zo", 576, BF), ("so", 576, BF), ("n1", 592, BF),
        ("nw", RG * len(NEAR), BF), ("nx", RG * len(FAR), BF), ("fl", 240, BF), ("sf", 96, BF),
        ("sc", C, BF), ("me", 52, BF), ("sr", 256, BF), ("vh2", 4 * C, BF), ("via", 64, BF),
        ("uoff", 16, U16), ("off1", 24, U16), ("off2", 12, U16), ("off5", 12, U16), ("off12", 12, U16),
        ("off41", 8, U16), ("ta", 2, U16), ("tb", 6, U16),
        ("x0", 16, U16), ("x1", 66, U16), ("x2", 66, U16), ("x3", 66, U16),
        ("ch", 16, U16), ("osel", 16, U16), ("gsel", 16, U16), ("soff", 16, U16), ("sofb", 4, U16), ("goff", 16, U16),
        ("koff", 12, U16), ("lq", 272, X4), ("ls", 272, U8),
        ("sb", 5 * A, BF), ("olf", A, F32), ("junk", 1248, BF), ("jb", 12, F32),
        ("ca", 60, F32), ("cr", 60, F32), ("cs", 60, F32),
        ("vh", 4 * RG, BF), ("fa", 4 * RG, BF), ("hw", 256, BF), ("yt", 192, F32)]:
    SCRATCH[_n] = ("sbuf", [128, _w], _d)
for _t in range(R + 1):
    for _n, _w, _d in [("t", 768, BF), ("tq", C, X4), ("ts", C, U8)]:
        SCRATCH["%s%d" % (_n, _t)] = ("sbuf", [128, _w], _d)
for _t in range(R):
    for _n, _w, _d in [("hq", 128, X4), ("hs", 128, U8), ("gq", C, X4), ("gs", C, U8),
                       ("exb", 68, BF), ("exu", 68, U16), ("loff", 12, U16), ("ll", 12, U16),
                       ("cand", 15, BF), ("lc", 15, BF), ("cu", 4, U16), ("lu", 4, U16),
                       ("lm0_", 4, U16), ("lm1_", 4, BF), ("lm2_", 4, U16 if VIA[_t] else BF)]:
        SCRATCH["%s%d" % (_n, _t)] = ("sbuf", [128, _w], _d)

POOL = {"v": ["v%d" % i for i in range(60)], "s": ["s%d" % i for i in range(28)],
        "t": ["t%d" % i for i in range(18)], "g": ["g%d" % i for i in range(4)],
        "d": ["d%d" % i for i in range(14)]}
SEMAPHORES = ([n for k in "vstgd" for n in POOL[k]] + ["sent"]
              + ["%s%d" % (n, t) for t in range(R) for n in ("aq", "al", "ac", "ah", "am0_", "am1_", "am2_")])


def clash(a, b):
    return a[0] == b[0] and (a[1] is None or b[1] is None or a[1] == b[1])


def keys(xs):
    return [x if isinstance(x, tuple) else (x, None) for x in xs]


def emit(g, T, ops, sent):
    queues = {"v": g.vector, "s": g.scalar, "t": g.tensor, "g": g, "y": g.sync}
    known = {q: set() for q in queues}
    groups = {}
    for n, o in enumerate(ops):
        if o.get("grp"):
            groups.setdefault(o["grp"], []).append(n)
    for n, o in enumerate(ops):
        if o["q"] is None:
            o["known"] = set()
            continue
        deps = set()
        for m in range(n):
            p = ops[m]
            if p["kind"] == "remote" or m in known[o["q"]]:
                continue
            if (any(clash(a, b) for a in o["r"] + o["w"] for b in p["w"])
                    or any(clash(a, b) for a in o["w"] for b in p["r"])):
                deps.add(m)
        deps = {m for m in deps if not any(m in ops[k]["known"] for k in deps)}
        for m in list(deps):
            if ops[m].get("grp"):
                assert groups[ops[m]["grp"]][-1] < n
                deps |= set(groups[ops[m]["grp"]])
        o["waits"] = sorted(deps)
        for m in deps:
            ops[m]["need"] = True
            known[o["q"]] |= {m} | ops[m]["known"]
        o["known"] = set(known[o["q"]])
    last = {}
    tail = []
    for n, o in enumerate(ops):
        if o["q"] is None:
            if not o.get("need"):
                tail.append(o["sig"])
            continue
        q = queues[o["q"]]
        done = []
        for m in o["waits"]:
            if ops[m]["sig"] not in done:
                done.append(ops[m]["sig"])
                q.wait_ge(T.sem[ops[m]["sig"][0]], ops[m]["sig"][1])
        ins = o["fn"]()
        if o["kind"] == "remote":
            continue
        if o["kind"] == "dma":
            name = [s for s in POOL["d"] if s not in last][0]
            last[name] = n
            o["sig"] = (name, 16)
            ins.then_inc(T.sem[name], 16)
            if not o.get("need"):
                tail.append(o["sig"])
        elif o.get("need"):
            if "sig" not in o:
                mates = groups[o["grp"]] if o.get("grp") else [n]
                name = [s for s in POOL[o["q"]] if s not in last or all(last[s] in ops[m]["known"] for m in mates)][0]
                sig = (name, (ops[last[name]]["sig"][1] if name in last else 0) + len(mates))
                last[name] = mates[-1]
                for m in mates:
                    ops[m]["sig"] = sig
            ins.then_inc(T.sem[o["sig"][0]], 1)
    tail.insert(0, ("sent", sent[0]))
    for name, val in tail:
        g.wait_ge(T.sem[name], val)


def rank_program(g, core, T, topo):
    rank = T.rank_of(core)
    if rank is None:
        return
    ops = []
    sent = [0]
    V, S, PE = g.vector, g.scalar, g.tensor
    sem = T.sem

    def op(q, fn, r=(), w=(), kind="compute"):
        ops.append({"q": q, "fn": fn, "r": keys(r), "w": keys(w), "kind": kind})

    def together(name):
        ops[-1]["grp"] = name

    def arrive(name, val, w):
        ops.append({"q": None, "r": [], "w": keys(w), "kind": "arrive", "sig": (name, val)})

    def ts(out, in0, s1, s2, o0, o1, r, w):
        if o1 is None:
            op("v", lambda: V.tensor_scalar(out, in0, s1, None, o0), r, w)
        else:
            op("v", lambda: V.tensor_scalar(out, in0, s1, s2, o0, o1), r, w)

    def tt(out, a, b, o, r, w):
        op("v", lambda: V.tensor_tensor(out, a, b, o), r, w)

    def cp(out, a, r, w):
        op("v", lambda: V.tensor_copy(out, a), r, w)

    def ms(out, c, w):
        op("v", lambda: V.memset(out, c), (), w)

    def scan(out, d0, d1, o0, o1, r, w):
        op("v", lambda: V.tensor_tensor_scan(out, d0, d1, 0.0, o0, o1), r, w)

    def act(out, a, r, w, func=ACT.Copy, **how):
        op("s", lambda: S.activation(out, a, func, **how), r, w)

    def quant(q, s, a, r, w):
        op("v", lambda: V.quantize_mx(q, s, a), r, w)

    def mm(bank, n, lq, ls, rq, rs, r):
        op("t", lambda: PE.matmul_mx(T.ps[:, 512 * bank:512 * bank + n], lq, ls, rq, rs, True, True), r, [("ps", bank)])

    def dma(q, out, a, r, w):
        e = {"y": g.sync, "s": S}[q]
        op(q, lambda: e.dma_start(out, a), r, w, "dma")

    def iota(out, pattern, base, w):
        op("g", lambda: g.iota(out, pattern, base, 0, allow_small_or_imprecise_dtypes=True), (), w)

    def send(to, out, a, name, r):
        if not to:
            return
        dst = [T.cores[k] for k in to]
        sent[0] += len(topo.engines(core, dst[0]))
        if len(dst) == 1:
            rid, pid = topo.addr(dst[0])[:2]
            op("g", lambda: g.remote_dma(out, a, sem[name], sem.sent, pid, rid, topo.mask(core, dst[0])), r, (), "remote")
        else:
            tr = RemoteDMATransfer(dst_ids=[DstId(rid=topo.addr(c)[0], pnc=topo.addr(c)[1]) for c in dst],
                                   dma_engine_mask=topo.mask(core, dst[0]), remote_sem=sem[name], srcs=[a],
                                   dsts=[out for c in dst])
            op("g", lambda: g.remote_dma_fused([tr], local_sem=sem.sent), r, (), "remote")

    def width(frm):
        return len(topo.engines(T.cores[frm], core))

    def ps(bank, a, b):
        return T.ps[:, 512 * bank + a:512 * bank + b]

    def u8(v):
        return v.bitcast(dt.uint8)

    def col(q, b):
        return q[:, 128 * b:128 * b + 128]

    def pf(k):
        return T.pf[:, k:k + 1]

    def home(m):
        return (T.nw, "nw", RG * NEAR.index(m)) if m in NEAR else (T.nx, "nx", RG * FAR.index(m))

    def made(m):
        return [(home(m)[1], "a%d" % m), (home(m)[1], "b%d" % m)]

    def table(m, first=0):
        if m == 1:
            return T.n1[:], ["n1"]
        buf, name, at = home(m)
        return buf[:, at + first:at + C + 5], made(m) + [(name, "stay")]

    def places(m, a, b):
        buf, name, at = home(m)
        return buf[:, at + a:at + b]

    def grow(call, m, have, by, a, b):
        win, wk = table(have)
        at = 12 if have == 1 else 0
        call(places(m, 16 * a + 1, 16 * b + 1), win.indirect(T["off%d" % by][:, at + a:at + b]),
             wk + [("off%d" % by, at)], [made(m)[0 if call is act else 1]])

    def own(out, src, n, r, w):
        scan(out, T.md[:, 0:n], src, ALU.mult, ALU.max, r + ["md"], w)

    def ends(out, src, n, r, w):
        ts(out, src[:, 15:n:16], T.sq[:, 15:16], None, ALU.mult, None, r + ["sq"], w)

    ne = 1 if rank == 0 else 4

    dma("y", T.ut[:], T.u[:], (), ["ut"])
    dma("y", T.t0[:], T.x[:], (), ["t0"])

    op("g", lambda: g.iota(T.pi[:, 0:1], [[0, 1]], 0, 1), (), [("pi", 0)])
    iota(T.jm[:], [[0, 12], [1, 16]], 0, ["jm"])
    iota(T.nw[:, 0:C + 5], [[1, C + 5]], 0, [("nw", "a0")])
    ms(T.eall[:], 0.0, ["eall"])
    ms(T.n1[:, 576:592], 0.0, [("n1", 1)])
    ts(T.pi[:, 1:2], T.pi[:, 0:1], 15, None, ALU.bitwise_and, None, [("pi", 0)], [("pi", 1)])
    for k, c in enumerate((0.0, 4.0, 0.5)):
        ms(T.zc[:, k:576:3], c, [("zc", k)])
        together("zc")
    cp(T.pf[:, 0:2], T.pi[:], ["pi"], [("pf", 0)])
    for p in (0, C + 1, C + 2, C + 3, C + 4):
        ms(T.nw[:, RG + p::RG], float(p), [("nw", "stay%d" % p)])
        together("stay")
    ts(pf(9), pf(1), 1.0, None, ALU.add, None, [("pf", 0)], [("pf", 9)])
    ms(places(53, 128, 129), 0.0, [("nw", "stay")])
    together("stay")
    ts(T.uoff[:, 0:8], T.jm[:, 0:8], 16.0, None, ALU.mult, None, ["jm"], [("uoff", 0)])
    together("uoff")
    ts(T.uoff[:, 8:16], T.jm[:, 0:8], 16.0, 1.0, ALU.mult, ALU.add, ["jm"], [("uoff", 1)])
    together("uoff")
    ts(T.sc[:], T.jm[:], pf(1), None, ALU.not_equal, None, ["jm", ("pf", 0)], ["sc"])
    ts(pf(3), pf(1), 15.0, 2.0 ** -30, ALU.is_equal, ALU.max, [("pf", 0)], [("pf", 3)])
    ts(T.sr[:, 0:C], T.jm[:], pf(9), 2.0 ** 30, ALU.is_equal, ALU.mult, ["jm", ("pf", 9)], ["sr"])
    ts(pf(5), pf(1), 2.0, None, ALU.min, None, [("pf", 0)], [("pf", 5)])
    together("pf")
    ts(pf(6), pf(1), 2.0, -4.0 * (C + 1), ALU.min, ALU.add, [("pf", 0)], [("pf", 6)])
    together("pf")
    ms(T.me[:, 13:16], 1.0, [("me", 1)])
    together("pf")
    ms(T.me[:, 12:13], 256.0, [("me", 3)])
    together("pf")
    iota(T.nx[:], [[0, RG * len(FAR)]], 200, ["nx"])
    act(T.zt[:], T.eall[:, 0:512], ["eall"], ["zt"])
    quant(T.uq[:], T.us[:], T.ut[:], ["ut"], ["uq"])
    act(T.zd[:, 2:576:3], T.nw[:, 0:C], [("nw", "a0")], [("zd", 2)], ACT.Identity, bias=2.0)
    ts(T.oh[:, 0:16], T.jm[:, 0:16], pf(1), None, ALU.is_equal, None, ["jm", ("pf", 0)], [("oh", 0)])
    together("sq")
    ts(T.oh[:, 16:32], T.jm[:, 0:16], pf(1), 2.0 ** -8, ALU.not_equal, ALU.mult, ["jm", ("pf", 0)], [("oh", 1)])
    together("sq")
    ts(pf(8), pf(3), 3.0, None, ALU.mult, None, [("pf", 3)], [("pf", 8)])
    ts(pf(2), pf(1), 1.5, None, ALU.add, None, [("pf", 0)], [("pf", 2)])

    def u_pick(k):
        offs = T.uoff[:, 8 * k:8 * k + 8]
        cp(col(T.upq, k).bitcast(dt.uint32), T.uq[:].bitcast(dt.uint32).indirect(offs), ["uq", "uoff"], [("upq", k)])
        together("up%d" % k)
        act(col(T.ups, k), T.us[:].indirect(offs), ["uq", "uoff"], [("ups", k)])
        together("up%d" % k)

    u_pick(0)

    def masks():
        u_pick(1)
        act(T.zo[:, 1:576:3], T.sc[:], ["sc"], [("zo", 1)], ACT.Identity, scale=-3.0, bias=4.0)
        together("zo")
        act(T.zo[:, 2:576:3], T.sc[:], ["sc"], [("zo", 2)], ACT.Identity, scale=0.5, bias=0.5)
        together("zo")
        dma("s", T.wsc[:], T.ws[:], ["t0"], ["wsc"])
        tt(T.zo[:, 0:576:3], T.sc[:], T.sr[:, 0:C], ALU.max, ["sc", "sr"], [("zo", 0)])
        cp(T.n1[:, 578:590:3], T.nw[:, C + 1:C + 5], [("nw", "a0")], [("n1", 1)])
        ms(T.fl[:], 1.0, ["fl"])

    def more_masks():
        ts(T.md[:], T.sc[:], 256.0, None, ALU.mult, None, ["sc"], ["md"])
        scan(T.sq[:], T.oh[:, 16:32], T.oh[:, 0:16], ALU.mult, ALU.add, ["oh"], ["sq"])
        cp(T.fl[:, 0:4], T.nw[:, 1:5], [("nw", "a0")], [("fl", 0)])

    def e_tile(b):
        quant(col(T.eq, b), col(T.es, b), T.eall[:, 3 - b:515 - b], ["eall"], [("eq", b)])

    later = [
        lambda: ts(T.eall[:, 3:515:4], T.nw[:, 0:128], pf(0), None, ALU.is_equal, None, [("nw", "a0"), ("pf", 0)], ["eall"]),
        lambda: cp(T.me[:, 0:12], T.md[:, 0:12], ["md"], [("me", 0)]),
        lambda: e_tile(0),
        lambda: e_tile(1),
        lambda: cp(T.me[:, 17:52], T.md[:, 13:48], ["md"], [("me", 2)]),
        lambda: e_tile(2),
        lambda: e_tile(3),
        lambda: ts(T.me[:, 16:17], T.md[:, 12:13], 2.0 ** -8, None, ALU.mult, None, ["md"], [("me", 4)]),
        lambda: ts(pf(7), pf(1), float(A - STEP), float(C + 1), ALU.is_lt, ALU.mult, [("pf", 0)], [("pf", 7)]),
        lambda: ts(T.jb[:], T.jm[:, 0:12], 16.0, pf(2), ALU.mult, ALU.add, ["jm", ("pf", 2)], ["jb"]),
    ]

    def fill(n):
        for k in range(min(n, len(later))):
            later.pop(0)()

    def borders():
        for out, n, on in [(T.vh[:, 0:4 * RG:RG], 4, ("vh", 8)), (T.vh[:, 1:4 * RG:RG], 4, ("vh", 9)),
                           (T.fa[:, 0:4 * RG:RG], 4, ("fa", 9)), (T.ft[:, 4 * A:], 320, ("ft", 9)),
                           (T.ht[:, 4 * A:], 320, ("ht", 9)), (T.hw[:, 0:256:64], 4, ("hw", 9)),
                           (T.cr[:, 0:60:5], 12, ("cr", 0))]:
            iota(out, [[0, n]], 0, [on])
            together("borders")
        for k in range(1, 5):
            iota(T.cr[:, k:60:5], [[0, 12]], 1, [("cr", k)])
            together("borders")
        iota(T.ca[:, 0:5 * SPLIT:5], [[8, SPLIT]], 0, [("ca", "c0")])
        together("borders")
        iota(T.ca[:, 5 * SPLIT:60:5], [[24, 12 - SPLIT]], 24 * SPLIT + 16, [("ca", "c1")])
        together("borders")

    for t in range(R):
        def B(name):
            return T["%s%d" % (name, t)]

        def K(name):
            return "%s%d" % (name, t)

        def both(m, have, by, cut=6):
            grow(act, m, have, by, 0, cut)
            together(K("n%d_" % m))
            grow(cp, m, have, by, cut, 12)
            together(K("n%d_" % m))

        def alone(m, have, by, a=0):
            grow(act, m, have, by, a, 12)
            together(K("n%d_" % m))

        def turn_a(m, n=C):
            own(T.sc[:, 0:n], places(m, 1, n + 1), n, made(m), ["sc"])

        def turn_b(m, n=C, mate=None):
            ends(T["off%d" % m][:, 0:n // 16], T.sc, n, ["sc"], ["off%d" % m])
            if mate:
                together(K("n%d_" % mate))

        def starts(call, m, on, n, by=None, a=0, w=()):
            win, wk = table(by or m)
            at = 4 * m + (16 if m >= 12 else 0)
            call(T.fl[:, at:at + 16 * n], win.indirect(T[on][:, a:a + n]), wk + [on], [("fl", m)] + list(w))

        def first(m):
            src, rk = (T.n1[:, 2:12:3], [("n1", 0)]) if m == 1 else (places(m, 1, 5), made(m))
            cp(T.fl[:, 4 * m:4 * m + 4], src, rk, [("fl", m)])

        helper, guest = (rank + HOP[t]) % N, (rank - HOP[t]) % N
        ahead = t > 0 and guest < rank and EU[0] >= 0
        copies, planes = list(range(8)), list(range(4))

        def unpack(n):
            if n and len(copies) == 8:
                for b in range(4):
                    mm(2 + b, C, col(T.eq, b), col(T.es, b), B("gq")[:], B("gs")[:], [("eq", b), K("gq")])
            for k in copies[:n]:
                b = k // 2
                out, on = (T.vh2[:, C * b:C * b + C], "vh2") if k % 2 else (T.vh[:, RG * b + 2:RG * b + 2 + C], "vh")
                act(out, ps(2 + b, 0, C), [("ps", 2 + b)], [(on, b)], scale=0.5)
                together(K("vh%d_" % b))
            del copies[:n]

        def pack():
            for b in planes[:1]:
                tt(T.fa[:, RG * b + 1:RG * b + 1 + C], T.vh[:, RG * b:RG * b + 2 + C].indirect(B("ll")[:]),
                   T.vh2[:, C * b:C * b + C], ALU.add, [("vh", b), ("vh2", b), ("vh", 8), ("vh", 9), K("ll")], [("fa", b)])
                together(K("fa"))
            del planes[:1]

        tq, tsc = B("tq"), B("ts")
        quant(tq[:], tsc[:], B("t")[:], [K("t")], [K("tq")])
        send([helper], u8(B("gq")[:]), u8(tq[:]), K("aq"), [K("tq")])
        send([helper], B("gs")[:], tsc[:], K("aq"), [K("tq")])
        if t == 0:
            masks()
        for k in (0, 1):
            mm(k, C, col(T.upq, k), col(T.ups, k), tq[:], tsc[:], [("upq", k), ("ups", k), K("tq")])
        ts(T.zd[:, 0:576:3], ps(1, 0, C), 0.0, 0.25, ALU.is_gt, ALU.add, (), [("ps", 1), ("zd", 0)])
        together(K("signs"))
        act(T.zd[:, 1:576:3], ps(0, 0, C), (), [("ps", 0), ("zd", 1)], ACT.Sign, bias=-1e-37)
        together(K("signs"))
        if t == 0:
            more_masks()
        scan(T.so[:], T.zo[:], T.zd[:], ALU.mult, ALU.add, ["zd", "zo"], ["so"])
        scan(T.n1[:, 0:576], T.zc[:], T.zd[:], ALU.mult, ALU.add, ["zd", "zc"], [("n1", 0)])
        together(K("n1_"))
        ts(T.off1[:, 12:24], T.so[:, 47:576:48], pf(8), -1.0, ALU.mult, ALU.add, ["so", ("pf", 8)], [("off1", 12)])
        together(K("n1_"))
        ts(T.off1[:, 0:12], T.so[:, 47:576:48], pf(3), None, ALU.mult, None, ["so", ("pf", 3)], [("off1", 0)])
        together(K("n2_"))
        both(2, 1, 1)
        ts(B("loff")[:], T.so[:, 47:576:48], pf(3), float(C + 1), ALU.mult, ALU.min, ["so", ("pf", 3)], [K("loff")])
        send([helper], B("ll")[:], B("loff")[:], K("al"), [K("loff")])
        if t == 0:
            dma("y", u8(T.wq[:]), T.wc[:], [K("loff")], ["wq"])
            borders()
        if t == 1:
            dma("y", T.vt[:], T.v[:], [K("loff")], ["vt"])
        arrive(K("aq"), 2 * width(guest), [K("gq")])
        arrive(K("al"), width(guest), [K("ll")])
        arrive(K("ac"), width(guest), [K("lc")])
        alone(3, 2, 1)
        first(1)
        together(K("fla"))
        fill(1)
        turn_a(2)
        first(2)
        together(K("fla"))
        fill(1)
        turn_b(2, C, 3)
        fill(1)
        both(5, 3, 2)
        alone(7, 5, 2)
        cp(T.fl[:, 16:32], table(2)[0].indirect(T.off2[:, 0:1]), table(2)[1] + ["off2"],
           [("fl", k) for k in (4, 5, 6, 7)])
        together(K("fla"))
        first(3)
        together(K("fla"))
        turn_a(5)
        first(5)
        together(K("flb"))
        cp(T.fl[:, 24:40], table(5)[0].indirect(T.off1[:, 0:1]), table(5)[1] + [("off1", 0)], [("fl", 6), ("fl", 7)])
        together(K("flb"))
        turn_b(5, C, 7)
        fill(2)
        own(T.sf[:, 0:32], T.fl[:, 0:32], 32, [("fl", k) for k in range(8)], ["sf"])
        both(12, 7, 5)
        unpack(EU[0] if ahead else 0)
        alone(17, 12, 5)
        unpack(EU[1] if ahead else 0)
        ends(T.ta[:], T.sf, 32, ["sf"], ["ta"])
        fill(1)
        turn_a(12)
        starts(cp, 7, "ta", 2)
        together(K("flc"))
        starts(cp, 12, "ta", 2, w=[("fl", 17)])
        together(K("flc"))
        turn_b(12, C, 17)
        fill(2)
        own(T.sf[:], T.fl[:, 0:96], 96, [("fl", k) for k in (0, 1, 2, 3, 4, 5, 6, 7, 12)], ["sf"])
        last = rank == N - 1
        both(29, 17, 12, 6 if last else 8)
        if not last:
            cp(T.x0[:], table(17)[0].indirect(T.off12[:, 0:1]), table(17)[1] + ["off12"], ["x0"])
            together(K("n29_"))
        unpack(EU[2] if ahead else 0)
        if not last:
            alone(41, 29, 12)
        xn = K("exb" if rank == 1 or (rank == 2 and not VIA[t]) else "exu")
        ex, cand, cu = T[xn], B("cand"), B("cu")

        def jump(step):
            m = (29, 41, 41, 53)[step]
            win, wk = table(m, 128 if step == 3 else 0)
            src, on = T["x%d" % step], "x%d" % step
            out, nn = (T["x%d" % (step + 1)], "x%d" % (step + 1)) if step < 3 else (ex, xn)
            add = (0.0, 0.0, -128.0, -float(C + 1))[step]
            if last:
                return
            if rank == 0:
                ts(out[:, 0:16], win.indirect(src[:, 0:1]), add, None, ALU.add, None, wk + [on], [(nn, 0)])
                if step == 3:
                    together(K("ex"))
                    ts(out[:, 16:32], win.indirect(src[:, 0:1]), 4.0, pf(6), ALU.mult, ALU.add, wk + [on, ("pf", 6)], [(nn, 1)])
                    together(K("ex"))
            elif step % 2 == 0:
                a = 0 if step == 0 else 30
                ts(out[:, 1:65], win.indirect(src[:, a:a + 4]), add, None, ALU.add, None, wk + [on], [nn])
            else:
                for h in range(2):
                    a = h if step == 1 else 2 + h
                    two = win.indirect(src[:, 16 + 32 * h:18 + 32 * h])
                    if step == 3 and rank == 2 and VIA[t]:
                        ts(out[:, a:a + 64:2], two, 4.0, pf(6), ALU.mult, ALU.add, wk + [on, ("pf", 6)], [(nn, h)])
                    else:
                        ts(out[:, a:a + 64:2], two, add, None, ALU.add, None, wk + [on], [(nn, h)])
                    together(K("j%d_" % step))

        ends(T.tb[:], T.sf, 96, ["sf"], ["tb"])
        fill(9)
        jump(0)
        if not last:
            together(K("n41_"))
        starts(cp, 29, "tb", 3)
        together(K("fld"))
        starts(cp, 41, "tb", 2, 29, 4)
        together(K("fld"))
        starts(act, 17, "tb", 3, w=[("fl", 12)])
        together(K("fld"))
        if not last:
            alone(53, 41, 12, 8)
        unpack(8)
        if last:
            alone(41, 29, 12)
            if ahead:
                pack()
        jump(1)
        for e in range(ne):
            scan(T.sr[:, 64 * e:64 * e + 52], T.me[:], T.fl[:, e:208:4], ALU.mult, ALU.max, ["fl", "me"], [("sr", e)])
            together(K("sr"))
        if last and ahead:
            pack()
        jump(2)
        if not last:
            together(K("n53_"))
        out, on = (cu[:, 0:3], K("cu")) if rank == 0 else (cand[:, 0:15], K("cand"))
        ts(out, T.sr[:, 19:64 * ne:16], T.sq[:, 15:16], None, ALU.mult, None, ["sr", "sq"], [on])
        jump(3)
        if not last:
            turn_a(41, 112)
        helpers = [r for r in range(N) if r != rank and (r - HOP[t]) % N > rank]
        helpers.sort(key=lambda r: ((r - HOP[t]) % N) * (SGN[t] if rank == 1 else SG0[t]))
        src = ex[:, 14:18] if rank == 0 else ex[:, 32:36]
        homes = [r for r in range(rank + 1, N) if r not in helpers]
        ORDER = ORD[t][rank]
        if not last and ORDER != 1:
            send(helpers, B("lm%d_" % rank)[:], src, K("am%d_" % rank), [xn])
        if rank == 0:
            send([helper], B("lu")[:, 0:3], cu[:, 0:3], K("ac"), [K("cu")])
        else:
            send([helper], B("lc")[:], cand[:], K("ac"), [K("cand")])
        if not last:
            send((helpers if ORDER == 1 else []) + homes, B("lm%d_" % rank)[:], src, K("am%d_" % rank), [xn])
        assert APART

        pack()
        if not last:
            turn_b(41, 112)
        if rank < guest:
            grow(act, 82, 41, 41, 0, 7)
            grow(act, 123, 82, 41, 0, 5)
        for b in range(3):
            pack()
        for r in range(max(rank, guest)):
            if r != rank:
                arrive(K("am%d_" % r), width(r), [K("lm%d_" % r)])

        def told(r, a=0, n=4):
            if r == rank:
                at = 14 if r == 0 else 32
                return ex[:, at + a:at + a + n], xn
            return B("lm%d_" % r)[:, a:a + n], K("lm%d_" % r)

        def choose(r, lists, ln, sel):
            if r >= 2:
                (win, wn), (v0, vn) = told(1), told(0, 0, 1)
                if r == 2:
                    ts(T[sel][:], win.indirect(v0), 4.0, pf(5), ALU.mult, ALU.add, [wn, vn, ("pf", 5)], [sel])
                elif VIA[t]:
                    ts(T[sel][:], win.indirect(v0), 16.0, pf(1), ALU.mult, ALU.add, [wn, vn, ("pf", 0)], [sel])
                    together(K("via"))
                    cp(T.via[:], lists[:].indirect(told(2)[0]), [ln, told(2)[1]], ["via"])
                    together(K("via"))
                else:
                    cp(T.ch[:], win.indirect(v0), [wn, vn], ["ch"])
                    ts(T[sel][:], told(2)[0].indirect(T.ch[:, 0:1]), 4.0, pf(5), ALU.mult, ALU.add,
                       [told(2)[1], "ch", ("pf", 5)], [sel])

        def pick(r, lists, ln, sel, out):
            if r == 1:
                cp(T[out][:], lists[:].indirect(told(0, 2, 1)[0]), [ln, told(0)[1]], [out])
            elif r == 3 and VIA[t]:
                cp(T[out][:], T.via[:].indirect(T[sel][:, 0:1]), ["via", sel], [out])
            elif r >= 2:
                cp(T[out][:], lists[:].indirect(T[sel][:, 0:1]), [ln, sel], [out])

        goff, gn = (T.goff, "goff") if guest > 0 else (B("lu"), K("lc"))
        soff, sn = (T.soff, "soff") if rank > 0 else (cu, K("cu"))

        def shared():
            ts(T.sofb[:, 0:1], soff[:, 0:1], pf(7), None, ALU.max, None, [sn, ("pf", 7)], [("sofb", 0)])
            together(K("sofb"))
            cp(T.sofb[:, 1:3], soff[:, 1:3], [sn], [("sofb", 1)])
            together(K("sofb"))

        def blocks():
            for m in range(5):
                win, wk = table(STEP * m)
                offs, on = (soff, sn) if m == 0 else (T.sofb, "sofb")
                mine = m < 3 if rank == 0 else m in (1, 2) and rank > guest
                (cp if mine else act)(T.sb[:, A * m:A * m + A], win.indirect(offs[:, 0:3]), wk + [on], [("sb", m)])
                if m > 0:
                    together(K("sb%d_" % (0 if m < 3 else 1)))

        def span(c):
            return 4 * c, 20 * c + 16, 8 * c * (c + 1), [("sb", i) for i in range((20 * c + 15) // A + 1)] + ["jb"]

        def count_scalar():
            for c in range(SPLIT, 12):
                lo, hi, at, rk = span(c)
                act(T.junk[:, at:at + hi - lo], T.sb[:, lo:hi], rk, [("ca", c), ("junk", c)], ACT.Sign,
                    bias=T.jb[:, c:c + 1], scale=-1.0, accum_out=T.ca[:, 5 * c + 4:5 * c + 5])
                together(K("sums"))

        def count_compare():
            for c in range(SPLIT):
                lo, hi, at, rk = span(c)
                ts(T.junk[:, at:at + hi - lo], T.sb[:, lo:hi], T.jb[:, c:c + 1], 2.0, ALU.is_lt, ALU.mult, rk, [("junk", c)])
                together(K("less"))
            for m in range(1, 4):
                at = m * (2 * A - STEP)
                ts(T.ca[:, m:60:5], T.jb[:], T.sb[:, at:at + 1], -96.0, ALU.is_gt, ALU.mult, ["jb", ("sb", m)],
                   [("ca", "m%d" % m)])
                together(K("sums"))

        def count_add(cs):
            for c in cs:
                lo, hi, at, rk = span(c)
                op("v", lambda c=c, lo=lo, hi=hi, at=at: V.tensor_reduce(
                    T.ca[:, 5 * c + 4:5 * c + 5], T.junk[:, at:at + hi - lo], AxisListType.X, ALU.add),
                   [("junk", c)], [("ca", c)])
                together(K("sums"))

        if rank == 0:
            shared()
            grow(act, 164, 123, 41, 0, 2)
            blocks()
        if t == 0:
            quant(T.lq[:, R * A:], T.ls[:, R * A:], T.zt[:], ["zt"], [("lq", "pad")])
        choose(guest, B("lc"), K("lc"), "gsel")
        if rank < guest:
            choose(rank, cand, K("cand"), "osel")
        pick(guest, B("lc"), K("lc"), "gsel", "goff")
        if guest > 0:
            together(K("fa"))
        if last:
            turn_a(41, 112)
        for b in range(4):
            src = T.fa[:, RG * b:RG * b + 1 + C].indirect(goff[:, 0:3])
            (cp if b % 2 == 0 else act)(T.ft[:, b:4 * A:4], src, [("fa", b), ("fa", 9), gn], [("ft", b)])
            together(K("ft"))
        if last:
            turn_b(41, 112)
        if rank > guest:
            grow(act, 82, 41, 41, 0, 7)
            grow(act, 123, 82, 41, 0, 5)
        if rank > 0:
            grow(act, 164, 123, 41, 0, 2)
        if rank < guest:
            pick(rank, cand, K("cand"), "osel", "soff")
        quant(T.fq[:], T.fs[:], T.ft[:], ["ft"], ["fq"])
        if rank == 0:
            count_scalar()
            count_compare()
        elif rank < guest:
            shared()
            blocks()
        for b in range(4):
            mm(2 + b, 128, col(T.wq, b), col(T.wsc, b), T.fq[:], T.fs[:], ["wq", "wsc", "fq"])
        if rank > guest and EARLY >= 2:
            choose(rank, cand, K("cand"), "osel")
        if rank > guest and EARLY == 3:
            pick(rank, cand, K("cand"), "osel", "soff")
        for b in range(4):
            ts(T.ht[:, b:4 * A:4], ps(2 + b, 0, A), 0.03125, None, ALU.mult, None, (), [("ps", 2 + b), ("ht", b)])
            together(K("ht"))
        if rank > guest and EARLY == 1:
            choose(rank, cand, K("cand"), "osel")
        if rank > guest and EARLY == 2:
            pick(rank, cand, K("cand"), "osel", "soff")
        if rank > guest and EARLY == 3:
            shared()
        if rank == 0:
            count_add(range(3))
        quant(B("hq")[:], B("hs")[:], T.ht[:], ["ht"], [K("hq")])
        if rank > guest:
            if EARLY == 0:
                choose(rank, cand, K("cand"), "osel")
            if EARLY < 2:
                pick(rank, cand, K("cand"), "osel", "soff")
            if EARLY < 3:
                shared()
            blocks()
        land = A * (R - 1 - t)
        send([guest], u8(T.lq[:, land:land + A]), u8(B("hq")[:, 0:A]), K("ah"), [K("hq")])
        send([guest], T.ls[:, land:land + A], B("hs")[:, 0:A], K("ah"), [K("hq")])
        if rank > 0:
            count_scalar()
            count_compare()
        count_add(range(3 if rank == 0 else 0, SPLIT))
        scan(T.cs[:], T.cr[:], T.ca[:], ALU.mult, ALU.add, ["cr", "ca"], ["cs"])
        if t == 1:
            quant(T.vq[:], T.vs[:], T.vt[:], ["vt"], ["vq"])
        ts(T.koff[:], T.cs[:, 4:60:5], 0.5, None, ALU.mult, None, ["cs"], ["koff"])
        together(K("hw"))
        if t == R - 1:
            act(T.olf[:], T.sb[:, 0:A], [("sb", 0)], ["olf"], ACT.Identity, bias=-1.0)
            dma("y", T.ol[:], T.olf[0:128:16, :], ["olf"], ())
        arrive(K("ah"), 2 * width(helper), [("lq", t)])
        banks = [0, 1, 6, 7]
        for b in range(4):
            mm(banks[b], 128, col(T.eq, b), col(T.es, b), T.lq[:, land:land + 128], T.ls[:, land:land + 128],
               [("eq", b), ("lq", "pad")] + [("lq", k) for k in range(t + 1)])
        for b in range(4):
            (cp if b == 0 else act)(T.hw[:, 64 * b + 1:64 * b + 1 + A], ps(banks[b], 0, A), (), [("ps", banks[b]), ("hw", b)])
            if b == 0:
                together(K("hw"))
        new = "t%d" % (t + 1)
        for b in range(4):
            tt(T[new][:, b:4 * C:4], T.hw[:, 64 * b:64 * b + 1 + A].indirect(T.koff[:]), B("t")[:, b:4 * C:4], ALU.add,
               [("hw", b), ("hw", 9), "koff", K("t")], [(new, b)])
            together(K("new"))

    tq, tsc, qn = T["tq%d" % R], T["ts%d" % R], "tq%d" % R
    quant(tq[:], tsc[:], T["t%d" % R][:], ["t%d" % R], [qn])
    mm(2, C, T.vq[:], T.vs[:], tq[:], tsc[:], ["vq", qn])
    dma("y", T.oc[:], u8(tq[:]), [qn], ())
    cp(T.yt[:], ps(2, 0, C), (), [("ps", 2), "yt"])
    for k in range(4):
        dma("s", T.osc[4 * k:4 * k + 4, :], tsc[32 * k:32 * k + 4, :], [qn], ())
    dma("y", T.y[:], T.yt[:], ["yt"], ())
    emit(g, T, ops, sent)
